import numpy as np, ml_dtypes
CORES = [25,29,65,69,153,157,193,197]
N = 8
BF = ml_dtypes.bfloat16
V, L, A, T = 4096, 128, 768, 4
H = L // 2; B = V - T * H
def draw0(rng):
    ax = np.clip(np.floor(rng.random((N, 8, 1, V)) * 300 - 22 + 140 * (rng.random((N, 8, 16, V)) - 0.5)), 0, 255).astype(np.int64)
    zp = np.clip(np.floor(rng.random((N, 8, 1, A)) * 170 + 40 + 160 * (rng.random((N, 8, 16, A)) - 0.5)), 0, 255).astype(np.int64)
    p = np.clip(np.floor(rng.random((N, 8, 1, L)) * 130 + 60 + 160 * (rng.random((N, 8, 16, L)) - 0.5)), 0, 255).astype(np.int64)
    near = (rng.random((N, 8, 1, H)) < 0.6) & (rng.random((N, 8, 16, H)) > 0.15)
    p[..., 1::2] = np.where(near, p[..., ::2], p[..., 1::2])
    rt = rng.integers(0, V, (N, 8, 16, A)); ex = rng.integers(0, V, (N, 8, 16, L))
    ex[..., 1::2] = np.where(rng.random((N, 8, 16, H)) < 0.2, ex[:, :, ::-1, ::2], ex[..., 1::2])
    return ax, rt, zp, ex, p, rng.integers(0, 4096, (N, 8, 16)), rng.integers(0, 4096, (N, 8, 16))
def pack(ax, rt, zp, ex, p, wt, km):
    b = lambda a: np.ascontiguousarray(a.reshape(N, 128, -1)).astype(np.float32).astype(BF)
    w = lambda a: np.ascontiguousarray(a.reshape(N, 128, -1)).astype(np.int32)
    return {"ax": b(ax), "rt": w(rt), "zp": b(zp), "ex": w(ex), "p0": b(p), "wt": w(wt), "km": w(km)}
def setup_inputs(rng):
    return pack(*draw0(rng))
def setup_inputs_spread(rng):
    def uneven(n): return np.minimum(np.floor(np.exp2(1 + 7.3 * rng.random((N, 8, 1, n))) * rng.random((N, 8, 16, n))), 255).astype(np.int64)
    ax, zp, p = uneven(V), uneven(A), uneven(L)
    p[..., 1::2] = np.where(rng.random((N, 8, 1, H)) < 0.4, p[..., ::2], p[..., 1::2])
    rt = np.minimum(np.floor(V * rng.random((N, 8, 16, A)) ** (0.5 + 3 * rng.random((N, 8, 1, A)))), V - 1).astype(np.int64)
    ex = np.minimum(np.floor(V * rng.random((N, 8, 16, L)) ** (0.5 + 3 * rng.random((N, 8, 1, L)))), V - 1).astype(np.int64)
    wt = np.minimum(np.floor(np.exp2(12.1 * rng.random((N, 8, 16)))) - 1, 4095).astype(np.int64)
    km = np.minimum(np.floor(np.exp2(12.1 * rng.random((N, 8, 16)))) - 1, 4095).astype(np.int64)
    return pack(ax, rt, zp, ex, p, wt, km)
def setup_inputs_ends(rng):
    den = np.array([0.0, 0.1, 0.25, 0.5, 0.75, 1.0])
    ax = 255 * (rng.random((N, 8, 16, V)) < rng.choice(den, (N, 8, 1, V))); zp = 255 * (rng.random((N, 8, 16, A)) < rng.choice(den, (N, 8, 1, A)))
    p = 255 * (rng.random((N, 8, 16, L)) < rng.choice(np.array([0.0, 0.25, 0.5, 0.75, 0.9, 1.0]), (N, 8, 1, L)))
    p[..., 1::2] = np.where(rng.random((N, 8, 1, H)) < 0.5, p[..., ::2], p[..., 1::2])
    for g, (a, b) in enumerate(((0.0, 0.4), (0.2, 1.0), (0.3, 0.7), (0.4, 0.0), (0.5, 0.3), (0.7, 0.2), (1.0, 0.3), (0.3, 0.5))):
        ax[:, g, :, 0] = 255 * (rng.random((N, 16)) < a); ax[:, g, :, V - 1] = 255 * (rng.random((N, 16)) < b)
    def names(n): return np.where(rng.random((N, 8, 16, n)) < 0.85, (V - 1) * rng.integers(0, 2, (N, 8, 16, n)), rng.integers(0, V, (N, 8, 16, n)))
    rt, ex = names(A), names(L)
    wt = 4095 * rng.integers(0, 2, (N, 8, 16)); km = 4095 * rng.integers(0, 2, (N, 8, 16))
    wt[:, 7] = 4095; wt[:, 5:7, 15] = 4095; wt[:, 0, 0] = 0; wt[:, 0, 1] = 4095
    for m, k in ((0, 0), (1, 4095), (3, 8), (9, 3856), (15, 3841)): km[:, 5:, m] = k
    one = np.zeros(16, np.int64); one[15] = 1
    for i in (0, 1, L - 2, L - 1): p[:, 5:, :, i] = one
    for i in (2, 3, L - 4, L - 3): p[:, 7, :, i] = 255; p[:, 6, :, i] = 0
    p[N - 1, 7, :, L - 2:] = 255
    for h in (3840, 3841, 4095, 4080, 3832): zp[:, 5:, :, (h * A) >> 12] = 255
    zp[:, 6, :, (4080 * A) >> 12] = 0; zp[:, 6, :, (4095 * A) >> 12] = 0; zp[:, 5, :, (4095 * A) >> 12] = 0
    for h in (8, 4088, 24, 264, 136): zp[:, 7, :, (h * A) >> 12] = 0
    zp[:, 6, :, 0] = 255
    return pack(ax, rt, zp, ex, p, wt, km)
def setup_inputs_corners(rng):
    ax, rt, zp, ex, p, wt, km = draw0(rng)
    cnt = rng.integers(0, 17, (N, 8, 1, V)); cnt[..., :17] = np.arange(17)
    hi = ((np.arange(16)[:, None] + rng.integers(0, 16, (N, 8, 1, V))) & 15) < cnt
    ax = np.where(hi, rng.integers(139, 256, ax.shape), rng.integers(0, 111, ax.shape))
    p = rng.integers(111, 140, p.shape); p[..., 1::2] = np.where(rng.random((N, 8, 1, H)) < 0.5, p[..., ::2], p[..., 1::2])
    sets = ((0, 1, 2, 3), (9, 10, 12, 16), (3, 4), (4, 5, 6, 7, 8), (8, 9), tuple(range(17)), (8,), ())
    full = int(rng.integers(0, N))
    for q in range(N):
        for g in range(8):
            s = 0 if q == full else (q + g) & 7
            cand = np.flatnonzero(np.isin(cnt[q, g, 0], np.array(sets[s], np.int64))) if s < 7 else np.array([0, B - 1, B, B + H - 1, B + H, V - 2, V - 1])
            if s == 6: cand = cand[:1]
            rt[q, g] = cand[rng.integers(0, len(cand), (16, A))]
    nm = (rng.integers(0, V, (N, 8, 1, H)) + (2 * rng.integers(0, V // 2, (N, 8, 1, H)) + 1) * np.arange(32)[:, None]) & (V - 1)
    ea, eb = nm[:, :, :16], nm[:, :, 16:]; rep = np.broadcast_to(nm[:, :, :1], ea.shape)
    kd = (np.arange(H)[None, None, None, :] + np.arange(8)[None, :, None, None] + np.arange(N)[:, None, None, None]) % 6
    lone = eb.copy(); lone[:, :, 0] = ea[:, :, 15]
    ex[..., ::2] = np.where(kd >= 4, rep, ea)
    ex[..., 1::2] = np.where(kd == 0, ea, np.where(kd == 1, ea[:, :, ::-1], np.where(kd == 3, lone, np.where(kd == 4, rep, eb))))
    ch = rng.integers(0, 3, (N, 8, 1, A)); ch[:, 1] = 0
    zp = np.take_along_axis(rng.integers(0, 256, (N, 8, 16, 3)), ch, 3)
    km[:, 2] = rng.integers(0, 4096, (N, 1)); km[:, 3, ::2] = 0; km[:, 3, 1::2] = 4095; wt[:, 4] = 0; wt[:, 6, 1:] = 0; wt[:, 6, 0] = 4095
    return pack(ax, rt, zp, ex, p, wt, km)
def setup_inputs_alike(rng):
    ax, rt, zp, ex, p, wt, km = draw0(rng)
    p[:, ::2] = p[:, ::2, :, :1]
    p[:, 1::2] = np.take_along_axis(p[:, 1::2, :, :4], rng.integers(0, 4, (N, 4, 1, L)), 3)
    rt = np.take_along_axis(rt[..., :8], rng.integers(0, 8, (N, 8, 1, A)), 3)
    rt[:, 3] = rng.choice(np.array([0, V - 1, B, B - 1]), (N, 16, A))
    ex[:, ::2] = rng.choice(np.array([0, 5, B - 1, B, B + H, V - 1]), (N, 4, 16, L))
    zp[:, 4:] = np.take_along_axis(zp[:, 4:, :, :16], rng.integers(0, 16, (N, 4, 1, A)), 3)
    wt[:, 5, :14] = rng.integers(3200, 4096, (N, 14)); wt[:, 5, 14] = 256; wt[:, 5, 15] = 1
    aim = np.array([0, 4095, 4075, 4077, 4087])[np.arange(H // 2) % 5]
    big = rng.integers(200, 256, (N, 14, H // 2))
    rest = (4096 + aim - np.sum(wt[:, 5, :14, None] * big, axis=1)) & 8191
    p[:, 5, :14, 2::4] = big; p[:, 5, 14, 2::4] = rest >> 8; p[:, 5, 15, 2::4] = rest & 255; p[:, 5, :, 3::4] = 0
    for k, v in ((5, V - 3), (6, V - 5), (7, V - 7)):
        rt[:, 5, k] = v; ax[:, 5, :, v] = 0; ax[:, 5, :4, v] = 255; ax[:, 5, 14:, v] = 255
    for v, u in ((V - 3, 4075), (V - 5, 4077), (V - 7, 4087), (V - 3, 4095), (V - 3, 4096)): ax[:, 5, :, (((v * u) >> 5) + v) & (V - 1)] = 255
    return pack(ax, rt, zp, ex, p, wt, km)
def check_inputs(d):
    bad = []
    for k, hi in (("ax", 255), ("rt", V - 1), ("zp", 255), ("ex", V - 1), ("p0", 255), ("wt", 4095), ("km", 4095)):
        v = np.asarray(d[k]).astype(np.float64)
        if not (np.min(v) >= 0 and np.max(v) <= hi): bad.append("range of " + k)
        elif np.any(v != np.floor(v)): bad.append("whole numbers of " + k)
    return bad
def pick(x, e):
    n = e.shape[3]
    return np.take_along_axis(x, e.reshape(N, 8, 1, 16 * n), 3).reshape(N, 8, 16, 16, n)
def reference(ax, rt, zp, ex, p0, wt, km):
    x = ax.astype(np.float32).astype(np.int64).reshape(N, 8, 16, V)
    r = np.zeros((N, 8, 16, A + T * L), np.int64); z = np.zeros((N, 8, 16, A + T * L), np.int64)
    r[..., :A] = rt.reshape(N, 8, 16, A); z[..., :A] = zp.astype(np.float32).astype(np.int64).reshape(N, 8, 16, A)
    e0 = ex.astype(np.int64).reshape(N, 8, 16, L); p = p0.astype(np.float32).astype(np.int64).reshape(N, 8, 16, L)
    w = wt.astype(np.int64).reshape(N, 8, 16, 1); k = km.astype(np.int64).reshape(N, 8, 16, 1); odd = np.zeros(N, np.int64)
    for t in range(T):
        n = A + L * t
        u = np.repeat(np.add.reduce(w * p, axis=2)[:, :, ::2] & 4095, 2, axis=2)[:, :, None, :]
        c = (((((u * u) >> 5) & 4095) + ((k * u) & 4095)) & 4095) * n >> 12
        score = np.sum(np.abs(pick(z, c) - p[:, :, :, None, :]), axis=2)
        a = np.minimum.reduce(score * 4096 + c, axis=2) & 4095
        e = np.take_along_axis(r, a[:, :, None, :], 3)
        v = np.sum(pick(x, e) >= p[:, :, :, None, :], axis=2)
        barred = v < 4 + odd[:, None, None, None]
        e2 = (((e * u) >> 5) + e + 77 * t) & (V - 1)
        v2 = np.sum(pick(x, e2) >= p[:, :, :, None, :], axis=2)
        f = np.where(barred, e0, np.where((v < 9) & (v2 >= v), e2, e))
        odd = np.sum(barred, axis=(1, 2, 3)) & 1
        fa, fb = f[..., ::2].copy(), f[..., 1::2].copy()
        same = fa[:, :, :, None, :] == fb[:, :, None, :, :]
        ca, cb = np.any(same, axis=3), np.any(same, axis=2)
        rec = np.maximum.reduce(np.where(ca[:, :, None], pick(x, fa), 0), axis=3)
        new = B + H * t + np.arange(H)
        f[..., ::2] = np.where(ca, new, fa); f[..., 1::2] = np.where(cb, new, fb)
        src = (np.arange(N) - 1 - t % 3) % N
        f, p = f[src], p[src]
        r[..., n:n + L] = f
        if t < T - 1: z[..., n:n + L] = p
        x[..., B + H * t:B + H * t + H] = rec[src]
        p = (p + 255 - np.take_along_axis(x, f[:, :, :1], 3)) >> 1
    return {"yr": r[..., A:].reshape(N, 128, T * L).astype(np.float32), "yp": p.reshape(N, 128, L).astype(np.float32)}

@@ -1,0 +1,393 @@
+from concourse.mybir import AluOpType as A, ActivationFunctionType as F
+
+LV = 76
+QS = 44
+_D = {"f": "float32", "b": "bfloat16", "h": "float16", "i": "int32", "u": "uint16"}
+_S = """XT 4112 b;RW 1280 f;ZW 1280 b;RI 768 i;EI 128 i;E128 128 f;WI 16 i;WI2 16 i;KI 16 i;COL 16 f;PI 128 b;PN 512 b;P 128 b;PT 128 b
+PRS 2048 b;PB 128 f;IP 4 i;IOT 128 f;R16 128 f;G16 128 f;NEW 256 f;KLI 8 i;KL 8 u;I 128 b;IPM 128 b;EX 2048 b;BB 128 b;NB 128 b
+B4 8 b;B8 8 b;B8F 8 f;B8H 8 h;IH 128 h;I8 128 b;MASK 128 f;RST 128 f;RQ 1024 b;ONESF 128 f;SEL 2048 b;BC 2048 h;WH 128 b;WL 128 b
+BAR 1 f;UI 64 i;UM 64 i;SQ 64 i;T1 64 i;H1 64 i;H2 64 i;C16 64 u;CF 64 h;ZG 1024 b;AB 2048 b;SC 128 f;LM 128 f;LI 8 i;LA 8 i;L16 8 u
+E16 128 u;EF 128 f;EFS 128 f;EU 128 i;SH 128 i;SM 128 i;SA 128 i;E216 128 u;VB 2048 b;VB2 2048 b;XG 1024 b;XG2 1024 b;VT 128 b;VT2 128 b
+BR 128 f;G9 128 f;TH2 128 f;BAS 128 f;BASC 128 f;JNK 128 f;CNT 1 f;CI 2 i;FC 128 h;FF 128 f;FQ 64 f;EQ 1024 b;Q16 64 u;GQ 1024 b
+SQM 1024 b;FL 128 f;FH 128 h;FM 128 h;FS 512 f;MS 288 u;ML 288 u;AF 128 h;YP 128 f;relp 512 b;relf 512 f;relm 288 u"""
+SCRATCH = {x.split()[0]: ("sbuf", [128, int(x.split()[1])], _D[x.split()[2]]) for x in _S.replace("\n", ";").split(";")}
+WID = {k: v[1][1] for k, v in SCRATCH.items()}
+for _b in range(8):
+    SCRATCH["pb%d" % _b] = ("psum", [128, 512], "float32")
+SEMAPHORES = (["sv", "sa", "st", "sg", "ls", "rl", "lp", "lw", "lk", "lz", "lr", "le", "lx0", "lx1", "o0", "o1", "o2"]
+              + ["a%s%d" % (k, t) for k in "pfm" for t in range(4)])
+N = 8
+
+
+def nxt(r, t):
+    return (r + 1 + t % 3) % N
+
+
+def hops(T, topo, src, dst, kind):
+    if topo.may_write(src, dst):
+        return [dst]
+    c = [x for x in topo.cores_of(src) if topo.die(x) == topo.die(src) and topo.may_write(x, dst) and T.rank_of(x) is None]
+    return [c[0] if kind == "f" else c[-1], dst]
+
+
+def send(g, topo, src, dst, out, in_, rsem, lsem):
+    rid, pid = topo.addr(dst, src)
+    g.remote_dma(out, in_, rsem, lsem, pid, rid, topo.mask(src, dst))
+    return len(topo.engines(src, dst))
+
+
+def final_place(T, kind, t):
+    n = 768 + 128 * t
+    if kind == "p":
+        return T.ZW[:, n:n + 128], T.relp[:, 128 * t:128 * t + 128]
+    if kind == "f":
+        return T.RW[:, n:n + 128], T.relf[:, 128 * t:128 * t + 128]
+    return T.ML[:, 72 * t:72 * t + 72], T.relm[:, 72 * t:72 * t + 72]
+
+
+def relay_program(g, core, T, topo):
+    sent = 0
+    for t in range(4):
+        for kind in "pmf":
+            for r in range(N):
+                src, dst = T.cores[r], T.cores[nxt(r, t)]
+                h = hops(T, topo, src, dst, kind)
+                if len(h) < 2 or h[0] != core:
+                    continue
+                sem = T.sem["a%s%d" % (kind, t)]
+                g.wait_ge(sem, len(topo.engines(src, core)))
+                a, b = final_place(T, kind, t)
+                sent += send(g, topo, core, dst, a, b, sem, T.sem.rl)
+    if sent:
+        g.wait_ge(T.sem.rl, sent)
+
+
+def rank_program(g, core, T, topo):
+    rank = T.rank_of(core)
+    if rank is None:
+        relay_program(g, core, T, topo)
+        return
+    eng = {"V": g.vector, "S": g.scalar, "T": g.tensor, "G": g, "Y": g.sync}
+    own = {"V": "sv", "S": "sa", "T": "st", "G": "sg"}
+    total, acc, clk, evc = {}, {}, {q: {} for q in eng}, {}
+
+    def merge(a, b):
+        for s, c in b.items():
+            if a.get(s, 0) < c:
+                a[s] = c
+
+    def note(buf, lo, hi, st, isw, sem, cnt, q):
+        keep = [x for x in acc.get(buf, []) if not (isw and st == 1 and lo <= x[0] and x[1] <= hi) and x[:5] != (lo, hi, st, isw, sem)]
+        acc[buf] = keep + [(lo, hi, st, isw, sem, cnt, q)]
+
+    def waits(q, regs):
+        need = {}
+        for buf, lo, hi, st, isw in regs:
+            ps = buf[:2] == "pb"
+            for lo2, hi2, st2, w2, sem, cnt, q2 in acc.get(buf, []):
+                if hi2 <= lo or hi <= lo2 or (st == st2 > 1 and (lo - lo2) % st):
+                    continue
+                if q2 == q and own.get(q) == sem:
+                    if not w2 or (q == "T" and isw):
+                        continue
+                elif not (isw or w2 or (ps and q2 != q)):
+                    continue
+                if clk[q].get(sem, 0) < cnt and need.get(sem, 0) < cnt:
+                    need[sem] = cnt
+        for s in sorted(need):
+            c = need[s]
+            if clk[q].get(s, 0) >= c or any(s2 != s and evc[(s2, c2)].get(s, 0) >= c for s2, c2 in need.items()):
+                continue
+            eng[q].wait_ge(T.sem[s], c)
+            merge(clk[q], evc[(s, c)])
+        for s, c in need.items():
+            merge(clk[q], evc[(s, c)])
+
+    def regions(reads, writes):
+        out = []
+        for isw, xs in ((False, reads), (True, writes)):
+            for x in xs:
+                for r in x[1]:
+                    out.append(((r[0], 0, 512, 1) if r[0][:2] == "pb" else r) + (isw,))
+        return out
+
+    def op(q, make, writes, reads, sem=None, inc=1):
+        regs = regions(reads, writes)
+        waits(q, regs)
+        sem = sem or own[q]
+        make(eng[q]).then_inc(T.sem[sem], inc)
+        total[sem] = total.get(sem, 0) + inc
+        c = dict(clk[q])
+        c[sem] = total[sem]
+        evc[(sem, total[sem])] = c
+        for r in regs:
+            note(*r, sem, total[sem], q if inc == 1 else "D")
+
+    def b(name, lo=0, hi=None, st=1, p=128, p0=0):
+        hi = WID.get(name, 128) if hi is None else hi
+        return (T[name][p0:p, lo:hi:st], [(name, lo, hi, st)])
+
+    def ind(w, o): return (w[0].indirect(o[0]), w[1] + o[1])
+    def ts(out, a, s1, s2, o0, o1=None):
+        ins = [a]
+        if isinstance(s1, tuple):
+            ins.append(s1)
+            s1 = s1[0]
+        if o1 is None:
+            op("V", lambda e: e.tensor_scalar(out[0], a[0], s1, s2, o0), [out], ins)
+        else:
+            op("V", lambda e: e.tensor_scalar(out[0], a[0], s1, s2, o0, o1), [out], ins)
+    def tt(out, a, c, o): op("V", lambda e: e.tensor_tensor(out[0], a[0], c[0], o), [out], [a, c])
+    def cp(out, a): op("V", lambda e: e.tensor_copy(out[0], a[0]), [out], [a])
+    def ms(out, c): op("V", lambda e: e.memset(out[0], c), [out], [])
+    def scan(out, a, c, o0, o1): op("V", lambda e: e.tensor_tensor_scan(out[0], a[0], c[0], 0.0, o0, o1), [out], [a, c])
+    def act(out, a, f=F.Copy, bias=0.0, scale=1.0, accum=None):
+        ins, outs = [a], [out]
+        kw = {"bias": bias, "scale": scale}
+        for k in kw:
+            if isinstance(kw[k], tuple):
+                ins.append(kw[k])
+                kw[k] = kw[k][0]
+        if accum is not None:
+            outs.append(accum)
+            kw["accum_out"] = accum[0]
+        op("S", lambda e: e.activation(out[0], a[0], f, **kw), outs, ins)
+    def mm(out, l, r, start=True, stop=True): op("T", lambda e: e.matmul(out[0], l[0], r[0], start, stop), [out], [l, r])
+    def dma(q, sem, out, in_, w, r): op(q, lambda e: e.dma_start(out, in_), w, r, sem, 16)
+    def iota(out, pat, base, cm, small=True):
+        if small:
+            op("G", lambda e: e.iota(out[0], pat, base, cm, allow_small_or_imprecise_dtypes=True), [out], [])
+        else:
+            op("G", lambda e: e.iota(out[0], pat, base, cm), [out], [])
+
+    sent = [0]
+    def push(kind, t, x):
+        waits("G", regions([x], []))
+        dst = T.cores[nxt(rank, t)]
+        h = hops(T, topo, core, dst, kind)
+        sent[0] += send(g, topo, core, h[0], final_place(T, kind, t)[len(h) - 1], x[0], T.sem["a%s%d" % (kind, t)], T.sem.ls)
+    def arrive(kind, t, x):
+        src = T.cores[(rank - 1 - t % 3) % N]
+        h = [src] + hops(T, topo, src, core, kind)
+        sem, cnt = "a%s%d" % (kind, t), len(topo.engines(h[-2], core))
+        total[sem] = cnt
+        evc[(sem, cnt)] = {sem: cnt}
+        note(*x[1][0], True, sem, cnt, "D")
+
+    dma("Y", "lp", T.PI[:], T.p0[:], [b("PI")], [])
+    dma("S", "lw", T.WI[:, 0:1], T.wt[:], [b("WI")], [])
+    dma("Y", "lk", T.KI[:, 0:1], T.km[:], [b("KI")], [])
+    dma("S", "lz", T.ZW[:, 0:768], T.zp[:], [b("ZW", 0, 768)], [])
+    dma("Y", "lr", T.RI[:], T.rt[:], [b("RI")], [])
+    dma("S", "lx0", T.XT[:, 16:2064], T.ax[:, 0:2048], [b("XT", 16, 2064)], [])
+    dma("Y", "lx1", T.XT[:, 2064:4112], T.ax[:, 2048:4096], [b("XT", 2064, 4112)], [])
+    dma("Y", "le", T.EI[:], T.ex[:], [b("EI")], [])
+    C = lambda j: b("COL", j, j + 1)
+    IP = lambda j: b("IP", j, j + 1)
+    iota(IP(0), [[0, 1]], 0, 1, False)
+    iota(b("IOT"), [[1, 128]], 0, 0)
+    iota(b("G16"), [[1, 8], [0, 16]], 0, 0)
+    iota(b("KLI"), [[16, 8]], 15, 0, False)
+    iota(b("R16"), [[0, 8], [1, 16]], 0, 0)
+    push("p", 0, b("PI"))
+    iota(b("NEW"), [[1, 256]], 3840, 0)
+    ms(b("RST"), -1.0e9)
+    ms(b("SEL"), 0.0)
+    ms(b("BAR"), 4.0)
+    ms(b("XT", 0, 16), 0.0)
+    ms(b("RST", 0, 128, 16), 1.0e9)
+    ts(IP(1), IP(0), 15, None, A.bitwise_and)
+    ts(IP(2), IP(0), 4, None, A.arith_shift_right)
+    for j in range(3):
+        cp(C(j), IP(j))
+    ts(b("I"), b("IOT"), C(0), None, A.is_equal)
+    ts(b("IPM", 0, 64), b("IOT", 0, 64), C(0), None, A.is_equal)
+    ts(b("IPM", 64, 128), b("IOT", 64, 128), C(0), -1.0, A.is_equal, A.mult)
+    ts(b("BB"), b("G16"), C(2), None, A.is_equal)
+    for m in range(16):
+        cp(b("EX", m, 2048, 16), b("IPM"))
+    for h in range(2):
+        cp(b("P", 64 * h, 64 * h + 64), b("PI", h, 128, 2))
+    ts(b("WI2", 0, 1), b("WI", 0, 1), 6, None, A.arith_shift_right)
+    ts(b("WI2", 1, 2), b("WI", 0, 1), 63, None, A.bitwise_and)
+    cp(C(6), b("KI", 0, 1))
+    for j in range(2):
+        cp(C(4 + j), b("WI2", j, j + 1))
+    ts(b("WH"), b("BB"), C(4), 64.0, A.mult, A.mult)
+    ts(b("WL"), b("BB"), C(5), None, A.mult)
+    ts(b("NB"), b("BB"), -2048.0, None, A.mult)
+    ts(b("B4"), b("BB", 0, 128, 16), 4096.0, None, A.mult)
+    cp(b("B8F"), b("BB", 0, 128, 16))
+    cp(b("B8"), b("BB", 0, 128, 16))
+    cp(b("IH"), b("I"))
+    ts(b("MASK"), b("R16"), C(1), None, A.is_equal)
+    cp(b("KL"), b("KLI"))
+
+    W0, W1, W2 = 16 * LV, min(16 * LV + 512, 2048), 2048
+    parts = [(W0, W1)] + ([(W1, W2)] if W2 > W1 else [])
+    XW, XQ = b("XT", 16, 4112), b("XT")
+    for t in range(4):
+        n = 768 + 128 * t
+        lane = lambda buf, h: b(buf, 128 * t + h, 128 * t + 128, 2)
+        half = lambda buf, h: b(buf, 64 * h, 64 * h + 64)
+        mm(b("pb5", 0, 64), b("WH"), half("P", 0), True, False)
+        mm(b("pb5", 0, 64), b("WL"), half("P", 0), False, True)
+        mm(b("pb7"), b("P"), b("I"))
+        act(b("PT"), b("pb7"))
+        for k in (2, 3, 0, 1):
+            mm(b("pb%d" % k, 0, 512), b("PT"), b("EX", 512 * k, 512 * k + 512), True, k < 2)
+        if t:
+            for h in range(2):
+                act(lane("PN", h), half("P", h))
+            push("p", t, b("PN", 128 * t, 128 * t + 128))
+        cp(b("UI"), b("pb5", 0, 64))
+        ts(b("UM"), b("UI"), 4095, None, A.bitwise_and)
+        tt(b("SQ"), b("UM"), b("UM"), A.mult)
+        ts(b("pb5", 64, 128), b("UM"), C(6), None, A.mult)
+        ts(b("T1"), b("SQ"), 5, 4095, A.arith_shift_right, A.bitwise_and)
+        tt(b("H1"), b("T1"), b("pb5", 64, 128), A.add)
+        ts(b("H2"), b("H1"), 4095, None, A.bitwise_and)
+        ts(b("C16"), b("H2"), n / 4096.0, -31.0 / 64.0, A.mult, A.add)
+        act(b("ZG", 512, 1024), ind(b("ZW", 0, n), b("C16", 32, 64)))
+        cp(b("ZG", 0, 512), ind(b("ZW", 0, n), b("C16", 0, 32)))
+        cp(b("CF"), b("C16"))
+        for h in range(2):
+            cp(b("pb5", 128 + 64 * h, 192 + 64 * h), b("UM"))
+        for k in (0, 1):
+            z = b("ZG", 512 * k, 512 * k + 512)
+            mm(b("pb%d" % (2 + k), 0, 512), b("I"), z, False, True)
+            tt(b("AB", 512 * k, 512 * k + 512), z, b("pb%d" % k, 0, 512), A.max)
+            act(b("AB", 1024 + 512 * k, 1536 + 512 * k), b("pb%d" % (2 + k), 0, 512), F.Abs, scale=0.5)
+        mm(b("pb4"), b("P"), b("NB"), True, False)
+        for m in range(16):
+            mm(b("pb4", m, 128, 16, 64), b("ZG", m, 1024, 16), b("NB", 0, 128, 16), False, False)
+        for h in range(2):
+            mm(b("pb4", p0=64 * h, p=64 * h + 64), b("CF"), b("IH"), False, False)
+        if LV > 64:
+            mm(b("pb6", 0, W0 - 1024), b("PT"), b("EX", 1024, W0))
+        for m in range(16):
+            mm(b("pb4", m, 128, 16), b("AB", m, 2048, 16), b("B4"), False, m == 15)
+        for k in (0, 1):
+            act(b("PRS", 512 * k, 512 * k + 512), b("pb%d" % k, 0, 512))
+        if LV > 64:
+            act(b("PRS", 1024, W0), b("pb6", 0, W0 - 1024), scale=-1.0)
+        if t == 0:
+            cp(b("RW", 0, 768), b("RI"))
+            for k in range(16):
+                cp(b("SEL", 128 * k + k, 128 * k + 128, 16), b("B8"))
+        scan(b("SC"), b("RST"), b("pb4"), A.max, A.min)
+        tt(b("LM"), ind(b("SC"), b("KL")), b("MASK"), A.mult)
+        mm(b("pb4", 128, 136), b("LM"), b("B8F"))
+        cp(b("LI"), b("pb4", 128, 136))
+        ts(b("LA"), b("LI"), 2047, None, A.bitwise_and)
+        cp(b("L16"), b("LA"))
+        act(b("EF"), ind(b("RW", 0, n), b("L16")))
+        cp(b("E16"), ind(b("RW", 0, n), b("L16")))
+        act(b("pb7"), b("EF"), bias=77.0 * t)
+        tt(b("EU"), b("EF"), b("pb5", 128, 256), A.mult)
+        ts(b("SH"), b("EU"), 5, None, A.arith_shift_right)
+        tt(b("SM"), b("SH"), b("pb7"), A.add)
+        ts(b("SA"), b("SM"), 4095, None, A.bitwise_and)
+        cp(b("E216"), b("SA"))
+        for k in (2, 0):
+            for i, (lo, hi) in enumerate(parts):
+                mm(b("pb%d" % (k + i), 0, hi - lo), b("PT"), b("EX", lo, hi), True, False)
+        sets = (("E16", "XG", "VB", "VT", 2, 6), ("E216", "XG2", "VB2", "VT2", 0, 7))
+        for lst, xg, vb, vt, k, c in sets:
+            act(b(xg, 0, W2 - W0), ind(XW, b(lst, LV, 128)))
+            tt(b(vb, 0, W0), ind(XW, b(lst, 0, LV)), b("PRS", 0, W0), A.is_ge)
+            for i, (lo, hi) in enumerate(parts):
+                mm(b("pb%d" % (k + i), 0, hi - lo), b("I"), b(xg, lo - W0, hi - W0), False, True)
+        for lst, xg, vb, vt, k, c in sets:
+            for i, (lo, hi) in enumerate(parts):
+                act(b(vb, lo, hi), b("pb%d" % (k + i), 0, hi - lo), F.Sign, bias=0.5)
+        for lst, xg, vb, vt, k, c in sets:
+            if t == 0 and c == 6:
+                ts(C(8), C(0), LV - 0.5, -0.5, A.is_ge, A.mult)
+                ts(C(9), C(8), 1.0, None, A.add)
+                ts(C(10), C(8), -16.0, None, A.mult)
+            for m in range(16):
+                mm(b("pb%d" % c, m, 128, 16), b(vb, m, 2048, 16), b("B8"))
+            act(b(vt), b("pb%d" % c), F.Identity, C(10), C(9))
+            mm(b("pb%d" % c), b(vt), b("I"))
+        act(b("EFS"), b("EF"), scale=1.0 / 128.0)
+        if t == 0:
+            for h in range(2):
+                ts(half("E128", h), b("EI", h, 128, 2), 1.0 / 128.0, None, A.mult)
+            for k in range(16):
+                ts(b("BC", 128 * k, 128 * k + 128), b("BB"), b("MASK", k, k + 1), None, A.mult)
+            cp(b("B8H"), b("BB", 0, 128, 16))
+            ts(b("I8"), b("I"), 8192.0, None, A.mult)
+            ms(b("ONESF"), 1.0)
+            ms(b("RQ"), 255.0)
+            ms(b("RQ", 0, 1024, 16), 0.0)
+        tt(b("pb5", 256, 384), b("SA"), b("EF"), A.subtract)
+        tt(b("pb5", 384, 512), b("E128"), b("EFS"), A.subtract)
+        ts(b("BR"), b("pb6"), b("BAR"), 128.0, A.is_lt, A.mult)
+        ts(b("G9"), b("pb6"), 9.0, 128.0, A.is_ge, A.mult)
+        tt(b("pb5", 384, 512), b("BR"), b("pb5", 384, 512), A.mult)
+        tt(b("pb6"), b("G9"), b("pb6"), A.max)
+        tt(b("BAS"), b("EF"), b("pb5", 384, 512), A.add)
+        tt(b("TH2"), b("BR"), b("pb6"), A.max)
+        act(b("BASC"), b("BAS"), bias=-2048.0)
+        if t < 3:
+            act(b("JNK"), b("BR"), scale=1.0 / 128.0, accum=b("CNT"))
+        tt(b("FL"), b("pb7"), b("TH2"), A.is_ge)
+        tt(b("pb5"), b("FL"), b("pb5", 256, 384), A.mult)
+        tt(b("FC"), b("BASC"), b("pb5"), A.add)
+        tt(b("FF"), b("BAS"), b("pb5"), A.add)
+        act(b("FQ"), half("FF", 0), bias=16.0)
+        for k in range(16):
+            mm(b("pb%d" % (k // 4), 64 * (k % 4), 64 * (k % 4) + 64), b("BC", 128 * k, 128 * k + 128), half("FC", 1))
+        for k in range(16):
+            tt(half("EQ", k), half("FC", 0), b("pb%d" % (k // 4), 64 * (k % 4), 64 * (k % 4) + 64), A.is_equal)
+            mm(b("pb4", 0, 64), b("I8"), half("EQ", k), k == 0, k == 15)
+        for k in range(16):
+            mm(b("pb6", 0, 64), b("SEL", 128 * k, 128 * k + 128), half("EQ", k), k == 0, k == 15)
+        for h in range(2):
+            tt(b("pb5", 256 + 64 * h, 320 + 64 * h), b("NEW", 64 * t, 64 * t + 64), half("FF", h), A.subtract)
+        tt(b("Q16"), b("FQ"), b("pb4", 0, 64), A.min)
+        act(b("GQ", 0, 16 * QS), ind(XQ, b("Q16", 0, QS)))
+        cp(b("GQ", 16 * QS, 1024), ind(XQ, b("Q16", QS, 64)))
+        for h, k in ((0, 4), (1, 6)):
+            ts(half("FL", h), b("pb%d" % k, 0, 64), 0.5, None, A.is_ge)
+        tt(b("pb5"), b("FL"), b("pb5", 256, 384), A.mult)
+        tt(b("FH"), b("FC"), b("pb5"), A.add)
+        mm(b("pb7"), b("FH"), b("BC", 0, 128))
+        scan(b("SQM", 16 * QS, 1024), b("RQ", 16 * QS, 1024), b("GQ", 16 * QS, 1024), A.min, A.max)
+        tt(b("FM"), b("MASK"), b("pb7"), A.mult)
+        mm(b("pb7", 256, 264), b("FM"), b("B8H"))
+        scan(b("SQM", 0, 16 * QS), b("RQ", 0, 16 * QS), b("GQ", 0, 16 * QS), A.min, A.max)
+        ts(b("MS", 72 * t, 72 * t + 8), b("pb7", 256, 264), 2048.0, None, A.add)
+        cp(b("MS", 72 * t + 8, 72 * t + 72), b("SQM", 15, 1024, 16))
+        push("m", t, b("MS", 72 * t, 72 * t + 72))
+        for h in range(2):
+            tt(lane("FS", h), half("FF", h), b("pb5", 64 * h, 64 * h + 64), A.add)
+        push("f", t, b("FS", 128 * t, 128 * t + 128))
+        if t < 3:
+            mm(b("pb7", 384, 385), b("ONESF"), b("CNT"))
+            cp(b("CI", 0, 1), b("pb7", 384, 385))
+            ts(b("CI", 1, 2), b("CI", 0, 1), 1, None, A.bitwise_and)
+            ts(b("BAR"), b("CI", 1, 2), 4.0, None, A.add)
+        ml = b("ML", 72 * t, 72 * t + 72)
+        arrive("p", t, b("ZW", n, n + 128))
+        arrive("f", t, b("RW", n, n + 128))
+        arrive("m", t, ml)
+        for h in range(2):
+            act(half("PB", h), b("ZW", n + h, n + 128, 2), bias=2302.75)
+        B = 3856 + 64 * t
+        cp(b("XT", B, B + 64), b("ML", 72 * t + 8, 72 * t + 72))
+        tt(b("AF"), ind(XW, b("ML", 72 * t, 72 * t + 8)), b("PB"), A.subtract)
+        if t < 3:
+            ts(b("P"), b("AF"), -0.5, -1024.0, A.mult, A.add)
+        else:
+            for h in range(2):
+                ts(b("YP", h, 128, 2), half("AF", h), -0.5, -1024.0, A.mult, A.add)
+        if t == 2:
+            dma("Y", "o0", T.yr[:, 0:384], T.RW[:, 768:1152], [], [b("RW", 768, 1152)])
+    dma("Y", "o1", T.yr[:, 384:512], T.RW[:, 1152:1280], [], [b("RW", 1152, 1280)])
+    dma("S", "o2", T.yp[:], T.YP[:], [], [b("YP")])
+    for s in sorted(total):
+        if clk["G"].get(s, 0) < total[s]:
+            g.wait_ge(T.sem[s], total[s])
+    g.wait_ge(T.sem.ls, sent[0])

@@ -1,19 +1,24 @@
 from concourse.mybir import AluOpType as A, ActivationFunctionType as F
 
-LV = 76
-QS = 44
+SW = [30, 28, 30, 14, 10]
+ORDER = "d0 v1 c2 c3 g2 f4 s1 c0 g3 c1 s2 c6 v0 b1 g4 s3 c7 r1 s4 c4 b0 l1 c5 r0 h1"
+VA = 8
+ZA = 4
+QA = 30
+QS = 38
 _D = {"f": "float32", "b": "bfloat16", "h": "float16", "i": "int32", "u": "uint16"}
-_S = """XT 4112 b;RW 1280 f;ZW 1280 b;RI 768 i;EI 128 i;E128 128 f;WI 16 i;WI2 16 i;KI 16 i;COL 16 f;PI 128 b;PN 512 b;P 128 b;PT 128 b
-PRS 2048 b;PB 128 f;IP 4 i;IOT 128 f;R16 128 f;G16 128 f;NEW 256 f;KLI 8 i;KL 8 u;I 128 b;IPM 128 b;EX 2048 b;BB 128 b;NB 128 b
-B4 8 b;B8 8 b;B8F 8 f;B8H 8 h;IH 128 h;I8 128 b;MASK 128 f;RST 128 f;RQ 1024 b;ONESF 128 f;SEL 2048 b;BC 2048 h;WH 128 b;WL 128 b
-BAR 1 f;UI 64 i;UM 64 i;SQ 64 i;T1 64 i;H1 64 i;H2 64 i;C16 64 u;CF 64 h;ZG 1024 b;AB 2048 b;SC 128 f;LM 128 f;LI 8 i;LA 8 i;L16 8 u
-E16 128 u;EF 128 f;EFS 128 f;EU 128 i;SH 128 i;SM 128 i;SA 128 i;E216 128 u;VB 2048 b;VB2 2048 b;XG 1024 b;XG2 1024 b;VT 128 b;VT2 128 b
-BR 128 f;G9 128 f;TH2 128 f;BAS 128 f;BASC 128 f;JNK 128 f;CNT 1 f;CI 2 i;FC 128 h;FF 128 f;FQ 64 f;EQ 1024 b;Q16 64 u;GQ 1024 b
-SQM 1024 b;FL 128 f;FH 128 h;FM 128 h;FS 512 f;MS 288 u;ML 288 u;AF 128 h;YP 128 f;relp 512 b;relf 512 f;relm 288 u"""
-SCRATCH = {x.split()[0]: ("sbuf", [128, int(x.split()[1])], _D[x.split()[2]]) for x in _S.replace("\n", ";").split(";")}
-WID = {k: v[1][1] for k, v in SCRATCH.items()}
+_S = """XT 4176 b;RI 1152 i;YR 512 f;ZW 1280 b;EI 128 i;EBH 128 h;WI 16 i;WI2 16 i;KI 16 i;COL 16 f;PI 128 b;PN 512 b;P 128 b;PT 128 b
+PRS 2048 b;PB 128 f;IP 4 i;IOT 128 f;R16 128 f;G16 128 f;NEW 256 h;KLI 8 i;KL 8 u;I 128 b;EX 128x16 b;BB 128 b;NB 128 b
+B4 8 b;B8 8 b;B8H 8 h;IH 128 h;NIH 128 h;I8 128 b;I128 128 b;BB8 128 b;ONES 128 b;MASK 128 f;MBIG 128 b;NXD 128 f;RST 128 f;RQ 1024 b
+SEL 2048 b;BC 2048 h;WH 128 b;WL 128 b;BAR 1 f;UI 64 i;UM 64 i;U2 128 f;SQ 64 i;T1 64 i;H1 64 i;H2 64 i;C16 64 u;CF 64 h
+ZG 1024 b;AB 128x16 b;SC 128 i;LA 8 i;LM 128 h;L16 8 u;E16 128 u;EH 128 h;EU 128 i;SH 128 i;SM 128 i;SA 128 i;E216 128 u;E2H 128 h
+VB 2048 b;VB2 2048 b;XG 2560 b;NI 128 b;BR 128 b;G9 128 f;TH 128 b;Y1 128 f;FLI 256 b;FS 256 h;JNK 128 f;CNT 1 f;CI 2 i
+FQ 64 f;EQ 1088 b;Q16 64 u;GQ 1024 b;SQM 1024 b;F0S 128 f;FL 128 f;FF 128 f;FO 512 f;MS 288 u;ML 288 u;AF 128 h;YP 128 f
+relp 512 b;relf 512 f;relm 288 u"""
+SHAPE = {x.split()[0]: [int(v) for v in x.split()[1].split("x")] for x in _S.replace("\n", ";").split(";")}
+SCRATCH = {x.split()[0]: ("sbuf", [128] + SHAPE[x.split()[0]], _D[x.split()[2]]) for x in _S.replace("\n", ";").split(";")}
 for _b in range(8):
-    SCRATCH["pb%d" % _b] = ("psum", [128, 512], "float32")
+    SCRATCH["pb%d" % _b] = ("psum", [128, 32, 16] if _b < 2 else [128, 512], "float32")
 SEMAPHORES = (["sv", "sa", "st", "sg", "ls", "rl", "lp", "lw", "lk", "lz", "lr", "le", "lx0", "lx1", "o0", "o1", "o2"]
               + ["a%s%d" % (k, t) for k in "pfm" for t in range(4)])
 N = 8
@@ -41,7 +46,7 @@ def final_place(T, kind, t):
     if kind == "p":
         return T.ZW[:, n:n + 128], T.relp[:, 128 * t:128 * t + 128]
     if kind == "f":
-        return T.RW[:, n:n + 128], T.relf[:, 128 * t:128 * t + 128]
+        return T.YR[:, 128 * t:128 * t + 128], T.relf[:, 128 * t:128 * t + 128]
     return T.ML[:, 72 * t:72 * t + 72], T.relm[:, 72 * t:72 * t + 72]
 
 
@@ -62,6 +67,11 @@ def relay_program(g, core, T, topo):
         g.wait_ge(T.sem.rl, sent)
 
 
+def bits(lo, hi, st, unit=1):
+    n = len(range(lo, hi, st))
+    return unit * (((1 << (st * n)) - 1) // ((1 << st) - 1)) << lo
+
+
 def rank_program(g, core, T, topo):
     rank = T.rank_of(core)
     if rank is None:
@@ -76,21 +86,19 @@ def rank_program(g, core, T, topo):
             if a.get(s, 0) < c:
                 a[s] = c
 
-    def note(buf, lo, hi, st, isw, sem, cnt, q):
-        keep = [x for x in acc.get(buf, []) if not (isw and st == 1 and lo <= x[0] and x[1] <= hi) and x[:5] != (lo, hi, st, isw, sem)]
-        acc[buf] = keep + [(lo, hi, st, isw, sem, cnt, q)]
+    def note(buf, m, isw, sem, cnt, q):
+        keep = [x for x in acc.get(buf, []) if not (isw and x[0] & ~m == 0) and x[:3] != (m, isw, sem)]
+        acc[buf] = keep + [(m, isw, sem, cnt, q)]
 
     def waits(q, regs):
         need = {}
-        for buf, lo, hi, st, isw in regs:
+        for buf, m, isw in regs:
             ps = buf[:2] == "pb"
-            for lo2, hi2, st2, w2, sem, cnt, q2 in acc.get(buf, []):
-                if hi2 <= lo or hi <= lo2 or (st == st2 > 1 and (lo - lo2) % st):
-                    continue
+            for m2, w2, sem, cnt, q2 in acc.get(buf, []):
                 if q2 == q and own.get(q) == sem:
-                    if not w2 or (q == "T" and isw):
+                    if not m & m2 or not w2 or (q == "T" and isw):
                         continue
-                elif not (isw or w2 or (ps and q2 != q)):
+                elif not (ps or (m & m2 and (isw or w2))):
                     continue
                 if clk[q].get(sem, 0) < cnt and need.get(sem, 0) < cnt:
                     need[sem] = cnt
@@ -104,12 +112,7 @@ def rank_program(g, core, T, topo):
             merge(clk[q], evc[(s, c)])
 
     def regions(reads, writes):
-        out = []
-        for isw, xs in ((False, reads), (True, writes)):
-            for x in xs:
-                for r in x[1]:
-                    out.append(((r[0], 0, 512, 1) if r[0][:2] == "pb" else r) + (isw,))
-        return out
+        return [r + (isw,) for isw, xs in ((False, reads), (True, writes)) for x in xs for r in x[1]]
 
     def op(q, make, writes, reads, sem=None, inc=1):
         regs = regions(reads, writes)
@@ -124,8 +127,12 @@ def rank_program(g, core, T, topo):
             note(*r, sem, total[sem], q if inc == 1 else "D")
 
     def b(name, lo=0, hi=None, st=1, p=128, p0=0):
-        hi = WID.get(name, 128) if hi is None else hi
-        return (T[name][p0:p, lo:hi:st], [(name, lo, hi, st)])
+        hi = SHAPE.get(name, [128])[0] if hi is None else hi
+        return (T[name][p0:p, lo:hi:st], [(name, bits(lo, hi, st))])
+
+    def b3(name, lo, hi, c0=0, c1=16):
+        ap = T[name][:, lo:hi, c0] if c1 is None else T[name][:, lo:hi, c0:c1]
+        return (ap, [(name, bits(16 * lo + c0, 16 * hi, 16, 1 if c1 is None else (1 << (c1 - c0)) - 1))])
 
     def ind(w, o): return (w[0].indirect(o[0]), w[1] + o[1])
     def ts(out, a, s1, s2, o0, o1=None):
@@ -159,6 +166,7 @@ def rank_program(g, core, T, topo):
             op("G", lambda e: e.iota(out[0], pat, base, cm, allow_small_or_imprecise_dtypes=True), [out], [])
         else:
             op("G", lambda e: e.iota(out[0], pat, base, cm), [out], [])
+    def gcp(out, a, n): op("G", lambda e: e.affine_select(out[0], a[0], [[0, n]], A.is_ge, 0.0, 0, 0), [out], [a])
 
     sent = [0]
     def push(kind, t, x):
@@ -178,214 +186,258 @@ def rank_program(g, core, T, topo):
     dma("S", "lw", T.WI[:, 0:1], T.wt[:], [b("WI")], [])
     dma("Y", "lk", T.KI[:, 0:1], T.km[:], [b("KI")], [])
     dma("S", "lz", T.ZW[:, 0:768], T.zp[:], [b("ZW", 0, 768)], [])
-    dma("Y", "lr", T.RI[:], T.rt[:], [b("RI")], [])
+    dma("Y", "lr", T.RI[:, 0:768], T.rt[:], [b("RI", 0, 768)], [])
     dma("S", "lx0", T.XT[:, 16:2064], T.ax[:, 0:2048], [b("XT", 16, 2064)], [])
     dma("Y", "lx1", T.XT[:, 2064:4112], T.ax[:, 2048:4096], [b("XT", 2064, 4112)], [])
     dma("Y", "le", T.EI[:], T.ex[:], [b("EI")], [])
     C = lambda j: b("COL", j, j + 1)
     IP = lambda j: b("IP", j, j + 1)
+    half = lambda buf, h: b(buf, 64 * h, 64 * h + 64)
+    pb = lambda k, lo=0, hi=128, st=1: b("pb%d" % k, lo, hi, st)
     iota(IP(0), [[0, 1]], 0, 1, False)
-    iota(b("IOT"), [[1, 128]], 0, 0)
     iota(b("G16"), [[1, 8], [0, 16]], 0, 0)
-    iota(b("KLI"), [[16, 8]], 15, 0, False)
+    iota(b("IOT"), [[1, 128]], 0, 0)
     iota(b("R16"), [[0, 8], [1, 16]], 0, 0)
+    iota(b("KLI"), [[1, 8]], 0, 0, False)
     push("p", 0, b("PI"))
-    iota(b("NEW"), [[1, 256]], 3840, 0)
+    iota(b("NEW"), [[1, 256]], 3840 - 2048, 0)
     ms(b("RST"), -1.0e9)
     ms(b("SEL"), 0.0)
-    ms(b("BAR"), 4.0)
-    ms(b("XT", 0, 16), 0.0)
     ms(b("RST", 0, 128, 16), 1.0e9)
     ts(IP(1), IP(0), 15, None, A.bitwise_and)
     ts(IP(2), IP(0), 4, None, A.arith_shift_right)
     for j in range(3):
         cp(C(j), IP(j))
-    ts(b("I"), b("IOT"), C(0), None, A.is_equal)
-    ts(b("IPM", 0, 64), b("IOT", 0, 64), C(0), None, A.is_equal)
-    ts(b("IPM", 64, 128), b("IOT", 64, 128), C(0), -1.0, A.is_equal, A.mult)
     ts(b("BB"), b("G16"), C(2), None, A.is_equal)
-    for m in range(16):
-        cp(b("EX", m, 2048, 16), b("IPM"))
+    ts(b("I"), b("IOT"), C(0), None, A.is_equal)
+    act(b("ONES"), b("G16"), F.Sigmoid, bias=40.0)
+    cp(b3("EX", 0, 128, 0, None), b("I"))
+    ts(b("NI"), b("I"), -1.0, None, A.mult)
+    ts(b("MASK"), b("R16"), C(1), None, A.is_equal)
+    for k in (1, 2, 4, 8):
+        cp(b3("EX", 0, 128, k, 2 * k), b3("EX", 0, 128, 0, k))
     for h in range(2):
-        cp(b("P", 64 * h, 64 * h + 64), b("PI", h, 128, 2))
+        cp(half("P", h), b("PI", h, 128, 2))
     ts(b("WI2", 0, 1), b("WI", 0, 1), 6, None, A.arith_shift_right)
     ts(b("WI2", 1, 2), b("WI", 0, 1), 63, None, A.bitwise_and)
-    cp(C(6), b("KI", 0, 1))
     for j in range(2):
         cp(C(4 + j), b("WI2", j, j + 1))
     ts(b("WH"), b("BB"), C(4), 64.0, A.mult, A.mult)
     ts(b("WL"), b("BB"), C(5), None, A.mult)
-    ts(b("NB"), b("BB"), -2048.0, None, A.mult)
-    ts(b("B4"), b("BB", 0, 128, 16), 4096.0, None, A.mult)
-    cp(b("B8F"), b("BB", 0, 128, 16))
-    cp(b("B8"), b("BB", 0, 128, 16))
-    cp(b("IH"), b("I"))
-    ts(b("MASK"), b("R16"), C(1), None, A.is_equal)
-    cp(b("KL"), b("KLI"))
+    cp(C(6), b("KI", 0, 1))
+    act(b("NB"), b("BB"), scale=-2048.0)
+    act(b("B4"), b("BB", 0, 128, 16), scale=4096.0)
+    act(b("IH"), b("I"))
+    act(b("B8H"), b("BB", 0, 128, 16))
+    act(b("KL"), b("KLI"))
+    for k in range(16):
+        act(b("SEL", 128 * k + k, 128 * k + 128, 16), b("BB", 0, 128, 16))
 
-    W0, W1, W2 = 16 * LV, min(16 * LV + 512, 2048), 2048
-    parts = [(W0, W1)] + ([(W1, W2)] if W2 > W1 else [])
-    XW, XQ = b("XT", 16, 4112), b("XT")
+    SP = ((0, 0, 128 - SW[0], 128), (0, 1, 0, SW[1]), (1, 2, 128 - SW[2], 128), (1, 3, 0, SW[3]), (1, 0, SW[3], SW[3] + SW[4]))
+    v0, v1 = min(SW[1], SW[3] + SW[4]), 128 - min(SW[0], SW[2])
+    copies = [(k, lo, min(lo + 32, v1)) for k, lo in zip((6, 7, 2), range(v0, v1, 32))]
+    def sbank(i):
+        _, k, lo, hi = SP[i]
+        return b3("pb%d" % k, 0, hi - lo) if k < 2 else pb(k, 0, 16 * (hi - lo))
+    XW, XQ, XN = b("XT", 16, 4112), b("XT", 0, 4112), b("XT", 16, 4176)
     for t in range(4):
         n = 768 + 128 * t
         lane = lambda buf, h: b(buf, 128 * t + h, 128 * t + 128, 2)
-        half = lambda buf, h: b(buf, 64 * h, 64 * h + 64)
-        mm(b("pb5", 0, 64), b("WH"), half("P", 0), True, False)
-        mm(b("pb5", 0, 64), b("WL"), half("P", 0), False, True)
-        mm(b("pb7"), b("P"), b("I"))
-        act(b("PT"), b("pb7"))
-        for k in (2, 3, 0, 1):
-            mm(b("pb%d" % k, 0, 512), b("PT"), b("EX", 512 * k, 512 * k + 512), True, k < 2)
+        ZW, RW = b("ZW", 0, n), b("RI", 0, n)
+        mm(pb(5, 0, 64), b("WH"), half("P", 0), True, False)
+        mm(pb(5, 0, 64), b("WL"), half("P", 0), False, True)
+        mm(pb(5, 64, 128), b("I"), half("P", 0))
+        mm(pb(7), b("P"), b("I"))
+        act(b("PT"), pb(7))
+        for a in range(2):
+            mm(b3("pb%d" % a, 0, 32), b("PT"), b3("EX", 64 + 32 * a, 96 + 32 * a), True, False)
+        mm(pb(4), b("P"), b("NB"), True, False)
+        for k, lo, hi in copies:
+            mm(pb(k, 0, 16 * (hi - lo)), b("PT"), b3("EX", lo, hi))
         if t:
             for h in range(2):
-                act(lane("PN", h), half("P", h))
+                gcp(lane("PN", h), half("P", h), 64)
             push("p", t, b("PN", 128 * t, 128 * t + 128))
-        cp(b("UI"), b("pb5", 0, 64))
+        cp(b("UI"), pb(5, 0, 64))
         ts(b("UM"), b("UI"), 4095, None, A.bitwise_and)
         tt(b("SQ"), b("UM"), b("UM"), A.mult)
-        ts(b("pb5", 64, 128), b("UM"), C(6), None, A.mult)
+        ts(pb(5, 128, 192), b("UM"), C(6), None, A.mult)
         ts(b("T1"), b("SQ"), 5, 4095, A.arith_shift_right, A.bitwise_and)
-        tt(b("H1"), b("T1"), b("pb5", 64, 128), A.add)
+        tt(b("H1"), b("T1"), pb(5, 128, 192), A.add)
         ts(b("H2"), b("H1"), 4095, None, A.bitwise_and)
         ts(b("C16"), b("H2"), n / 4096.0, -31.0 / 64.0, A.mult, A.add)
-        act(b("ZG", 512, 1024), ind(b("ZW", 0, n), b("C16", 32, 64)))
-        cp(b("ZG", 0, 512), ind(b("ZW", 0, n), b("C16", 0, 32)))
-        cp(b("CF"), b("C16"))
         for h in range(2):
-            cp(b("pb5", 128 + 64 * h, 192 + 64 * h), b("UM"))
-        for k in (0, 1):
-            z = b("ZG", 512 * k, 512 * k + 512)
-            mm(b("pb%d" % (2 + k), 0, 512), b("I"), z, False, True)
-            tt(b("AB", 512 * k, 512 * k + 512), z, b("pb%d" % k, 0, 512), A.max)
-            act(b("AB", 1024 + 512 * k, 1536 + 512 * k), b("pb%d" % (2 + k), 0, 512), F.Abs, scale=0.5)
-        mm(b("pb4"), b("P"), b("NB"), True, False)
+            act(half("U2", h), b("UM"))
+        def zsum(lo, hi, m):
+            mm(b("pb4", m, 128, 16, hi, lo), b("ZG", 16 * lo + m, 16 * hi, 16), b("NB", 0, 128, 16), False, False)
+        for a in range(2):
+            cp(b("ZG", 512 * a, 512 * a + 256), ind(ZW, b("C16", 32 * a, 32 * a + 16)))
+            act(b("ZG", 512 * a + 256, 512 * a + 512), ind(ZW, b("C16", 32 * a + 16, 32 * a + 32)))
+            mm(b3("pb%d" % a, 0, 32), b("NI"), b("ZG", 512 * a, 512 * a + 512), False, True)
+            if a == 0:
+                cp(b("CF"), b("C16"))
+                for h in range(2):
+                    mm(b("pb4", p0=64 * h, p=64 * h + 64), b("CF"), b("IH"), False, False)
+                for m in range(ZA):
+                    zsum(0, 32, m)
         for m in range(16):
-            mm(b("pb4", m, 128, 16, 64), b("ZG", m, 1024, 16), b("NB", 0, 128, 16), False, False)
-        for h in range(2):
-            mm(b("pb4", p0=64 * h, p=64 * h + 64), b("CF"), b("IH"), False, False)
-        if LV > 64:
-            mm(b("pb6", 0, W0 - 1024), b("PT"), b("EX", 1024, W0))
-        for m in range(16):
-            mm(b("pb4", m, 128, 16), b("AB", m, 2048, 16), b("B4"), False, m == 15)
-        for k in (0, 1):
-            act(b("PRS", 512 * k, 512 * k + 512), b("pb%d" % k, 0, 512))
-        if LV > 64:
-            act(b("PRS", 1024, W0), b("pb6", 0, W0 - 1024), scale=-1.0)
-        if t == 0:
-            cp(b("RW", 0, 768), b("RI"))
-            for k in range(16):
-                cp(b("SEL", 128 * k + k, 128 * k + 128, 16), b("B8"))
-        scan(b("SC"), b("RST"), b("pb4"), A.max, A.min)
-        tt(b("LM"), ind(b("SC"), b("KL")), b("MASK"), A.mult)
-        mm(b("pb4", 128, 136), b("LM"), b("B8F"))
-        cp(b("LI"), b("pb4", 128, 136))
-        ts(b("LA"), b("LI"), 2047, None, A.bitwise_and)
-        cp(b("L16"), b("LA"))
-        act(b("EF"), ind(b("RW", 0, n), b("L16")))
-        cp(b("E16"), ind(b("RW", 0, n), b("L16")))
-        act(b("pb7"), b("EF"), bias=77.0 * t)
-        tt(b("EU"), b("EF"), b("pb5", 128, 256), A.mult)
+            zsum(32 if m < ZA else 0, 64, m)
+        for q in range(2):
+            for a in range(2):
+                act(b3("AB", 64 + 32 * a, 96 + 32 * a, 8 * q, 8 * q + 8), b3("pb%d" % a, 0, 32, 8 * q, 8 * q + 8), F.Abs, scale=0.5)
+            for m in range(8 * q, 8 * q + 8):
+                tt(b3("AB", 0, 64, m, None), b("ZG", m, 1024, 16), pb(5, 64, 128), A.max)
+            for m in range(8 * q, 8 * q + 8):
+                mm(pb(4, m, 128, 16), b3("AB", 0, 128, m, None), b("B4"), False, m == 15)
+        for k, lo, hi in copies:
+            act(b("PRS", 16 * lo, 16 * hi), pb(k, 0, 16 * (hi - lo)))
+        def fill(i):
+            mm(sbank(i), b("PT"), b3("EX", SP[i][2], SP[i][3]), True, False)
+        fill(0)
+        fill(1)
+        if t:
+            act(b("RI", n - 128, n), b("YR", 128 * t - 128, 128 * t))
+        scan(b("SC"), b("RST"), pb(4), A.max, A.min)
+        ts(b("LA"), b("SC", 15, 128, 16), 2047, None, A.bitwise_and)
+        tt(b("LM"), ind(b("LA"), b("KL")), b("MASK"), A.mult)
+        mm(pb(4, 128, 136), b("LM"), b("B8H"))
+        cp(b("L16"), pb(4, 128, 136))
+        fill(2)
+        fill(3)
+        LST, VBS = ("E16", "E216"), ("VB", "VB2")
+        def vpiece(e, lo, hi):
+            tt(b(VBS[e], 16 * lo, 16 * hi), ind(XW, b(LST[e], lo, hi)), b("PRS", 16 * lo, 16 * hi), A.is_ge)
+        def sgather(i):
+            e, _, lo, hi = SP[i]
+            x = b("XG", 512 * i, 512 * i + 16 * (hi - lo))
+            act(x, ind(XW, b(LST[e], lo, hi)))
+            mm(sbank(i), b("NI"), x, False, True)
+        def ssign(i):
+            e, _, lo, hi = SP[i]
+            act(b(VBS[e], 16 * lo, 16 * hi), sbank(i), F.Sigmoid, bias=32.0, scale=-64.0)
+        VOTES = {(0, 1): 6, (0, 0): 4, (1, 1): 7, (1, 0): 6}
+        def count(e, h, ms_=range(16)):
+            for m in ms_:
+                mm(pb(VOTES[e, h], 0, 64), b("SEL", 128 * m, 128 * m + 128), b(VBS[e], 1024 * h + m, 1024 * h + 1024, 16), m == 0, e == 0 and m == 15)
+        def before(h):
+            v = pb(VOTES[0, h], 0, 64)
+            ts(half("BR", h), v, b("BAR"), None, A.is_lt)
+            ts(half("G9", h), v, 8.5, 128.0, A.is_ge, A.mult)
+            tt(half("Y1", h), half("BR", h), pb(5, 128 + 64 * h, 192 + 64 * h), A.mult)
+            tt(half("TH", h), half("G9", h), v, A.max)
+            tt(pb(5, 256 + 128 * h, 384 + 128 * h, 2), half("Y1", h), pb(5, 64 * h, 64 * h + 64), A.add)
+        def barred(h):
+            mm(pb(VOTES[1, h], 0, 64), b("I128"), half("BR", h), False, True)
+        def flag(h):
+            tt(b("FLI", 128 * h + 1, 128 * h + 128, 2), pb(VOTES[1, h], 0, 64), half("TH", h), A.is_ge)
+        def choose(h):
+            scan(b("FS", 128 * h, 128 * h + 128), b("FLI", 128 * h, 128 * h + 128), pb(5, 256 + 128 * h, 384 + 128 * h), A.mult, A.add)
+        act(b("E16"), ind(RW, b("L16")))
+        tt(b("EU"), ind(RW, b("L16")), b("U2"), A.mult)
+        act(pb(5), b("E16"), bias=77.0 * t)
+        sgather(0)
         ts(b("SH"), b("EU"), 5, None, A.arith_shift_right)
-        tt(b("SM"), b("SH"), b("pb7"), A.add)
+        ts(b("EH"), b("E16"), -2048.0, None, A.add)
+        tt(b("SM"), b("SH"), pb(5), A.add)
+        vpiece(0, 64, 64 + VA)
         ts(b("SA"), b("SM"), 4095, None, A.bitwise_and)
+        vpiece(0, 64 + VA, SP[0][2])
         cp(b("E216"), b("SA"))
-        for k in (2, 0):
-            for i, (lo, hi) in enumerate(parts):
-                mm(b("pb%d" % (k + i), 0, hi - lo), b("PT"), b("EX", lo, hi), True, False)
-        sets = (("E16", "XG", "VB", "VT", 2, 6), ("E216", "XG2", "VB2", "VT2", 0, 7))
-        for lst, xg, vb, vt, k, c in sets:
-            act(b(xg, 0, W2 - W0), ind(XW, b(lst, LV, 128)))
-            tt(b(vb, 0, W0), ind(XW, b(lst, 0, LV)), b("PRS", 0, W0), A.is_ge)
-            for i, (lo, hi) in enumerate(parts):
-                mm(b("pb%d" % (k + i), 0, hi - lo), b("I"), b(xg, lo - W0, hi - W0), False, True)
-        for lst, xg, vb, vt, k, c in sets:
-            for i, (lo, hi) in enumerate(parts):
-                act(b(vb, lo, hi), b("pb%d" % (k + i), 0, hi - lo), F.Sign, bias=0.5)
-        for lst, xg, vb, vt, k, c in sets:
-            if t == 0 and c == 6:
-                ts(C(8), C(0), LV - 0.5, -0.5, A.is_ge, A.mult)
-                ts(C(9), C(8), 1.0, None, A.add)
-                ts(C(10), C(8), -16.0, None, A.mult)
-            for m in range(16):
-                mm(b("pb%d" % c, m, 128, 16), b(vb, m, 2048, 16), b("B8"))
-            act(b(vt), b("pb%d" % c), F.Identity, C(10), C(9))
-            mm(b("pb%d" % c), b(vt), b("I"))
-        act(b("EFS"), b("EF"), scale=1.0 / 128.0)
+        ts(b("E2H"), b("SA"), -2048.0, None, A.add)
+        sgather(1)
+        ssign(0)
+        vpiece(0, SP[1][3], 64)
         if t == 0:
             for h in range(2):
-                ts(half("E128", h), b("EI", h, 128, 2), 1.0 / 128.0, None, A.mult)
+                ts(half("EBH", h), b("EI", h, 128, 2), -2048.0, None, A.add)
+            ts(b("NIH"), b("I"), -1.0, None, A.mult)
+            ts(b("I128"), b("I"), 128.0, None, A.mult)
+            ms(b("BAR"), 3.5)
+            ms(b("FLI"), 0.0)
+        def deltas():
+            mm(pb(5, 128, 256), b("IH"), b("EBH"), True, False)
+            mm(pb(5, 128, 256), b("NIH"), b("E2H"), False, False)
+            mm(pb(5, 0, 128), b("IH"), b("E2H"), False, False)
+            mm(pb(5, 0, 128), b("NIH"), b("EH"), False, False)
+            mm(pb(5, 257, 512, 2), b("IH"), b("EH"), False, True)
+        step = {"g": sgather, "s": ssign, "f": fill, "b": before, "r": barred, "l": flag, "h": choose, "d": lambda _: deltas(),
+                "c": lambda i: count(i // 4, i // 2 % 2, range(8 * (i % 2), 8 * (i % 2) + 8)),
+                "v": lambda h: vpiece(1, 64, SP[2][2]) if h else vpiece(1, SP[4][3], 64)}
+        for x in ORDER.split():
+            step[x[0]](int(x[1]))
+        if t == 0:
             for k in range(16):
-                ts(b("BC", 128 * k, 128 * k + 128), b("BB"), b("MASK", k, k + 1), None, A.mult)
-            cp(b("B8H"), b("BB", 0, 128, 16))
+                act(b("BC", 128 * k, 128 * k + 128), b("BB"), scale=b("MASK", k, k + 1))
             ts(b("I8"), b("I"), 8192.0, None, A.mult)
-            ms(b("ONESF"), 1.0)
+            ts(b("BB8"), b("BB"), 8192.0, None, A.mult)
+            ts(b("MBIG"), b("MASK"), -14336.0, 16384.0, A.mult, A.add)
+            for h in range(2):
+                ts(half("JNK", h), b("IOT", 0, 64), 4096.0, None, A.add)
+            tt(b("NXD"), b("JNK"), b("MASK"), A.mult)
             ms(b("RQ"), 255.0)
             ms(b("RQ", 0, 1024, 16), 0.0)
-        tt(b("pb5", 256, 384), b("SA"), b("EF"), A.subtract)
-        tt(b("pb5", 384, 512), b("E128"), b("EFS"), A.subtract)
-        ts(b("BR"), b("pb6"), b("BAR"), 128.0, A.is_lt, A.mult)
-        ts(b("G9"), b("pb6"), 9.0, 128.0, A.is_ge, A.mult)
-        tt(b("pb5", 384, 512), b("BR"), b("pb5", 384, 512), A.mult)
-        tt(b("pb6"), b("G9"), b("pb6"), A.max)
-        tt(b("BAS"), b("EF"), b("pb5", 384, 512), A.add)
-        tt(b("TH2"), b("BR"), b("pb6"), A.max)
-        act(b("BASC"), b("BAS"), bias=-2048.0)
-        if t < 3:
-            act(b("JNK"), b("BR"), scale=1.0 / 128.0, accum=b("CNT"))
-        tt(b("FL"), b("pb7"), b("TH2"), A.is_ge)
-        tt(b("pb5"), b("FL"), b("pb5", 256, 384), A.mult)
-        tt(b("FC"), b("BASC"), b("pb5"), A.add)
-        tt(b("FF"), b("BAS"), b("pb5"), A.add)
-        act(b("FQ"), half("FF", 0), bias=16.0)
+            ms(b("XT", 0, 16), 0.0)
+        fh = lambda h: b("FS", 128 * h + 1, 128 * h + 128, 2)
+        fall = b("FS", 1, 256, 2)
+        BC = lambda k: b("BC", 128 * k, 128 * k + 128)
+        spread = lambda k: b3("pb%d" % (k // 4), 4 * (k % 4), 4 * (k % 4) + 4) if k < 8 else pb(k // 4, 64 * (k % 4), 64 * (k % 4) + 64)
         for k in range(16):
-            mm(b("pb%d" % (k // 4), 64 * (k % 4), 64 * (k % 4) + 64), b("BC", 128 * k, 128 * k + 128), half("FC", 1))
+            mm(spread(k), BC(k), fh(1))
+        flag(0)
+        choose(0)
+        mm(pb(7, 0, 64), BC(0), fh(0))
+        mm(pb(6), BC(0), fall, True, False)
+        mm(pb(6), b("I"), b("MBIG"), False, False)
+        act(b("FQ"), fh(0), bias=2064.0)
         for k in range(16):
-            tt(half("EQ", k), half("FC", 0), b("pb%d" % (k // 4), 64 * (k % 4), 64 * (k % 4) + 64), A.is_equal)
-            mm(b("pb4", 0, 64), b("I8"), half("EQ", k), k == 0, k == 15)
-        for k in range(16):
-            mm(b("pb6", 0, 64), b("SEL", 128 * k, 128 * k + 128), half("EQ", k), k == 0, k == 15)
+            tt(half("EQ", k + 1), fh(0), spread(k), A.is_equal)
+            mm(pb(4, 0, 64), b("I8"), half("EQ", k + 1), k == 0, k == 15)
+            if k == 5:
+                tt(half("EQ", 0), fh(1), pb(7, 0, 64), A.is_equal)
+                mm(pb(6), b("BB8"), b("EQ", 0, 128), False, True)
         for h in range(2):
-            tt(b("pb5", 256 + 64 * h, 320 + 64 * h), b("NEW", 64 * t, 64 * t + 64), half("FF", h), A.subtract)
-        tt(b("Q16"), b("FQ"), b("pb4", 0, 64), A.min)
-        act(b("GQ", 0, 16 * QS), ind(XQ, b("Q16", 0, QS)))
+            scan(half("F0S", h), half("NXD", h), pb(6, 64 * h, 64 * h + 64), A.max, A.min)
+        tt(b("Q16"), b("FQ"), pb(4, 0, 64), A.min)
+        cp(b("MS", 72 * t, 72 * t + 8), b("F0S", 15, 128, 16))
+        for lo, hi in ((0, QA), (QA, QS)):
+            act(b("GQ", 16 * lo, 16 * hi), ind(XQ, b("Q16", lo, hi)))
         cp(b("GQ", 16 * QS, 1024), ind(XQ, b("Q16", QS, 64)))
-        for h, k in ((0, 4), (1, 6)):
-            ts(half("FL", h), b("pb%d" % k, 0, 64), 0.5, None, A.is_ge)
-        tt(b("pb5"), b("FL"), b("pb5", 256, 384), A.mult)
-        tt(b("FH"), b("FC"), b("pb5"), A.add)
-        mm(b("pb7"), b("FH"), b("BC", 0, 128))
-        scan(b("SQM", 16 * QS, 1024), b("RQ", 16 * QS, 1024), b("GQ", 16 * QS, 1024), A.min, A.max)
-        tt(b("FM"), b("MASK"), b("pb7"), A.mult)
-        mm(b("pb7", 256, 264), b("FM"), b("B8H"))
-        scan(b("SQM", 0, 16 * QS), b("RQ", 0, 16 * QS), b("GQ", 0, 16 * QS), A.min, A.max)
-        ts(b("MS", 72 * t, 72 * t + 8), b("pb7", 256, 264), 2048.0, None, A.add)
+        for lo, hi in ((QS, 64), (0, QA), (QA, QS)):
+            scan(b("SQM", 16 * lo, 16 * hi), b("RQ", 16 * lo, 16 * hi), b("GQ", 16 * lo, 16 * hi), A.min, A.max)
         cp(b("MS", 72 * t + 8, 72 * t + 72), b("SQM", 15, 1024, 16))
         push("m", t, b("MS", 72 * t, 72 * t + 72))
+        for k in range(16):
+            mm(pb(7, 64, 128), b("SEL", 128 * k, 128 * k + 128), half("EQ", k + 1), k == 0, k == 15)
         for h in range(2):
-            tt(lane("FS", h), half("FF", h), b("pb5", 64 * h, 64 * h + 64), A.add)
-        push("f", t, b("FS", 128 * t, 128 * t + 128))
+            mm(pb(5, 64 * h, 64 * h + 64), b("IH"), b("NEW", 64 * t, 64 * t + 64), h == 0, False)
+        mm(pb(5), b("NIH"), fall, False, True)
+        act(b("FF"), fall, bias=2048.0)
+        ts(half("FL", 0), pb(4, 0, 64), 0.5, None, A.is_ge)
+        ts(half("FL", 1), pb(7, 64, 128), 0.5, None, A.is_ge)
+        tt(pb(5), b("FL"), pb(5), A.mult)
+        for h in range(2):
+            tt(lane("FO", h), half("FF", h), pb(5, 64 * h, 64 * h + 64), A.add)
+        push("f", t, b("FO", 128 * t, 128 * t + 128))
         if t < 3:
-            mm(b("pb7", 384, 385), b("ONESF"), b("CNT"))
-            cp(b("CI", 0, 1), b("pb7", 384, 385))
+            mm(pb(6), b("ONES"), b("BR"))
+            act(b("JNK"), pb(6), accum=b("CNT"))
+            cp(b("CI", 0, 1), b("CNT"))
             ts(b("CI", 1, 2), b("CI", 0, 1), 1, None, A.bitwise_and)
-            ts(b("BAR"), b("CI", 1, 2), 4.0, None, A.add)
-        ml = b("ML", 72 * t, 72 * t + 72)
+            ts(b("BAR"), b("CI", 1, 2), 3.5, None, A.add)
         arrive("p", t, b("ZW", n, n + 128))
-        arrive("f", t, b("RW", n, n + 128))
-        arrive("m", t, ml)
+        arrive("f", t, b("YR", 128 * t, 128 * t + 128))
+        arrive("m", t, b("ML", 72 * t, 72 * t + 72))
         for h in range(2):
             act(half("PB", h), b("ZW", n + h, n + 128, 2), bias=2302.75)
         B = 3856 + 64 * t
         cp(b("XT", B, B + 64), b("ML", 72 * t + 8, 72 * t + 72))
-        tt(b("AF"), ind(XW, b("ML", 72 * t, 72 * t + 8)), b("PB"), A.subtract)
-        if t < 3:
-            ts(b("P"), b("AF"), -0.5, -1024.0, A.mult, A.add)
-        else:
-            for h in range(2):
-                ts(b("YP", h, 128, 2), half("AF", h), -0.5, -1024.0, A.mult, A.add)
+        act(b("XT", 4112, 4176), b("ML", 72 * t + 8, 72 * t + 72))
+        for h in range(2):
+            tt(half("AF", h), ind(XN, b("ML", 72 * t + 4 * h, 72 * t + 4 * h + 4)), half("PB", h), A.subtract)
+            ts(half("P", h) if t < 3 else b("YP", h, 128, 2), half("AF", h), -0.5, -1024.0, A.mult, A.add)
         if t == 2:
-            dma("Y", "o0", T.yr[:, 0:384], T.RW[:, 768:1152], [], [b("RW", 768, 1152)])
-    dma("Y", "o1", T.yr[:, 384:512], T.RW[:, 1152:1280], [], [b("RW", 1152, 1280)])
+            dma("Y", "o0", T.yr[:, 0:384], T.YR[:, 0:384], [], [b("YR", 0, 384)])
+    dma("Y", "o1", T.yr[:, 384:512], T.YR[:, 384:512], [], [b("YR", 384, 512)])
     dma("S", "o2", T.yp[:], T.YP[:], [], [b("YP")])
     for s in sorted(total):
         if clk["G"].get(s, 0) < total[s]:

@@ -6,33 +6,42 @@ VA = 8
 ZA = 4
 QA = 30
 QS = 38
+XA = 2064
 _D = {"f": "float32", "b": "bfloat16", "h": "float16", "i": "int32", "u": "uint16"}
-_S = """XT 4176 b;RI 1152 i;YR 512 f;ZW 1280 b;EI 128 i;EBH 128 h;WI 16 i;WI2 16 i;KI 16 i;COL 16 f;PI 128 b;PN 512 b;P 128 b;PT 128 b
+_S = """XT 4176 b;RI 1152 i;YR 512 f;ZW 1280 b;EI 130 i;EBH 128 h;WH 128 b;WL 128 b;KC 1 f
+XT2 4176 b;RI2 1152 i;ZW2 1280 b;EI2 130 i;EBH2 128 h;WH2 128 b;WL2 128 b;KC2 1 f;BAR2 1 f
+WI2 16 i;COL 16 f;PI 128 b;PN 512 b;P 128 b;PT 128 b
 PRS 2048 b;PB 128 f;IP 4 i;IOT 128 f;R16 128 f;G16 128 f;NEW 256 h;KLI 8 i;KL 8 u;I 128 b;EX 128x16 b;BB 128 b;NB 128 b
-B4 8 b;B8 8 b;B8H 8 h;IH 128 h;NIH 128 h;I8 128 b;I128 128 b;BB8 128 b;ONES 128 b;MASK 128 f;MBIG 128 b;NXD 128 f;RST 128 f;RQ 1024 b
-SEL 2048 b;BC 2048 h;WH 128 b;WL 128 b;BAR 1 f;UI 64 i;UM 64 i;U2 128 f;SQ 64 i;T1 64 i;H1 64 i;H2 64 i;C16 64 u;CF 64 h
+B4 8 b;B8H 8 h;IH 128 h;NIH 128 h;I8 128 b;I128 128 b;BB8 128 b;ONES 128 b;C2K 128 b;MASK 128 f;MBIG 128 b;NXD 128 f;RST 128 f;RQ 1024 b
+SEL 144 b;BC 2048 h;BAR 1 f;BARS 1 f;UI 64 i;UM 64 i;U2 128 f;SQ 64 i;T1 64 i;H1 64 i;H2 64 i;C16 64 u;CF 64 h
 ZG 1024 b;AB 128x16 b;SC 128 i;LA 8 i;LM 128 h;L16 8 u;E16 128 u;EH 128 h;EU 128 i;SH 128 i;SM 128 i;SA 128 i;E216 128 u;E2H 128 h
 VB 2048 b;VB2 2048 b;XG 2560 b;NI 128 b;BR 128 b;G9 128 f;TH 128 b;Y1 128 f;FLI 256 b;FS 256 h;JNK 128 f;CNT 1 f;CI 2 i
-FQ 64 f;EQ 1088 b;Q16 64 u;GQ 1024 b;SQM 1024 b;F0S 128 f;FL 128 f;FF 128 f;FO 512 f;MS 288 u;ML 288 u;AF 128 h;YP 128 f
+FQ 64 f;EQ 1088 b;Q16 64 u;GQ 1024 b;SQM 1024 b;F0S 128 f;FL 256 b;FF 256 f;FO 512 f;MS 288 u;ML 288 u;AF 128 h;YP 128 f
 relp 512 b;relf 512 f;relm 288 u"""
 SHAPE = {x.split()[0]: [int(v) for v in x.split()[1].split("x")] for x in _S.replace("\n", ";").split(";")}
 SCRATCH = {x.split()[0]: ("sbuf", [128] + SHAPE[x.split()[0]], _D[x.split()[2]]) for x in _S.replace("\n", ";").split(";")}
 for _b in range(8):
     SCRATCH["pb%d" % _b] = ("psum", [128, 32, 16] if _b < 2 else [128, 512], "float32")
-SEMAPHORES = (["sv", "sa", "st", "sg", "ls", "rl", "lp", "lw", "lk", "lz", "lr", "le", "lx0", "lx1", "o0", "o1", "o2"]
-              + ["a%s%d" % (k, t) for k in "pfm" for t in range(4)])
 N = 8
+STAND = 3
+COPIES = (("EI", 0, 130), ("XT", 16, XA), ("XT", XA, 3856), ("ZW", 0, 768), ("XT", 3856, 4112), ("ZW", 768, 1024), ("RI", 0, 768), ("RI", 768, 1024))
+MESSAGES = ("p0", "m0", "f0", "p1", "m1", "f1", "m2", "b2", "f2", "p3", "m3", "f3")
+SEMAPHORES = (["sv", "sa", "st", "sg", "ls", "lu", "rl", "lp", "lw", "lk", "lz", "lr", "le", "lx0", "lx1", "o0", "o1", "o2"]
+              + ["a" + m for m in MESSAGES] + ["ak%d" % i for i in range(len(COPIES))])
 
 
-def nxt(r, t):
-    return (r + 1 + t % 3) % N
+def shift(m):
+    if m[0] in "kb":
+        return -STAND
+    t = int(m[1])
+    return 1 + t % 3 + (STAND if t == STAND else 0)
 
 
-def hops(T, topo, src, dst, kind):
-    if topo.may_write(src, dst):
+def hops(T, topo, src, dst, m):
+    if m[0] != "k" and topo.may_write(src, dst):
         return [dst]
     c = [x for x in topo.cores_of(src) if topo.die(x) == topo.die(src) and topo.may_write(x, dst) and T.rank_of(x) is None]
-    return [c[0] if kind == "f" else c[-1], dst]
+    return [c[0] if m[0] == "k" else c[-1], dst]
 
 
 def send(g, topo, src, dst, out, in_, rsem, lsem):
@@ -41,28 +50,28 @@ def send(g, topo, src, dst, out, in_, rsem, lsem):
     return len(topo.engines(src, dst))
 
 
-def final_place(T, kind, t):
-    n = 768 + 128 * t
-    if kind == "p":
-        return T.ZW[:, n:n + 128], T.relp[:, 128 * t:128 * t + 128]
-    if kind == "f":
-        return T.YR[:, 128 * t:128 * t + 128], T.relf[:, 128 * t:128 * t + 128]
-    return T.ML[:, 72 * t:72 * t + 72], T.relm[:, 72 * t:72 * t + 72]
+def places(m):
+    t = int(m[1])
+    if m[0] == "k":
+        buf, lo, hi = COPIES[t]
+        return (buf + "2", lo, hi), (buf + "2", lo, hi)
+    if m[0] == "b":
+        return ("BAR2", 0, 1), ("BAR2", 0, 1)
+    buf, rel, lo, w = {"p": ("ZW", "relp", 768, 128), "f": ("YR", "relf", 0, 128), "m": ("ML", "relm", 0, 72)}[m[0]]
+    return (buf, lo + w * t, lo + w * t + w), (rel, w * t, w * t + w)
 
 
 def relay_program(g, core, T, topo):
     sent = 0
-    for t in range(4):
-        for kind in "pmf":
-            for r in range(N):
-                src, dst = T.cores[r], T.cores[nxt(r, t)]
-                h = hops(T, topo, src, dst, kind)
-                if len(h) < 2 or h[0] != core:
-                    continue
-                sem = T.sem["a%s%d" % (kind, t)]
-                g.wait_ge(sem, len(topo.engines(src, core)))
-                a, b = final_place(T, kind, t)
-                sent += send(g, topo, core, dst, a, b, sem, T.sem.rl)
+    for m in MESSAGES + tuple("k%d" % i for i in range(len(COPIES))):
+        for r in range(N):
+            src, dst = T.cores[r], T.cores[(r + shift(m)) % N]
+            h = hops(T, topo, src, dst, m)
+            if len(h) < 2 or h[0] != core:
+                continue
+            g.wait_ge(T.sem["a" + m], len(topo.engines(src, core)))
+            a, b = [T[x[0]][:, x[1]:x[2]] for x in places(m)]
+            sent += send(g, topo, core, dst, a, b, T.sem["a" + m], T.sem.rl)
     if sent:
         g.wait_ge(T.sem.rl, sent)
 
@@ -166,72 +175,100 @@ def rank_program(g, core, T, topo):
             op("G", lambda e: e.iota(out[0], pat, base, cm, allow_small_or_imprecise_dtypes=True), [out], [])
         else:
             op("G", lambda e: e.iota(out[0], pat, base, cm), [out], [])
-    def gcp(out, a, n): op("G", lambda e: e.affine_select(out[0], a[0], [[0, n]], A.is_ge, 0.0, 0, 0), [out], [a])
+    def keep(out, a, pat, base): op("G", lambda e: e.affine_select(out[0], a[0], pat, A.is_equal, 0.0, base, 0), [out], [a])
 
     sent = [0]
-    def push(kind, t, x):
+    def push(m, x, watch=None):
         waits("G", regions([x], []))
-        dst = T.cores[nxt(rank, t)]
-        h = hops(T, topo, core, dst, kind)
-        sent[0] += send(g, topo, core, h[0], final_place(T, kind, t)[len(h) - 1], x[0], T.sem["a%s%d" % (kind, t)], T.sem.ls)
-    def arrive(kind, t, x):
-        src = T.cores[(rank - 1 - t % 3) % N]
-        h = [src] + hops(T, topo, src, core, kind)
-        sem, cnt = "a%s%d" % (kind, t), len(topo.engines(h[-2], core))
+        h = hops(T, topo, core, T.cores[(rank + shift(m)) % N], m)
+        n_ = send(g, topo, core, h[0], b(*places(m)[len(h) - 1])[0], x[0], T.sem["a" + m], T.sem[watch or "ls"])
+        if watch:
+            total[watch] = n_
+            evc[(watch, n_)] = {watch: n_}
+            note(*x[1][0], False, watch, n_, "D")
+        else:
+            sent[0] += n_
+    def arrive(m):
+        src = T.cores[(rank - shift(m)) % N]
+        sem, cnt = "a" + m, len(topo.engines(([src] + hops(T, topo, src, core, m))[-2], core))
         total[sem] = cnt
         evc[(sem, cnt)] = {sem: cnt}
-        note(*x[1][0], True, sem, cnt, "D")
+        note(*b(*places(m)[0])[1][0], True, sem, cnt, "D")
+    def copy_out(i): push("k%d" % i, b(*COPIES[i]), "lu" if i == 4 else None)
 
     dma("Y", "lp", T.PI[:], T.p0[:], [b("PI")], [])
-    dma("S", "lw", T.WI[:, 0:1], T.wt[:], [b("WI")], [])
-    dma("Y", "lk", T.KI[:, 0:1], T.km[:], [b("KI")], [])
-    dma("S", "lz", T.ZW[:, 0:768], T.zp[:], [b("ZW", 0, 768)], [])
+    dma("S", "lw", T.EI[:, 128:129], T.wt[:], [b("EI", 128, 129)], [])
+    dma("S", "lk", T.EI[:, 129:130], T.km[:], [b("EI", 129, 130)], [])
+    dma("Y", "lz", T.ZW[:, 0:768], T.zp[:], [b("ZW", 0, 768)], [])
     dma("Y", "lr", T.RI[:, 0:768], T.rt[:], [b("RI", 0, 768)], [])
     dma("S", "lx0", T.XT[:, 16:2064], T.ax[:, 0:2048], [b("XT", 16, 2064)], [])
     dma("Y", "lx1", T.XT[:, 2064:4112], T.ax[:, 2048:4096], [b("XT", 2064, 4112)], [])
-    dma("Y", "le", T.EI[:], T.ex[:], [b("EI")], [])
+    dma("Y", "le", T.EI[:, 0:128], T.ex[:], [b("EI", 0, 128)], [])
+    for m in MESSAGES + tuple("k%d" % i for i in range(len(COPIES))):
+        arrive(m)
     C = lambda j: b("COL", j, j + 1)
     IP = lambda j: b("IP", j, j + 1)
     half = lambda buf, h: b(buf, 64 * h, 64 * h + 64)
     pb = lambda k, lo=0, hi=128, st=1: b("pb%d" % k, lo, hi, st)
+    BC = lambda k: b("BC", 128 * k, 128 * k + 128)
+    SEL = lambda k: b("SEL", 16 - k, 144 - k)
+    def weights(x):
+        ts(b("WI2", 0, 1), b("EI" + x, 128, 129), 6, None, A.arith_shift_right)
+        ts(b("WI2", 1, 2), b("EI" + x, 128, 129), 63, None, A.bitwise_and)
+        for j in range(2):
+            cp(C(4 + j), b("WI2", j, j + 1))
+        ts(b("WH" + x), b("BB"), C(4), 64.0, A.mult, A.mult)
+        ts(b("WL" + x), b("BB"), C(5), None, A.mult)
+        act(b("KC" + x), b("EI" + x, 129, 130))
+    def explicit(x):
+        for h in range(2):
+            act(half("EBH" + x, h), b("EI" + x, h, 128, 2), bias=-2048.0)
     iota(IP(0), [[0, 1]], 0, 1, False)
-    iota(b("G16"), [[1, 8], [0, 16]], 0, 0)
     iota(b("IOT"), [[1, 128]], 0, 0)
+    iota(b("G16"), [[1, 8], [0, 16]], 0, 0)
     iota(b("R16"), [[0, 8], [1, 16]], 0, 0)
     iota(b("KLI"), [[1, 8]], 0, 0, False)
-    push("p", 0, b("PI"))
-    iota(b("NEW"), [[1, 256]], 3840 - 2048, 0)
     ms(b("RST"), -1.0e9)
-    ms(b("SEL"), 0.0)
-    ms(b("RST", 0, 128, 16), 1.0e9)
+    ms(b("FLI"), 0.0)
+    cp(C(0), IP(0))
     ts(IP(1), IP(0), 15, None, A.bitwise_and)
     ts(IP(2), IP(0), 4, None, A.arith_shift_right)
-    for j in range(3):
+    ms(b("RST", 0, 128, 16), 1.0e9)
+    for j in (1, 2):
         cp(C(j), IP(j))
-    ts(b("BB"), b("G16"), C(2), None, A.is_equal)
+    act(b("ONES"), b("IOT"), F.Sigmoid, bias=40.0)
     ts(b("I"), b("IOT"), C(0), None, A.is_equal)
-    act(b("ONES"), b("G16"), F.Sigmoid, bias=40.0)
+    ms(b("BAR"), 3.5)
     cp(b3("EX", 0, 128, 0, None), b("I"))
     ts(b("NI"), b("I"), -1.0, None, A.mult)
+    cp(b3("EX", 0, 128, 1, 2), b3("EX", 0, 128, 0, 1))
+    ts(b("BB"), b("G16"), C(2), None, A.is_equal)
+    cp(b3("EX", 0, 128, 2, 4), b3("EX", 0, 128, 0, 2))
+    ms(b("XT", 0, 16), 0.0)
+    cp(b3("EX", 0, 128, 4, 8), b3("EX", 0, 128, 0, 4))
     ts(b("MASK"), b("R16"), C(1), None, A.is_equal)
-    for k in (1, 2, 4, 8):
-        cp(b3("EX", 0, 128, k, 2 * k), b3("EX", 0, 128, 0, k))
-    for h in range(2):
-        cp(half("P", h), b("PI", h, 128, 2))
-    ts(b("WI2", 0, 1), b("WI", 0, 1), 6, None, A.arith_shift_right)
-    ts(b("WI2", 1, 2), b("WI", 0, 1), 63, None, A.bitwise_and)
-    for j in range(2):
-        cp(C(4 + j), b("WI2", j, j + 1))
-    ts(b("WH"), b("BB"), C(4), 64.0, A.mult, A.mult)
-    ts(b("WL"), b("BB"), C(5), None, A.mult)
-    cp(C(6), b("KI", 0, 1))
+    cp(half("P", 0), b("PI", 0, 128, 2))
+    weights("")
+    act(half("P", 1), b("PI", 1, 128, 2))
+    push("p0", b("PI"))
+    iota(b("NEW"), [[1, 256]], 3840 - 2048, 0)
+    waits("G", regions([b("XT", 16, 4112)], []))
+    for i in range(2):
+        copy_out(i)
     act(b("NB"), b("BB"), scale=-2048.0)
     act(b("B4"), b("BB", 0, 128, 16), scale=4096.0)
     act(b("IH"), b("I"))
     act(b("B8H"), b("BB", 0, 128, 16))
     act(b("KL"), b("KLI"))
-    for k in range(16):
-        act(b("SEL", 128 * k + k, 128 * k + 128, 16), b("BB", 0, 128, 16))
+    bcv = lambda k: lambda: ts(BC(k), b("BB"), b("MASK", k, k + 1), None, A.mult)
+    later = [bcv(k) for k in range(16)] + [
+        lambda: ts(b("NIH"), b("I"), -1.0, None, A.mult), lambda: ts(b("I128"), b("I"), 128.0, None, A.mult),
+        lambda: ts(b("I8"), b("I"), 8192.0, None, A.mult), lambda: ts(b("BB8"), b("BB"), 8192.0, None, A.mult),
+        lambda: ts(b("MBIG"), b("MASK"), -14336.0, 16384.0, A.mult, A.add), lambda: ms(b("C2K"), 2048.0), lambda: ms(b("FL"), 0.0),
+        lambda: ms(b("XT2", 0, 16), 0.0), lambda: ms(b("SEL"), 0.0), lambda: cp(b("SEL", 16, 144, 16), b("BB", 0, 128, 16))]
+    def spare(k):
+        for _ in range(min(k, len(later))):
+            later.pop(0)()
 
     SP = ((0, 0, 128 - SW[0], 128), (0, 1, 0, SW[1]), (1, 2, 128 - SW[2], 128), (1, 3, 0, SW[3]), (1, 0, SW[3], SW[3] + SW[4]))
     v0, v1 = min(SW[1], SW[3] + SW[4]), 128 - min(SW[0], SW[2])
@@ -239,14 +276,43 @@ def rank_program(g, core, T, topo):
     def sbank(i):
         _, k, lo, hi = SP[i]
         return b3("pb%d" % k, 0, hi - lo) if k < 2 else pb(k, 0, 16 * (hi - lo))
-    XW, XQ, XN = b("XT", 16, 4112), b("XT", 0, 4112), b("XT", 16, 4176)
+    fh = lambda h: b("FS", 128 * h + 1, 128 * h + 128, 2)
+    fall = b("FS", 1, 256, 2)
+
+    def names_prepare(t):
+        for k in range(16):
+            mm(pb(7, 64, 128), SEL(k), half("EQ", k + 1), k == 0, k == 15)
+        for h in range(2):
+            mm(pb(3, 2 * h, 256, 4), b("IH"), b("NEW", 64 * t, 64 * t + 64), h == 0, False)
+            mm(pb(3, 2 * h, 256, 4), b("NIH"), fh(h), False, False)
+            mm(pb(3, 2 * h + 1, 256, 4), b("IH"), fh(h), False, False)
+        mm(pb(3, 1, 256, 2), b("I"), b("C2K"), False, True)
+    def names_flags():
+        act(b("FL", 1, 256, 4), pb(4, 0, 64), F.Sign)
+        act(b("FL", 3, 256, 4), pb(7, 64, 128), F.Sign)
+    def names():
+        scan(b("FF"), b("FL"), pb(3, 0, 256), A.mult, A.add)
+    def names_out(t):
+        act(b("FO", 128 * t, 128 * t + 128), b("FF", 1, 256, 2))
+        push("f%d" % t, b("FO", 128 * t, 128 * t + 128))
+    def bar_count():
+        mm(pb(6), b("ONES"), b("BR"))
+        act(b("JNK"), pb(6), accum=b("CNT"))
+    bar = [lambda: cp(b("CI", 0, 1), b("CNT")), lambda: ts(b("CI", 1, 2), b("CI", 0, 1), 1, None, A.bitwise_and)]
+
     for t in range(4):
         n = 768 + 128 * t
-        lane = lambda buf, h: b(buf, 128 * t + h, 128 * t + 128, 2)
-        ZW, RW = b("ZW", 0, n), b("RI", 0, n)
-        mm(pb(5, 0, 64), b("WH"), half("P", 0), True, False)
-        mm(pb(5, 0, 64), b("WL"), half("P", 0), False, True)
+        x = "2" if t == STAND else ""
+        stay = t + 1 == STAND
+        XW, XQ = b("XT" + x, 16, 4112), b("XT" + x, 0, 4112)
+        ZW, RW = b("ZW" + x, 0, n), b("RI" + x, 0, n)
+        if t == STAND:
+            later += bar + [lambda: ts(b("BARS"), b("CI", 1, 2), 3.5, None, A.add), lambda: push("b2", b("BARS"))]
+        mm(pb(5, 0, 64), b("WH" + x), half("P", 0), True, False)
+        mm(pb(5, 0, 64), b("WL" + x), half("P", 0), False, True)
         mm(pb(5, 64, 128), b("I"), half("P", 0))
+        if t == 0:
+            cp(b3("EX", 0, 128, 8, 16), b3("EX", 0, 128, 0, 8))
         mm(pb(7), b("P"), b("I"))
         act(b("PT"), pb(7))
         for a in range(2):
@@ -254,18 +320,27 @@ def rank_program(g, core, T, topo):
         mm(pb(4), b("P"), b("NB"), True, False)
         for k, lo, hi in copies:
             mm(pb(k, 0, 16 * (hi - lo)), b("PT"), b3("EX", lo, hi))
+        cp(b("UI"), pb(5, 0, 64))
+        spare(1)
+        ts(b("UM"), b("UI"), 4095, None, A.bitwise_and)
+        spare(1)
+        tt(b("SQ"), b("UM"), b("UM"), A.mult)
+        ts(pb(5, 128, 192), b("UM"), b("KC" + x), None, A.mult)
+        ts(b("T1"), b("SQ"), 5, 4095, A.arith_shift_right, A.bitwise_and)
+        spare(1)
+        tt(b("H1"), b("T1"), pb(5, 128, 192), A.add)
+        spare(1)
+        ts(b("H2"), b("H1"), 4095, None, A.bitwise_and)
+        spare(1)
+        ts(b("C16"), b("H2"), n / 4096.0, -31.0 / 64.0, A.mult, A.add)
+        spare(1)
         if t:
             for h in range(2):
-                gcp(lane("PN", h), half("P", h), 64)
-            push("p", t, b("PN", 128 * t, 128 * t + 128))
-        cp(b("UI"), pb(5, 0, 64))
-        ts(b("UM"), b("UI"), 4095, None, A.bitwise_and)
-        tt(b("SQ"), b("UM"), b("UM"), A.mult)
-        ts(pb(5, 128, 192), b("UM"), C(6), None, A.mult)
-        ts(b("T1"), b("SQ"), 5, 4095, A.arith_shift_right, A.bitwise_and)
-        tt(b("H1"), b("T1"), pb(5, 128, 192), A.add)
-        ts(b("H2"), b("H1"), 4095, None, A.bitwise_and)
-        ts(b("C16"), b("H2"), n / 4096.0, -31.0 / 64.0, A.mult, A.add)
+                keep(b("ZW2", n + h, n + 128, 2) if stay else b("PN", 128 * t + h, 128 * t + 128, 2), half("P", h), [[0, 64]], 0)
+            if not stay:
+                push("p%d" % t, b("PN", 128 * t, 128 * t + 128))
+        for i in {1: (2, 3), 2: (4, 5, 6)}.get(t, ()):
+            copy_out(i)
         for h in range(2):
             act(half("U2", h), b("UM"))
         def zsum(lo, hi, m):
@@ -289,19 +364,31 @@ def rank_program(g, core, T, topo):
                 tt(b3("AB", 0, 64, m, None), b("ZG", m, 1024, 16), pb(5, 64, 128), A.max)
             for m in range(8 * q, 8 * q + 8):
                 mm(pb(4, m, 128, 16), b3("AB", 0, 128, m, None), b("B4"), False, m == 15)
+        if t == STAND:
+            names()
+            act(b("RI2", n - 128, n), b("FF", 1, 256, 2))
+        spare(4)
         for k, lo, hi in copies:
             act(b("PRS", 16 * lo, 16 * hi), pb(k, 0, 16 * (hi - lo)))
         def fill(i):
             mm(sbank(i), b("PT"), b3("EX", SP[i][2], SP[i][3]), True, False)
         fill(0)
         fill(1)
-        if t:
+        if t in (1, 2):
             act(b("RI", n - 128, n), b("YR", 128 * t - 128, 128 * t))
+        if t == 0:
+            explicit("")
+        if t == 2:
+            copy_out(7)
         scan(b("SC"), b("RST"), pb(4), A.max, A.min)
+        spare(1)
         ts(b("LA"), b("SC", 15, 128, 16), 2047, None, A.bitwise_and)
+        spare(1)
         tt(b("LM"), ind(b("LA"), b("KL")), b("MASK"), A.mult)
+        spare(3)
         mm(pb(4, 128, 136), b("LM"), b("B8H"))
         cp(b("L16"), pb(4, 128, 136))
+        spare(1)
         fill(2)
         fill(3)
         LST, VBS = ("E16", "E216"), ("VB", "VB2")
@@ -309,19 +396,19 @@ def rank_program(g, core, T, topo):
             tt(b(VBS[e], 16 * lo, 16 * hi), ind(XW, b(LST[e], lo, hi)), b("PRS", 16 * lo, 16 * hi), A.is_ge)
         def sgather(i):
             e, _, lo, hi = SP[i]
-            x = b("XG", 512 * i, 512 * i + 16 * (hi - lo))
-            act(x, ind(XW, b(LST[e], lo, hi)))
-            mm(sbank(i), b("NI"), x, False, True)
+            y = b("XG", 512 * i, 512 * i + 16 * (hi - lo))
+            act(y, ind(XW, b(LST[e], lo, hi)))
+            mm(sbank(i), b("NI"), y, False, True)
         def ssign(i):
             e, _, lo, hi = SP[i]
             act(b(VBS[e], 16 * lo, 16 * hi), sbank(i), F.Sigmoid, bias=32.0, scale=-64.0)
         VOTES = {(0, 1): 6, (0, 0): 4, (1, 1): 7, (1, 0): 6}
-        def count(e, h, ms_=range(16)):
-            for m in ms_:
-                mm(pb(VOTES[e, h], 0, 64), b("SEL", 128 * m, 128 * m + 128), b(VBS[e], 1024 * h + m, 1024 * h + 1024, 16), m == 0, e == 0 and m == 15)
+        def count(e, h, slots):
+            for m in slots:
+                mm(pb(VOTES[e, h], 0, 64), SEL(m), b(VBS[e], 1024 * h + m, 1024 * h + 1024, 16), m == 0, e == 0 and m == 15)
         def before(h):
             v = pb(VOTES[0, h], 0, 64)
-            ts(half("BR", h), v, b("BAR"), None, A.is_lt)
+            ts(half("BR", h), v, b("BAR" + x), None, A.is_lt)
             ts(half("G9", h), v, 8.5, 128.0, A.is_ge, A.mult)
             tt(half("Y1", h), half("BR", h), pb(5, 128 + 64 * h, 192 + 64 * h), A.mult)
             tt(half("TH", h), half("G9", h), v, A.max)
@@ -334,11 +421,13 @@ def rank_program(g, core, T, topo):
             scan(b("FS", 128 * h, 128 * h + 128), b("FLI", 128 * h, 128 * h + 128), pb(5, 256 + 128 * h, 384 + 128 * h), A.mult, A.add)
         act(b("E16"), ind(RW, b("L16")))
         tt(b("EU"), ind(RW, b("L16")), b("U2"), A.mult)
+        spare(1)
         act(pb(5), b("E16"), bias=77.0 * t)
         sgather(0)
         ts(b("SH"), b("EU"), 5, None, A.arith_shift_right)
         ts(b("EH"), b("E16"), -2048.0, None, A.add)
         tt(b("SM"), b("SH"), pb(5), A.add)
+        spare(len(later))
         vpiece(0, 64, 64 + VA)
         ts(b("SA"), b("SM"), 4095, None, A.bitwise_and)
         vpiece(0, 64 + VA, SP[0][2])
@@ -347,15 +436,8 @@ def rank_program(g, core, T, topo):
         sgather(1)
         ssign(0)
         vpiece(0, SP[1][3], 64)
-        if t == 0:
-            for h in range(2):
-                ts(half("EBH", h), b("EI", h, 128, 2), -2048.0, None, A.add)
-            ts(b("NIH"), b("I"), -1.0, None, A.mult)
-            ts(b("I128"), b("I"), 128.0, None, A.mult)
-            ms(b("BAR"), 3.5)
-            ms(b("FLI"), 0.0)
         def deltas():
-            mm(pb(5, 128, 256), b("IH"), b("EBH"), True, False)
+            mm(pb(5, 128, 256), b("IH"), b("EBH" + x), True, False)
             mm(pb(5, 128, 256), b("NIH"), b("E2H"), False, False)
             mm(pb(5, 0, 128), b("IH"), b("E2H"), False, False)
             mm(pb(5, 0, 128), b("NIH"), b("EH"), False, False)
@@ -363,28 +445,24 @@ def rank_program(g, core, T, topo):
         step = {"g": sgather, "s": ssign, "f": fill, "b": before, "r": barred, "l": flag, "h": choose, "d": lambda _: deltas(),
                 "c": lambda i: count(i // 4, i // 2 % 2, range(8 * (i % 2), 8 * (i % 2) + 8)),
                 "v": lambda h: vpiece(1, 64, SP[2][2]) if h else vpiece(1, SP[4][3], 64)}
-        for x in ORDER.split():
-            step[x[0]](int(x[1]))
+        for y in ORDER.split():
+            step[y[0]](int(y[1]))
+        if t == STAND:
+            names_out(t - 1)
         if t == 0:
-            for k in range(16):
-                act(b("BC", 128 * k, 128 * k + 128), b("BB"), scale=b("MASK", k, k + 1))
-            ts(b("I8"), b("I"), 8192.0, None, A.mult)
-            ts(b("BB8"), b("BB"), 8192.0, None, A.mult)
-            ts(b("MBIG"), b("MASK"), -14336.0, 16384.0, A.mult, A.add)
+            act(b("JNK"), b("MASK"), scale=4096.0)
             for h in range(2):
-                ts(half("JNK", h), b("IOT", 0, 64), 4096.0, None, A.add)
-            tt(b("NXD"), b("JNK"), b("MASK"), A.mult)
+                tt(half("NXD", h), half("MASK", h), b("IOT", 0, 64), A.mult)
             ms(b("RQ"), 255.0)
-            ms(b("RQ", 0, 1024, 16), 0.0)
-            ms(b("XT", 0, 16), 0.0)
-        fh = lambda h: b("FS", 128 * h + 1, 128 * h + 128, 2)
-        fall = b("FS", 1, 256, 2)
-        BC = lambda k: b("BC", 128 * k, 128 * k + 128)
         spread = lambda k: b3("pb%d" % (k // 4), 4 * (k % 4), 4 * (k % 4) + 4) if k < 8 else pb(k // 4, 64 * (k % 4), 64 * (k % 4) + 64)
         for k in range(16):
             mm(spread(k), BC(k), fh(1))
         flag(0)
+        if t == 0:
+            ms(b("RQ", 0, 1024, 16), 0.0)
         choose(0)
+        if t == 0:
+            tt(b("NXD"), b("NXD"), b("JNK"), A.add)
         mm(pb(7, 0, 64), BC(0), fh(0))
         mm(pb(6), BC(0), fall, True, False)
         mm(pb(6), b("I"), b("MBIG"), False, False)
@@ -402,41 +480,46 @@ def rank_program(g, core, T, topo):
         for lo, hi in ((0, QA), (QA, QS)):
             act(b("GQ", 16 * lo, 16 * hi), ind(XQ, b("Q16", lo, hi)))
         cp(b("GQ", 16 * QS, 1024), ind(XQ, b("Q16", QS, 64)))
+        names_prepare(t)
+        if t < 3:
+            bar_count()
+        names_flags()
+        B = 3856 + 64 * t
+        if stay:
+            for h in range(2):
+                act(half("PB", h), half("P", h), bias=2302.75)
         for lo, hi in ((QS, 64), (0, QA), (QA, QS)):
             scan(b("SQM", 16 * lo, 16 * hi), b("RQ", 16 * lo, 16 * hi), b("GQ", 16 * lo, 16 * hi), A.min, A.max)
-        cp(b("MS", 72 * t + 8, 72 * t + 72), b("SQM", 15, 1024, 16))
-        push("m", t, b("MS", 72 * t, 72 * t + 72))
-        for k in range(16):
-            mm(pb(7, 64, 128), b("SEL", 128 * k, 128 * k + 128), half("EQ", k + 1), k == 0, k == 15)
+        rec = b("SQM", 15, 1024, 16)
+        if stay:
+            cp(b("XT2", B, B + 64), rec)
+            act(b("XT2", 4112, 4176), rec)
+            act(b("MS", 72 * t + 8, 72 * t + 72), rec)
+            push("m%d" % t, b("MS", 72 * t, 72 * t + 72))
+            src, XN = "MS", b("XT2", 16, 4176)
+        else:
+            cp(b("MS", 72 * t + 8, 72 * t + 72), rec)
+            push("m%d" % t, b("MS", 72 * t, 72 * t + 72))
+            names()
+            names_out(t)
+            if t < 2:
+                for f_ in bar:
+                    f_()
+                ts(b("BAR"), b("CI", 1, 2), 3.5, None, A.add)
+            if t == 1:
+                weights("2")
+                explicit("2")
+            if t == STAND:
+                act(b("XT", B - 64, B), b("ML", 72 * t - 64, 72 * t))
+            for h in range(2):
+                act(half("PB", h), b("ZW", n + h, n + 128, 2), bias=2302.75)
+            cp(b("XT", B, B + 64), b("ML", 72 * t + 8, 72 * t + 72))
+            act(b("XT", 4112, 4176), b("ML", 72 * t + 8, 72 * t + 72))
+            src, XN = "ML", b("XT", 16, 4176)
         for h in range(2):
-            mm(pb(5, 64 * h, 64 * h + 64), b("IH"), b("NEW", 64 * t, 64 * t + 64), h == 0, False)
-        mm(pb(5), b("NIH"), fall, False, True)
-        act(b("FF"), fall, bias=2048.0)
-        ts(half("FL", 0), pb(4, 0, 64), 0.5, None, A.is_ge)
-        ts(half("FL", 1), pb(7, 64, 128), 0.5, None, A.is_ge)
-        tt(pb(5), b("FL"), pb(5), A.mult)
-        for h in range(2):
-            tt(lane("FO", h), half("FF", h), pb(5, 64 * h, 64 * h + 64), A.add)
-        push("f", t, b("FO", 128 * t, 128 * t + 128))
-        if t < 3:
-            mm(pb(6), b("ONES"), b("BR"))
-            act(b("JNK"), pb(6), accum=b("CNT"))
-            cp(b("CI", 0, 1), b("CNT"))
-            ts(b("CI", 1, 2), b("CI", 0, 1), 1, None, A.bitwise_and)
-            ts(b("BAR"), b("CI", 1, 2), 3.5, None, A.add)
-        arrive("p", t, b("ZW", n, n + 128))
-        arrive("f", t, b("YR", 128 * t, 128 * t + 128))
-        arrive("m", t, b("ML", 72 * t, 72 * t + 72))
-        for h in range(2):
-            act(half("PB", h), b("ZW", n + h, n + 128, 2), bias=2302.75)
-        B = 3856 + 64 * t
-        cp(b("XT", B, B + 64), b("ML", 72 * t + 8, 72 * t + 72))
-        act(b("XT", 4112, 4176), b("ML", 72 * t + 8, 72 * t + 72))
-        for h in range(2):
-            tt(half("AF", h), ind(XN, b("ML", 72 * t + 4 * h, 72 * t + 4 * h + 4)), half("PB", h), A.subtract)
+            tt(half("AF", h), ind(XN, b(src, 72 * t + 4 * h, 72 * t + 4 * h + 4)), half("PB", h), A.subtract)
             ts(half("P", h) if t < 3 else b("YP", h, 128, 2), half("AF", h), -0.5, -1024.0, A.mult, A.add)
-        if t == 2:
-            dma("Y", "o0", T.yr[:, 0:384], T.YR[:, 0:384], [], [b("YR", 0, 384)])
+    dma("Y", "o0", T.yr[:, 0:384], T.YR[:, 0:384], [], [b("YR", 0, 384)])
     dma("Y", "o1", T.yr[:, 384:512], T.YR[:, 384:512], [], [b("YR", 384, 512)])
     dma("S", "o2", T.yp[:], T.YP[:], [], [b("YP")])
     for s in sorted(total):

@@ -1,47 +1,55 @@
 from concourse.mybir import AluOpType as A, ActivationFunctionType as F
 
-SW = [30, 28, 30, 14, 10]
-ORDER = "d0 v1 c2 c3 g2 f4 s1 c0 g3 c1 s2 c6 v0 b1 g4 s3 c7 r1 s4 c4 b0 l1 c5 r0 h1"
+SETS = ((0, 1), (0, 0), (1, 1), (1, 0), (1, 0))
+SW = [32, 32, 24, 18, 10]
+ORDER = "g0 a4 a0 v0 g1 a1 s0 v2 a2 a3 v1 a5 v3 c2 c3 g2 j1 g3 s1 f4 c0 d1 v4 e1 g4 s2 s4 c1 k1 d0 c6 c7 s3 j0 r1 i1 r0 l1 e0 c4 k0 h1 c5 i0"
 VA = 8
-ZA = 4
+ZO = ((0, 16), (1, 10), (2, 10), (1, 16), (2, 16))
 QA = 30
 QS = 38
-XA = 2064
+EQ0 = 11
+ZV = [16, 22]
 _D = {"f": "float32", "b": "bfloat16", "h": "float16", "i": "int32", "u": "uint16"}
-_S = """XT 4176 b;RI 1152 i;YR 512 f;ZW 1280 b;EI 130 i;EBH 128 h;WH 128 b;WL 128 b;KC 1 f
-XT2 4176 b;RI2 1152 i;ZW2 1280 b;EI2 130 i;EBH2 128 h;WH2 128 b;WL2 128 b;KC2 1 f;BAR2 1 f
+_S = """XT 4176 b;RI 1152 i;YR 512 f;ZW 1280 b;EI 130 i;EBH 128 h;WH 128 h;WL 128 h;KC 1 f
+XT1 4176 b;RI1 896 i;ZW1 896 b;EI1 130 i;EBH1 128 h;WH1 128 h;WL1 128 h;KC1 1 f
+XT3 4176 b;RI3 1152 i;ZW3 1152 b;EI3 130 i;EBH3 128 h;WH3 128 h;WL3 128 h;KC3 1 f
 WI2 16 i;COL 16 f;PI 128 b;PN 512 b;P 128 b;PT 128 b
 PRS 2048 b;PB 128 f;IP 4 i;IOT 128 f;R16 128 f;G16 128 f;NEW 256 h;KLI 8 i;KL 8 u;I 128 b;EX 128x16 b;BB 128 b;NB 128 b
-B4 8 b;B8H 8 h;IH 128 h;NIH 128 h;I8 128 b;I128 128 b;BB8 128 b;ONES 128 b;C2K 128 b;MASK 128 f;MBIG 128 b;NXD 128 f;RST 128 f;RQ 1024 b
-SEL 144 b;BC 2048 h;BAR 1 f;BARS 1 f;UI 64 i;UM 64 i;U2 128 f;SQ 64 i;T1 64 i;H1 64 i;H2 64 i;C16 64 u;CF 64 h
+B4 8 b;B8H 8 h;IH 128 h;NIH 128 h;I8 128 b;I128 128 b;BB8 128 b;ONES 128 b;C2K 128 h;IHH 128 h;MASK 128 f;MBIG 128 b;NXD 128 f;RST 128 f;RQ 1024 b
+SEL 144 b;BC 2048 h;BAR 16 f;BARS 16 f;UI 64 i;UM 64 i;U2 128 f;SQ 64 i;T1 64 i;H1 64 i;H2 64 i;C16 64 u;CF 64 h
 ZG 1024 b;AB 128x16 b;SC 128 i;LA 8 i;LM 128 h;L16 8 u;E16 128 u;EH 128 h;EU 128 i;SH 128 i;SM 128 i;SA 128 i;E216 128 u;E2H 128 h
-VB 2048 b;VB2 2048 b;XG 2560 b;NI 128 b;BR 128 b;G9 128 f;TH 128 b;Y1 128 f;FLI 256 b;FS 256 h;JNK 128 f;CNT 1 f;CI 2 i
+VB 2048 b;VB2 2048 b;XG 3072 b;NI 128 b;BR 128 b;G9 128 f;TH 128 b;Y1 128 f;FLI 256 b;FS 256 h;JNK 128 f;CNT 1 f;CI 2 i
 FQ 64 f;EQ 1088 b;Q16 64 u;GQ 1024 b;SQM 1024 b;F0S 128 f;FL 256 b;FF 256 f;FO 512 f;MS 288 u;ML 288 u;AF 128 h;YP 128 f
 relp 512 b;relf 512 f;relm 288 u"""
 SHAPE = {x.split()[0]: [int(v) for v in x.split()[1].split("x")] for x in _S.replace("\n", ";").split(";")}
 SCRATCH = {x.split()[0]: ("sbuf", [128] + SHAPE[x.split()[0]], _D[x.split()[2]]) for x in _S.replace("\n", ";").split(";")}
 for _b in range(8):
-    SCRATCH["pb%d" % _b] = ("psum", [128, 32, 16] if _b < 2 else [128, 512], "float32")
+    SCRATCH["pb%d" % _b] = ("psum", [128, 32, 16] if _b < 3 else [128, 512], "float32")
 N = 8
-STAND = 3
-COPIES = (("EI", 0, 130), ("XT", 16, XA), ("XT", XA, 3856), ("ZW", 0, 768), ("XT", 3856, 4112), ("ZW", 768, 1024), ("RI", 0, 768), ("RI", 768, 1024))
-MESSAGES = ("p0", "m0", "f0", "p1", "m1", "f1", "m2", "b2", "f2", "p3", "m3", "f3")
-SEMAPHORES = (["sv", "sa", "st", "sg", "ls", "lu", "rl", "lp", "lw", "lk", "lz", "lr", "le", "lx0", "lx1", "o0", "o1", "o2"]
-              + ["a" + m for m in MESSAGES] + ["ak%d" % i for i in range(len(COPIES))])
+PLAY = (0, 1, 0, 3, 0)
+COPIES = ((1, "EI", 0, 130, 0, 0), (1, "XT", 16, 1040, 0, 0), (1, "XT", 1040, 2064, 1, 0), (1, "XT", 2064, 3088, 0, 0), (1, "XT", 3088, 4112, 1, 0),
+          (1, "ZW", 0, 768, 0, 0), (1, "RI", 0, 384, 1, 0), (1, "RI", 384, 768, 0, 0),
+          (3, "EI", 0, 130, 0, 0), (3, "XT", 16, 1040, 0, 0), (3, "XT", 1040, 3856, 0, 1), (3, "ZW", 0, 768, 0, 1),
+          (3, "XT", 3856, 4112, 0, 2), (3, "ZW", 768, 1024, 0, 2), (3, "RI", 0, 768, 0, 2), (3, "RI", 768, 1024, 0, 2))
+MESSAGES = ("p0", "m0", "b0", "p1", "f0", "m1", "f1", "b1", "m2", "b2", "p3", "f2", "m3", "f3")
+WRITES = MESSAGES + tuple("k%d" % i for i in range(len(COPIES)))
+SEMAPHORES = (["sv", "sa", "st", "sg", "ls", "lu1", "lu3", "rl", "lp", "lw", "lk", "lz", "lr", "le", "lx0", "lx1", "o0", "o1", "o2"]
+              + ["a" + m for m in WRITES])
 
 
 def shift(m):
-    if m[0] in "kb":
-        return -STAND
-    t = int(m[1])
-    return 1 + t % 3 + (STAND if t == STAND else 0)
+    t = int(m[1:])
+    if m[0] == "k":
+        return -PLAY[COPIES[t][0]]
+    return PLAY[t] - PLAY[t + 1] if m[0] == "b" else PLAY[t] + 1 + t % 3
 
 
 def hops(T, topo, src, dst, m):
-    if m[0] != "k" and topo.may_write(src, dst):
+    if dst in topo.cores_of(src) or (m[0] != "k" and topo.may_write(src, dst)):
         return [dst]
-    c = [x for x in topo.cores_of(src) if topo.die(x) == topo.die(src) and topo.may_write(x, dst) and T.rank_of(x) is None]
-    return [c[0] if m[0] == "k" else c[-1], dst]
+    way = COPIES[int(m[1:])][4] if m[0] == "k" else 2
+    c = [x for x in topo.cores_of(src) if (topo.die(x) != topo.die(src)) == way % 2 and topo.may_write(x, dst) and T.rank_of(x) is None]
+    return [c[-(way // 2)], dst]
 
 
 def send(g, topo, src, dst, out, in_, rsem, lsem):
@@ -51,19 +59,19 @@ def send(g, topo, src, dst, out, in_, rsem, lsem):
 
 
 def places(m):
-    t = int(m[1])
+    t = int(m[1:])
     if m[0] == "k":
-        buf, lo, hi = COPIES[t]
-        return (buf + "2", lo, hi), (buf + "2", lo, hi)
+        t, buf, lo, hi = COPIES[t][:4]
+        return (buf + str(t), lo, hi), (buf + str(t), lo, hi)
     if m[0] == "b":
-        return ("BAR2", 0, 1), ("BAR2", 0, 1)
+        return ("BAR", 4 * t + 4, 4 * t + 5), ("BAR", 4 * t + 4, 4 * t + 5)
     buf, rel, lo, w = {"p": ("ZW", "relp", 768, 128), "f": ("YR", "relf", 0, 128), "m": ("ML", "relm", 0, 72)}[m[0]]
     return (buf, lo + w * t, lo + w * t + w), (rel, w * t, w * t + w)
 
 
 def relay_program(g, core, T, topo):
     sent = 0
-    for m in MESSAGES + tuple("k%d" % i for i in range(len(COPIES))):
+    for m in WRITES:
         for r in range(N):
             src, dst = T.cores[r], T.cores[(r + shift(m)) % N]
             h = hops(T, topo, src, dst, m)
@@ -194,7 +202,10 @@ def rank_program(g, core, T, topo):
         total[sem] = cnt
         evc[(sem, cnt)] = {sem: cnt}
         note(*b(*places(m)[0])[1][0], True, sem, cnt, "D")
-    def copy_out(i): push("k%d" % i, b(*COPIES[i]), "lu" if i == 4 else None)
+    def copy_out(when, last):
+        for i, (t, buf, lo, hi, _, w) in enumerate(COPIES):
+            if w == when and last == (i == len(COPIES) - 1):
+                push("k%d" % i, b(buf, lo, hi), "lu%d" % t if (buf, hi) == ("XT", 4112) else None)
 
     dma("Y", "lp", T.PI[:], T.p0[:], [b("PI")], [])
     dma("S", "lw", T.EI[:, 128:129], T.wt[:], [b("EI", 128, 129)], [])
@@ -204,7 +215,7 @@ def rank_program(g, core, T, topo):
     dma("S", "lx0", T.XT[:, 16:2064], T.ax[:, 0:2048], [b("XT", 16, 2064)], [])
     dma("Y", "lx1", T.XT[:, 2064:4112], T.ax[:, 2048:4096], [b("XT", 2064, 4112)], [])
     dma("Y", "le", T.EI[:, 0:128], T.ex[:], [b("EI", 0, 128)], [])
-    for m in MESSAGES + tuple("k%d" % i for i in range(len(COPIES))):
+    for m in WRITES:
         arrive(m)
     C = lambda j: b("COL", j, j + 1)
     IP = lambda j: b("IP", j, j + 1)
@@ -213,13 +224,16 @@ def rank_program(g, core, T, topo):
     BC = lambda k: b("BC", 128 * k, 128 * k + 128)
     SEL = lambda k: b("SEL", 16 - k, 144 - k)
     def weights(x):
-        ts(b("WI2", 0, 1), b("EI" + x, 128, 129), 6, None, A.arith_shift_right)
-        ts(b("WI2", 1, 2), b("EI" + x, 128, 129), 63, None, A.bitwise_and)
-        for j in range(2):
-            cp(C(4 + j), b("WI2", j, j + 1))
-        ts(b("WH" + x), b("BB"), C(4), 64.0, A.mult, A.mult)
-        ts(b("WL" + x), b("BB"), C(5), None, A.mult)
-        act(b("KC" + x), b("EI" + x, 129, 130))
+        return [lambda: ts(b("WI2", 0, 1), b("EI" + x, 128, 129), 6, None, A.arith_shift_right),
+                lambda: ts(b("WI2", 1, 2), b("EI" + x, 128, 129), 63, None, A.bitwise_and),
+                lambda: cp(b("COL", 4, 6), b("WI2", 0, 2)),
+                lambda: ts(b("WH" + x), b("BB"), C(4), -32.0, A.mult, A.mult),
+                lambda: ts(b("WL" + x), b("BB"), C(5), -0.5, A.mult, A.mult),
+                lambda: act(b("KC" + x), b("EI" + x, 129, 130))]
+    def offsets(x):
+        mm(pb(5, 0, 64), b("WL" + x), half("C2K", 0), True, False)
+        mm(pb(5, 0, 64), b("WH" + x), half("C2K", 0), False, False)
+        mm(pb(5, 64, 128), b("IHH"), half("C2K", 0), False, False)
     def explicit(x):
         for h in range(2):
             act(half("EBH" + x, h), b("EI" + x, h, 128, 2), bias=-2048.0)
@@ -238,7 +252,7 @@ def rank_program(g, core, T, topo):
         cp(C(j), IP(j))
     act(b("ONES"), b("IOT"), F.Sigmoid, bias=40.0)
     ts(b("I"), b("IOT"), C(0), None, A.is_equal)
-    ms(b("BAR"), 3.5)
+    ms(b("BAR", 0, 1), 3.5)
     cp(b3("EX", 0, 128, 0, None), b("I"))
     ts(b("NI"), b("I"), -1.0, None, A.mult)
     cp(b3("EX", 0, 128, 1, 2), b3("EX", 0, 128, 0, 1))
@@ -247,14 +261,19 @@ def rank_program(g, core, T, topo):
     ms(b("XT", 0, 16), 0.0)
     cp(b3("EX", 0, 128, 4, 8), b3("EX", 0, 128, 0, 4))
     ts(b("MASK"), b("R16"), C(1), None, A.is_equal)
-    cp(half("P", 0), b("PI", 0, 128, 2))
-    weights("")
-    act(half("P", 1), b("PI", 1, 128, 2))
+    ms(b("C2K"), 2048.0)
+    ts(b("IHH"), b("I"), -0.5, None, A.mult)
+    ts(half("AF", 0), b("PI", 0, 128, 2), -2.0, -2048.0, A.mult, A.add)
+    for f_ in weights(""):
+        f_()
+    offsets("")
+    for h in range(2):
+        act(half("P", h), b("PI", h, 128, 2))
     push("p0", b("PI"))
     iota(b("NEW"), [[1, 256]], 3840 - 2048, 0)
+    keep(b("ZW1", 768, 896), b("PI"), [[0, 128]], 0)
     waits("G", regions([b("XT", 16, 4112)], []))
-    for i in range(2):
-        copy_out(i)
+    copy_out(0, False)
     act(b("NB"), b("BB"), scale=-2048.0)
     act(b("B4"), b("BB", 0, 128, 16), scale=4096.0)
     act(b("IH"), b("I"))
@@ -264,18 +283,23 @@ def rank_program(g, core, T, topo):
     later = [bcv(k) for k in range(16)] + [
         lambda: ts(b("NIH"), b("I"), -1.0, None, A.mult), lambda: ts(b("I128"), b("I"), 128.0, None, A.mult),
         lambda: ts(b("I8"), b("I"), 8192.0, None, A.mult), lambda: ts(b("BB8"), b("BB"), 8192.0, None, A.mult),
-        lambda: ts(b("MBIG"), b("MASK"), -14336.0, 16384.0, A.mult, A.add), lambda: ms(b("C2K"), 2048.0), lambda: ms(b("FL"), 0.0),
-        lambda: ms(b("XT2", 0, 16), 0.0), lambda: ms(b("SEL"), 0.0), lambda: cp(b("SEL", 16, 144, 16), b("BB", 0, 128, 16))]
+        lambda: ts(b("MBIG"), b("MASK"), -14336.0, 16384.0, A.mult, A.add), lambda: ms(b("FL"), 0.0),
+        lambda: ms(b("XT1", 0, 16), 0.0), lambda: ms(b("XT3", 0, 16), 0.0), lambda: ms(b("SEL"), 0.0), lambda: cp(b("SEL", 16, 144, 16), b("BB", 0, 128, 16))]
     def spare(k):
         for _ in range(min(k, len(later))):
             later.pop(0)()
 
-    SP = ((0, 0, 128 - SW[0], 128), (0, 1, 0, SW[1]), (1, 2, 128 - SW[2], 128), (1, 3, 0, SW[3]), (1, 0, SW[3], SW[3] + SW[4]))
-    v0, v1 = min(SW[1], SW[3] + SW[4]), 128 - min(SW[0], SW[2])
+    SP, edge = [], {(e, h): 128 * h for e in range(2) for h in range(2)}
+    for i, ((e, h), w) in enumerate(zip(SETS, SW)):
+        lo = edge[e, h] - w * h
+        SP.append((e, i % 4, lo, lo + w))
+        edge[e, h] = lo if h else lo + w
+    VP = ((0, 64, 64 + VA), (0, 64 + VA, edge[0, 1]), (0, edge[0, 0], 64), (1, 64, edge[1, 1]), (1, edge[1, 0], 64))
+    v0, v1 = min(edge[0, 0], edge[1, 0]), max(edge[0, 1], edge[1, 1])
     copies = [(k, lo, min(lo + 32, v1)) for k, lo in zip((6, 7, 2), range(v0, v1, 32))]
-    def sbank(i):
-        _, k, lo, hi = SP[i]
-        return b3("pb%d" % k, 0, hi - lo) if k < 2 else pb(k, 0, 16 * (hi - lo))
+    bank = lambda k, w: b3("pb%d" % k, 0, w) if k < 3 else pb(k, 0, 16 * w)
+    sbank = lambda i: bank(SP[i][1], SP[i][3] - SP[i][2])
+    ZP = ((0, ZV[0]), (ZV[0] + ZV[1], 64), (ZV[0], ZV[0] + ZV[1]))
     fh = lambda h: b("FS", 128 * h + 1, 128 * h + 128, 2)
     fall = b("FS", 1, 256, 2)
 
@@ -286,7 +310,7 @@ def rank_program(g, core, T, topo):
             mm(pb(3, 2 * h, 256, 4), b("IH"), b("NEW", 64 * t, 64 * t + 64), h == 0, False)
             mm(pb(3, 2 * h, 256, 4), b("NIH"), fh(h), False, False)
             mm(pb(3, 2 * h + 1, 256, 4), b("IH"), fh(h), False, False)
-        mm(pb(3, 1, 256, 2), b("I"), b("C2K"), False, True)
+        mm(pb(3, 1, 256, 2), b("IH"), b("C2K"), False, True)
     def names_flags():
         act(b("FL", 1, 256, 4), pb(4, 0, 64), F.Sign)
         act(b("FL", 3, 256, 4), pb(7, 64, 128), F.Sign)
@@ -298,33 +322,38 @@ def rank_program(g, core, T, topo):
     def bar_count():
         mm(pb(6), b("ONES"), b("BR"))
         act(b("JNK"), pb(6), accum=b("CNT"))
-    bar = [lambda: cp(b("CI", 0, 1), b("CNT")), lambda: ts(b("CI", 1, 2), b("CI", 0, 1), 1, None, A.bitwise_and)]
+    def bar(t):
+        return [lambda: cp(b("CI", 0, 1), b("CNT")), lambda: ts(b("CI", 1, 2), b("CI", 0, 1), 1, None, A.bitwise_and),
+                lambda: ts(b("BARS", 4 * t, 4 * t + 1), b("CI", 1, 2), 3.5, None, A.add), lambda: push("b%d" % t, b("BARS", 4 * t, 4 * t + 1))]
 
     for t in range(4):
         n = 768 + 128 * t
-        x = "2" if t == STAND else ""
-        stay = t + 1 == STAND
+        x, nx = [str(u) if PLAY[u] else "" for u in (t, t + 1)]
+        stay = nx != ""
         XW, XQ = b("XT" + x, 16, 4112), b("XT" + x, 0, 4112)
         ZW, RW = b("ZW" + x, 0, n), b("RI" + x, 0, n)
-        if t == STAND:
-            later += bar + [lambda: ts(b("BARS"), b("CI", 1, 2), 3.5, None, A.add), lambda: push("b2", b("BARS"))]
-        mm(pb(5, 0, 64), b("WH" + x), half("P", 0), True, False)
-        mm(pb(5, 0, 64), b("WL" + x), half("P", 0), False, True)
-        mm(pb(5, 64, 128), b("I"), half("P", 0))
+        mm(pb(5, 0, 64), b("WH" + x), half("AF", 0), False, False)
+        mm(pb(5, 0, 64), b("WL" + x), half("AF", 0), False, False)
+        mm(pb(5, 64, 128), b("IHH"), half("AF", 0), False, True)
+        if x:
+            later += bar(t - 1)
         if t == 0:
             cp(b3("EX", 0, 128, 8, 16), b3("EX", 0, 128, 0, 8))
         mm(pb(7), b("P"), b("I"))
-        act(b("PT"), pb(7))
-        for a in range(2):
-            mm(b3("pb%d" % a, 0, 32), b("PT"), b3("EX", 64 + 32 * a, 96 + 32 * a), True, False)
         mm(pb(4), b("P"), b("NB"), True, False)
-        for k, lo, hi in copies:
-            mm(pb(k, 0, 16 * (hi - lo)), b("PT"), b3("EX", lo, hi))
         cp(b("UI"), pb(5, 0, 64))
         spare(1)
         ts(b("UM"), b("UI"), 4095, None, A.bitwise_and)
         spare(1)
         tt(b("SQ"), b("UM"), b("UM"), A.mult)
+        act(b("PT"), pb(7))
+        for k, (lo, hi) in enumerate(ZP):
+            mm(b3("pb%d" % k, 0, hi - lo), b("PT"), b3("EX", 64 + lo, 64 + hi), True, False)
+        def spread_p(i):
+            k, lo, hi = copies[i]
+            mm(bank(k, hi - lo), b("PT"), b3("EX", lo, hi))
+        spread_p(0)
+        spread_p(1)
         ts(pb(5, 128, 192), b("UM"), b("KC" + x), None, A.mult)
         ts(b("T1"), b("SQ"), 5, 4095, A.arith_shift_right, A.bitwise_and)
         spare(1)
@@ -336,50 +365,57 @@ def rank_program(g, core, T, topo):
         spare(1)
         if t:
             for h in range(2):
-                keep(b("ZW2", n + h, n + 128, 2) if stay else b("PN", 128 * t + h, 128 * t + 128, 2), half("P", h), [[0, 64]], 0)
+                keep(b("ZW" + nx, n + h, n + 128, 2) if stay else b("PN", 128 * t + h, 128 * t + 128, 2), half("P", h), [[0, 64]], 0)
             if not stay:
                 push("p%d" % t, b("PN", 128 * t, 128 * t + 128))
-        for i in {1: (2, 3), 2: (4, 5, 6)}.get(t, ()):
-            copy_out(i)
+            copy_out(t, False)
         for h in range(2):
             act(half("U2", h), b("UM"))
         def zsum(lo, hi, m):
             mm(b("pb4", m, 128, 16, hi, lo), b("ZG", 16 * lo + m, 16 * hi, 16), b("NB", 0, 128, 16), False, False)
-        for a in range(2):
-            cp(b("ZG", 512 * a, 512 * a + 256), ind(ZW, b("C16", 32 * a, 32 * a + 16)))
-            act(b("ZG", 512 * a + 256, 512 * a + 512), ind(ZW, b("C16", 32 * a + 16, 32 * a + 32)))
-            mm(b3("pb%d" % a, 0, 32), b("NI"), b("ZG", 512 * a, 512 * a + 512), False, True)
-            if a == 0:
-                cp(b("CF"), b("C16"))
-                for h in range(2):
-                    mm(b("pb4", p0=64 * h, p=64 * h + 64), b("CF"), b("IH"), False, False)
-                for m in range(ZA):
-                    zsum(0, 32, m)
+        def zdiff(k):
+            lo, hi = ZP[k]
+            mm(b3("pb%d" % k, 0, hi - lo), b("NI"), b("ZG", 16 * lo, 16 * hi), False, True)
+        def zabs(k, m0, m1):
+            lo, hi = ZP[k]
+            act(b3("AB", 64 + lo, 64 + hi, m0, m1), b3("pb%d" % k, 0, hi - lo, m0, m1), F.Abs, scale=0.5)
+        zget = lambda k: (b("ZG", 16 * ZP[k][0], 16 * ZP[k][1]), ind(ZW, b("C16", *ZP[k])))
+        cp(*zget(0))
+        act(*zget(1))
+        cp(b("CF"), b("C16"))
+        cp(*zget(2))
+        zdiff(0)
+        zdiff(1)
+        for h in range(2):
+            mm(b("pb4", p0=64 * h, p=64 * h + 64), b("CF"), b("IH"), False, False)
+        zdiff(2)
         for m in range(16):
-            zsum(32 if m < ZA else 0, 64, m)
-        for q in range(2):
-            for a in range(2):
-                act(b3("AB", 64 + 32 * a, 96 + 32 * a, 8 * q, 8 * q + 8), b3("pb%d" % a, 0, 32, 8 * q, 8 * q + 8), F.Abs, scale=0.5)
-            for m in range(8 * q, 8 * q + 8):
-                tt(b3("AB", 0, 64, m, None), b("ZG", m, 1024, 16), pb(5, 64, 128), A.max)
-            for m in range(8 * q, 8 * q + 8):
+            zsum(0, 64, m)
+            tt(b3("AB", 0, 64, m, None), b("ZG", m, 1024, 16), pb(5, 64, 128), A.max)
+        done, summed = [0, 0, 0], 0
+        for k, m1 in ZO:
+            zabs(k, done[k], m1)
+            done[k] = m1
+            for m in range(summed, min(done)):
                 mm(pb(4, m, 128, 16), b3("AB", 0, 128, m, None), b("B4"), False, m == 15)
-        if t == STAND:
+            summed = min(done)
+        spread_p(2)
+        if x:
             names()
-            act(b("RI2", n - 128, n), b("FF", 1, 256, 2))
         spare(4)
         for k, lo, hi in copies:
-            act(b("PRS", 16 * lo, 16 * hi), pb(k, 0, 16 * (hi - lo)))
+            act(b("PRS", 16 * lo, 16 * hi), bank(k, hi - lo))
+        if x:
+            act(b("RI" + x, n - 128, n), b("FF", 1, 256, 2))
         def fill(i):
             mm(sbank(i), b("PT"), b3("EX", SP[i][2], SP[i][3]), True, False)
         fill(0)
         fill(1)
-        if t in (1, 2):
-            act(b("RI", n - 128, n), b("YR", 128 * t - 128, 128 * t))
         if t == 0:
             explicit("")
         if t == 2:
-            copy_out(7)
+            act(b("RI", n - 128, n), b("YR", 128 * t - 128, 128 * t))
+            copy_out(t, True)
         scan(b("SC"), b("RST"), pb(4), A.max, A.min)
         spare(1)
         ts(b("LA"), b("SC", 15, 128, 16), 2047, None, A.bitwise_and)
@@ -401,60 +437,53 @@ def rank_program(g, core, T, topo):
             mm(sbank(i), b("NI"), y, False, True)
         def ssign(i):
             e, _, lo, hi = SP[i]
-            act(b(VBS[e], 16 * lo, 16 * hi), sbank(i), F.Sigmoid, bias=32.0, scale=-64.0)
+            act(b(VBS[e], 16 * lo, 16 * hi), sbank(i), F.Sigmoid, bias=128.0, scale=-256.0)
         VOTES = {(0, 1): 6, (0, 0): 4, (1, 1): 7, (1, 0): 6}
         def count(e, h, slots):
             for m in slots:
-                mm(pb(VOTES[e, h], 0, 64), SEL(m), b(VBS[e], 1024 * h + m, 1024 * h + 1024, 16), m == 0, e == 0 and m == 15)
-        def before(h):
-            v = pb(VOTES[0, h], 0, 64)
-            ts(half("BR", h), v, b("BAR" + x), None, A.is_lt)
-            ts(half("G9", h), v, 8.5, 128.0, A.is_ge, A.mult)
-            tt(half("Y1", h), half("BR", h), pb(5, 128 + 64 * h, 192 + 64 * h), A.mult)
-            tt(half("TH", h), half("G9", h), v, A.max)
-            tt(pb(5, 256 + 128 * h, 384 + 128 * h, 2), half("Y1", h), pb(5, 64 * h, 64 * h + 64), A.add)
+                mm(pb(VOTES[e, h], 0, 64), SEL(m), b(VBS[e], 1024 * h + m, 1024 * h + 1024, 16), m == 0 and (e, h) != (1, 0), m == 15 and (e, h) != (1, 1))
+        votes = lambda h: pb(VOTES[0, h], 0, 64)
+        before = {
+            "d": lambda h: ts(half("BR", h), votes(h), b("BAR", 4 * t, 4 * t + 1), None, A.is_lt),
+            "e": lambda h: tt(half("Y1", h), half("BR", h), pb(5, 128 + 64 * h, 192 + 64 * h), A.mult),
+            "i": lambda h: tt(pb(5, 256 + 128 * h, 384 + 128 * h, 2), half("Y1", h), pb(5, 64 * h, 64 * h + 64), A.add),
+            "j": lambda h: ts(half("G9", h), votes(h), 8.5, 128.0, A.is_ge, A.mult),
+            "k": lambda h: tt(half("TH", h), half("G9", h), votes(h), A.max)}
         def barred(h):
-            mm(pb(VOTES[1, h], 0, 64), b("I128"), half("BR", h), False, True)
+            mm(pb(VOTES[1, h], 0, 64), b("I128"), half("BR", h), h == 0, h == 1)
         def flag(h):
             tt(b("FLI", 128 * h + 1, 128 * h + 128, 2), pb(VOTES[1, h], 0, 64), half("TH", h), A.is_ge)
         def choose(h):
             scan(b("FS", 128 * h, 128 * h + 128), b("FLI", 128 * h, 128 * h + 128), pb(5, 256 + 128 * h, 384 + 128 * h), A.mult, A.add)
-        act(b("E16"), ind(RW, b("L16")))
-        tt(b("EU"), ind(RW, b("L16")), b("U2"), A.mult)
-        spare(1)
-        act(pb(5), b("E16"), bias=77.0 * t)
-        sgather(0)
-        ts(b("SH"), b("EU"), 5, None, A.arith_shift_right)
-        ts(b("EH"), b("E16"), -2048.0, None, A.add)
-        tt(b("SM"), b("SH"), pb(5), A.add)
-        spare(len(later))
-        vpiece(0, 64, 64 + VA)
-        ts(b("SA"), b("SM"), 4095, None, A.bitwise_and)
-        vpiece(0, 64 + VA, SP[0][2])
-        cp(b("E216"), b("SA"))
-        ts(b("E2H"), b("SA"), -2048.0, None, A.add)
-        sgather(1)
-        ssign(0)
-        vpiece(0, SP[1][3], 64)
         def deltas():
             mm(pb(5, 128, 256), b("IH"), b("EBH" + x), True, False)
             mm(pb(5, 128, 256), b("NIH"), b("E2H"), False, False)
             mm(pb(5, 0, 128), b("IH"), b("E2H"), False, False)
             mm(pb(5, 0, 128), b("NIH"), b("EH"), False, False)
             mm(pb(5, 257, 512, 2), b("IH"), b("EH"), False, True)
-        step = {"g": sgather, "s": ssign, "f": fill, "b": before, "r": barred, "l": flag, "h": choose, "d": lambda _: deltas(),
-                "c": lambda i: count(i // 4, i // 2 % 2, range(8 * (i % 2), 8 * (i % 2) + 8)),
-                "v": lambda h: vpiece(1, 64, SP[2][2]) if h else vpiece(1, SP[4][3], 64)}
+        act(b("E16"), ind(RW, b("L16")))
+        tt(b("EU"), ind(RW, b("L16")), b("U2"), A.mult)
+        spare(1)
+        act(pb(5), b("E16"), bias=77.0 * t)
+        ts(b("SH"), b("EU"), 5, None, A.arith_shift_right)
+        spare(len(later))
+        adapt = (lambda: tt(b("SM"), b("SH"), pb(5), A.add), lambda: ts(b("SA"), b("SM"), 4095, None, A.bitwise_and),
+                 lambda: cp(b("E216"), b("SA")), lambda: ts(b("E2H"), b("E216"), -2048.0, None, A.add),
+                 lambda: ts(b("EH"), b("E16"), -2048.0, None, A.add), deltas)
+        step = {"g": sgather, "s": ssign, "f": fill, **before, "r": barred, "l": flag, "h": choose, "a": lambda i: adapt[i](),
+                "c": lambda i: count(i // 4, i // 2 % 2, range(8 * (i % 2), 8 * (i % 2) + 8)), "v": lambda i: vpiece(*VP[i])}
         for y in ORDER.split():
             step[y[0]](int(y[1]))
-        if t == STAND:
+        if x:
             names_out(t - 1)
         if t == 0:
+            later += weights("1")
+            explicit("1")
             act(b("JNK"), b("MASK"), scale=4096.0)
             for h in range(2):
                 tt(half("NXD", h), half("MASK", h), b("IOT", 0, 64), A.mult)
             ms(b("RQ"), 255.0)
-        spread = lambda k: b3("pb%d" % (k // 4), 4 * (k % 4), 4 * (k % 4) + 4) if k < 8 else pb(k // 4, 64 * (k % 4), 64 * (k % 4) + 64)
+        spread = lambda k: b3("pb%d" % (k // 4), 4 * (k % 4), 4 * (k % 4) + 4) if k < 12 else pb(k // 4, 64 * (k % 4), 64 * (k % 4) + 64)
         for k in range(16):
             mm(spread(k), BC(k), fh(1))
         flag(0)
@@ -463,18 +492,19 @@ def rank_program(g, core, T, topo):
         choose(0)
         if t == 0:
             tt(b("NXD"), b("NXD"), b("JNK"), A.add)
+        act(b("FQ"), fh(0), bias=2064.0)
         mm(pb(7, 0, 64), BC(0), fh(0))
         mm(pb(6), BC(0), fall, True, False)
         mm(pb(6), b("I"), b("MBIG"), False, False)
-        act(b("FQ"), fh(0), bias=2064.0)
         for k in range(16):
             tt(half("EQ", k + 1), fh(0), spread(k), A.is_equal)
             mm(pb(4, 0, 64), b("I8"), half("EQ", k + 1), k == 0, k == 15)
-            if k == 5:
+            if k == EQ0:
                 tt(half("EQ", 0), fh(1), pb(7, 0, 64), A.is_equal)
                 mm(pb(6), b("BB8"), b("EQ", 0, 128), False, True)
         for h in range(2):
             scan(half("F0S", h), half("NXD", h), pb(6, 64 * h, 64 * h + 64), A.max, A.min)
+        spare(1)
         tt(b("Q16"), b("FQ"), pb(4, 0, 64), A.min)
         cp(b("MS", 72 * t, 72 * t + 8), b("F0S", 15, 128, 16))
         for lo, hi in ((0, QA), (QA, QS)):
@@ -489,36 +519,42 @@ def rank_program(g, core, T, topo):
             for h in range(2):
                 act(half("PB", h), half("P", h), bias=2302.75)
         for lo, hi in ((QS, 64), (0, QA), (QA, QS)):
+            spare(1)
             scan(b("SQM", 16 * lo, 16 * hi), b("RQ", 16 * lo, 16 * hi), b("GQ", 16 * lo, 16 * hi), A.min, A.max)
         rec = b("SQM", 15, 1024, 16)
         if stay:
-            cp(b("XT2", B, B + 64), rec)
-            act(b("XT2", 4112, 4176), rec)
+            spare(1)
+            cp(b("XT" + nx, B, B + 64), rec)
+            act(b("XT" + nx, 4112, 4176), rec)
             act(b("MS", 72 * t + 8, 72 * t + 72), rec)
             push("m%d" % t, b("MS", 72 * t, 72 * t + 72))
-            src, XN = "MS", b("XT2", 16, 4176)
+            spare(len(later))
+            src, XN = "MS", b("XT" + nx, 16, 4176)
         else:
             cp(b("MS", 72 * t + 8, 72 * t + 72), rec)
             push("m%d" % t, b("MS", 72 * t, 72 * t + 72))
             names()
             names_out(t)
-            if t < 2:
-                for f_ in bar:
-                    f_()
-                ts(b("BAR"), b("CI", 1, 2), 3.5, None, A.add)
             if t == 1:
-                weights("2")
-                explicit("2")
-            if t == STAND:
-                act(b("XT", B - 64, B), b("ML", 72 * t - 64, 72 * t))
+                for f_ in bar(t) + weights("3"):
+                    f_()
+                explicit("3")
+                act(b("RI", n - 128, n), b("YR", 128 * t - 128, 128 * t))
+            act(b("XT", B - 64, B), b("ML", 72 * t - 64, 72 * t))
             for h in range(2):
                 act(half("PB", h), b("ZW", n + h, n + 128, 2), bias=2302.75)
             cp(b("XT", B, B + 64), b("ML", 72 * t + 8, 72 * t + 72))
             act(b("XT", 4112, 4176), b("ML", 72 * t + 8, 72 * t + 72))
             src, XN = "ML", b("XT", 16, 4176)
-        for h in range(2):
-            tt(half("AF", h), ind(XN, b(src, 72 * t + 4 * h, 72 * t + 4 * h + 4)), half("PB", h), A.subtract)
-            ts(half("P", h) if t < 3 else b("YP", h, 128, 2), half("AF", h), -0.5, -1024.0, A.mult, A.add)
+        if t < 3:
+            offsets(nx)
+            for h in range(2):
+                tt(half("AF", h), ind(XN, b(src, 72 * t + 4 * h, 72 * t + 4 * h + 4)), half("PB", h), A.subtract)
+            ts(b("P"), b("AF"), -0.5, -1024.0, A.mult, A.add)
+        else:
+            tt(b("AF"), ind(XN, b(src, 72 * t, 72 * t + 8)), b("PB"), A.subtract)
+            for h in range(2):
+                ts(b("YP", h, 128, 2), half("AF", h), -0.5, -1024.0, A.mult, A.add)
     dma("Y", "o0", T.yr[:, 0:384], T.YR[:, 0:384], [], [b("YR", 0, 384)])
     dma("Y", "o1", T.yr[:, 384:512], T.YR[:, 384:512], [], [b("YR", 384, 512)])
     dma("S", "o2", T.yp[:], T.YP[:], [], [b("YP")])

@@ -1,92 +1,626 @@
+import numpy as np
 from concourse.mybir import AluOpType as A, ActivationFunctionType as F
 
+N, WORLD = 8, 256
+PLAY = (0, 1, -4, -1, 0)
 SETS = ((0, 1), (0, 0), (1, 1), (1, 0), (1, 0))
 SW = [32, 32, 24, 18, 10]
-ORDER = "g0 a4 a0 v0 g1 a1 s0 v2 a2 a3 v1 a5 v3 c2 c3 g2 j1 g3 s1 f4 c0 d1 v4 e1 g4 s2 s4 c1 k1 d0 c6 c7 s3 j0 r1 i1 r0 l1 e0 c4 k0 h1 c5 i0"
+SB = (0, 1, 2, 3, 0)
+HG = (0, 1)
+FT = 0
+BG = 0
+BS = 0
+FAC = 1.2
+ONS = (0, 0)
+VB4 = 16
+ORDER = "o1 o0 q0 z1 o2 z0 U0 t0 b0 t1 z2 b1 t2 u0 m0 m1 b2 m2 u1 b4 w0 w1 b3 m3 w2 w3 f2 p1 f1 p0 n0 n1 n2 p2 n3 U1 f3 n4 E1 H1 S1 v1 E0 H0 A1 f0 S0 v0 g0 g1 s0 B1 f4 A0 c2 v2 B0 g2 s1 v3 c3 j1 c0 g4 a0 v5 c1 d1 a1 g3 d0 s2 k1 v4 j0 s4 c6 s3 c7 e1 i1 r0 k0 y1 c4 l1 e0 h1 c5 i0 l0 P0 P1 h0 P2 P3 F1 x0 x1 x2 x3 F0 F2 Q0 G1 F3 M1 G0 M0 G2 M2 F4"
 VA = 8
-ZO = ((0, 16), (1, 10), (2, 10), (1, 16), (2, 16))
-QA = 30
-QS = 38
-EQ0 = 11
+ZO = ((0, 0, 16), (1, 0, 8), (2, 0, 8), (1, 8, 16), (2, 8, 16))
+QP = (("S", 0, 30), ("V", 38, 64), ("S", 30, 38))
 ZV = [16, 22]
+LAT, GAT, HOP, DMA = 0.18, 1.5, 2.0, 1.7
+SLACK = 6.0
+GATE = "FQ"
 _D = {"f": "float32", "b": "bfloat16", "h": "float16", "i": "int32", "u": "uint16"}
-_S = """XT 4176 b;RI 1152 i;YR 512 f;ZW 1280 b;EI 130 i;EBH 128 h;WH 128 h;WL 128 h;KC 1 f
-XT1 4176 b;RI1 896 i;ZW1 896 b;EI1 130 i;EBH1 128 h;WH1 128 h;WL1 128 h;KC1 1 f
-XT3 4176 b;RI3 1152 i;ZW3 1152 b;EI3 130 i;EBH3 128 h;WH3 128 h;WL3 128 h;KC3 1 f
-WI2 16 i;COL 16 f;PI 128 b;PN 512 b;P 128 b;PT 128 b
-PRS 2048 b;PB 128 f;IP 4 i;IOT 128 f;R16 128 f;G16 128 f;NEW 256 h;KLI 8 i;KL 8 u;I 128 b;EX 128x16 b;BB 128 b;NB 128 b
-B4 8 b;B8H 8 h;IH 128 h;NIH 128 h;I8 128 b;I128 128 b;BB8 128 b;ONES 128 b;C2K 128 h;IHH 128 h;MASK 128 f;MBIG 128 b;NXD 128 f;RST 128 f;RQ 1024 b
-SEL 144 b;BC 2048 h;BAR 16 f;BARS 16 f;UI 64 i;UM 64 i;U2 128 f;SQ 64 i;T1 64 i;H1 64 i;H2 64 i;C16 64 u;CF 64 h
-ZG 1024 b;AB 128x16 b;SC 128 i;LA 8 i;LM 128 h;L16 8 u;E16 128 u;EH 128 h;EU 128 i;SH 128 i;SM 128 i;SA 128 i;E216 128 u;E2H 128 h
-VB 2048 b;VB2 2048 b;XG 3072 b;NI 128 b;BR 128 b;G9 128 f;TH 128 b;Y1 128 f;FLI 256 b;FS 256 h;JNK 128 f;CNT 1 f;CI 2 i
-FQ 64 f;EQ 1088 b;Q16 64 u;GQ 1024 b;SQM 1024 b;F0S 128 f;FL 256 b;FF 256 f;FO 512 f;MS 288 u;ML 288 u;AF 128 h;YP 128 f
-relp 512 b;relf 512 f;relm 288 u"""
+_S = """XT 4176 b;ZW 1280 b;RI 1280 i;WE 648 h;KC 4 f;YR 512 f;EI 128 i;WK 4 i;QL 576 b
+WI2 16 i;COL 16 f;PI 128 b;PN 512 b;P 128 b;PT 128 b;FN 512 i
+PRS 2048 b;PB 128 f;IP 4 i;IOT 128 f;R16 128 f;G16 128 f;NEW 256 h;KL 8 u;I 128 b;EX 128x16 b;BB 128 b;N8 8 b
+B4 8 b;B8H 8 h;IH 128 h;NIH 128 h;I8 128 b;I128 128 b;FLI 256 b;IQ 128 b;NG 128 b;NQ 128 b;SEQ 144 b;C2Z 128 h;BB8 128 b;ONES 128 b;C2K 128 h;IHH 128 h;MASK 128 f;MBIG 128 b;NXD 128 f;RST 128 f;RQ 512 b
+SEL 144 b;BC 2048 h;BAR 16 f;BARS 16 f;CR 448 b;VG 128 f;UC 256 f;SQ 128 i;H2 64 i;C16 64 u;CFZ 192 h
+ZG 1024 b;AB 128x16 b;SC 128 i;LA 8 i;LM 128 h;L16 8 u;E16 128 u;EH 256 h;ES 256 i;SA 128 i;E216 128 u;E2H 128 h
+VB 2048 b;VB2 2048 b;XG 3072 b;NI 128 b;BR 128 b;G9 128 b;TH 128 b;Y1 128 f;D1 256 f;FS 256 h;JNK 128 f;CNT 1 f;CI 2 i
+FQ 64 f;EQ 1088 b;Q16 64 u;GQ 1024 b;SQM 1024 b;F0S 128 f;FL 256 b;FF 256 f;MS 288 u;ML 576 u;AF 128 h;YP 128 f"""
+TAB = [str(t) if PLAY[t] else "" for t in range(5)]
+for _t in range(1, 4):
+    if PLAY[_t]:
+        _S += ";XT%d 4176 b;ZW%d %d b;RI%d %d i;WE%d 648 h;KC%d 4 f" % (_t, _t, 768 + 128 * _t, _t, 768 + 128 * _t, _t, _t)
 SHAPE = {x.split()[0]: [int(v) for v in x.split()[1].split("x")] for x in _S.replace("\n", ";").split(";")}
 SCRATCH = {x.split()[0]: ("sbuf", [128] + SHAPE[x.split()[0]], _D[x.split()[2]]) for x in _S.replace("\n", ";").split(";")}
 for _b in range(8):
-    SCRATCH["pb%d" % _b] = ("psum", [128, 32, 16] if _b < 3 else [128, 512], "float32")
-N = 8
-PLAY = (0, 1, 0, 3, 0)
-COPIES = ((1, "EI", 0, 130, 0, 0), (1, "XT", 16, 1040, 0, 0), (1, "XT", 1040, 2064, 1, 0), (1, "XT", 2064, 3088, 0, 0), (1, "XT", 3088, 4112, 1, 0),
-          (1, "ZW", 0, 768, 0, 0), (1, "RI", 0, 384, 1, 0), (1, "RI", 384, 768, 0, 0),
-          (3, "EI", 0, 130, 0, 0), (3, "XT", 16, 1040, 0, 0), (3, "XT", 1040, 3856, 0, 1), (3, "ZW", 0, 768, 0, 1),
-          (3, "XT", 3856, 4112, 0, 2), (3, "ZW", 768, 1024, 0, 2), (3, "RI", 0, 768, 0, 2), (3, "RI", 768, 1024, 0, 2))
-MESSAGES = ("p0", "m0", "b0", "p1", "f0", "m1", "f1", "b1", "m2", "b2", "p3", "f2", "m3", "f3")
-WRITES = MESSAGES + tuple("k%d" % i for i in range(len(COPIES)))
-SEMAPHORES = (["sv", "sa", "st", "sg", "ls", "lu1", "lu3", "rl", "lp", "lw", "lk", "lz", "lr", "le", "lx0", "lx1", "o0", "o1", "o2"]
+    SHAPE["pb%d" % _b] = [32, 16] if _b < 3 else [512]
+    SCRATCH["pb%d" % _b] = ("psum", [128] + SHAPE["pb%d" % _b], "float32")
+OWNER = [(PLAY[t] + 1 + t % 3) % N for t in range(4)]
+LANES = [(OWNER[t] - PLAY[t + 1]) % N for t in range(4)]
+COPIES = ((1, "WE", 0, 520, 0, 0), (1, "ZW", 0, 768, 1, 0), (1, "XT", 16, 1040, 1, 0), (1, "XT", 1040, 2064, 0, 0),
+          (1, "XT", 2064, 3088, 1, 0), (1, "XT", 3088, 4112, 0, 0), (1, "RI", 0, 448, 3, 0), (1, "RI", 448, 768, 2, 0), (1, "WE", 520, 648, 1, 0),
+          (2, "XT", 16, 1040, 2, 1), (2, "WE", 0, 648, 0, 1), (2, "XT", 1040, 2064, 2, 1), (2, "XT", 2064, 3088, 0, 1), (2, "XT", 3088, 4112, 0, 1),
+          (2, "RI", 0, 768, 2, 1), (2, "ZW", 0, 768, 0, 1),
+          (3, "XT", 16, 1040, 2, 3), (3, "XT", 1040, 2064, 3, 3), (3, "WE", 0, 648, 0, 3), (3, "XT", 2064, 3088, 1, 3), (3, "XT", 3088, 4112, 0, 3),
+          (3, "ZW", 0, 768, 1, 3), (3, "RI", 0, 384, 2, 3), (3, "RI", 384, 768, 3, 3))
+MESSAGES = ([k + str(t) for t in range(4) if LANES[t] for k in "pmf"] + [k + str(t) for t in range(3) for k in "bqyz"[:4 - t // 2]])
+WRITES = MESSAGES + ["k%d" % i for i in range(len(COPIES))]
+SEMAPHORES = (["sv", "sa", "st", "sg", "ls", "lu1", "lu2", "lu3", "rl", "lp", "lw", "lz", "lr", "le", "lx0", "lx1", "o0", "o1", "o2"]
               + ["a" + m for m in WRITES])
 
 
 def shift(m):
-    t = int(m[1:])
     if m[0] == "k":
-        return -PLAY[COPIES[t][0]]
-    return PLAY[t] - PLAY[t + 1] if m[0] == "b" else PLAY[t] + 1 + t % 3
+        return -PLAY[COPIES[int(m[1:])][0]]
+    t = int(m[1])
+    return PLAY[t] - PLAY[t + 1] if m[0] == "b" else PLAY[t + 1] - PLAY[t + 2] if m[0] in "zqy" else LANES[t]
 
 
 def hops(T, topo, src, dst, m):
     if dst in topo.cores_of(src) or (m[0] != "k" and topo.may_write(src, dst)):
-        return [dst]
-    way = COPIES[int(m[1:])][4] if m[0] == "k" else 2
-    c = [x for x in topo.cores_of(src) if (topo.die(x) != topo.die(src)) == way % 2 and topo.may_write(x, dst) and T.rank_of(x) is None]
-    return [c[-(way // 2)], dst]
+        return [src, dst]
+    way = COPIES[int(m[1:])][4] if m[0] == "k" else 0
+    idle = lambda cores, to: [x for x in cores if (topo.die(x) != topo.die(src)) == way % 2 and topo.may_write(x, to) and T.rank_of(x) is None]
+    if way < 2:
+        return [src, idle(topo.cores_of(src), dst)[0 if m[0] == "k" else -1], dst]
+    far = idle([x for x in range(WORLD) if topo.mates(x, dst)], dst)[0]
+    return [src, idle(topo.cores_of(src), far)[0], far, dst]
 
 
-def send(g, topo, src, dst, out, in_, rsem, lsem):
+def engines(topo, src, dst, m):
+    e = topo.engines(src, dst)
+    if dst not in topo.cores_of(src) or m[0] == "m" or (m[0] == "k" and COPIES[int(m[1:])][0] == 1):
+        return e
+    return e[len(e) // 2:] if m[0] == "k" else e[:len(e) // 2]
+
+
+def send(g, topo, src, dst, m, out, in_, rsem, lsem):
     rid, pid = topo.addr(dst, src)
-    g.remote_dma(out, in_, rsem, lsem, pid, rid, topo.mask(src, dst))
-    return len(topo.engines(src, dst))
+    e = engines(topo, src, dst, m)
+    g.remote_dma(out, in_, rsem, lsem, pid, rid, sum(1 << x for x in e))
+    return len(e)
 
 
-def places(m):
-    t = int(m[1:])
+def view(name, *ix, p=(0, 128)):
+    sh = SHAPE[name]
+    ix = tuple(slice(*x.indices(n)) if isinstance(x, slice) else x for x, n in zip(ix + (slice(None),) * len(sh), sh))
+    cols = np.arange(int(np.prod(sh))).reshape(sh)[ix].reshape(-1)
+    m = np.zeros(int(np.prod(sh)), np.uint8)
+    m[cols] = 1
+    return (name, (slice(*p),) + ix, int.from_bytes(np.packbits(m, bitorder="little").tobytes(), "little"), len(cols), None)
+
+
+def b(name, lo=0, hi=None, st=1, p=128, p0=0):
+    return view(name, slice(lo, hi, st), p=(p0, p))
+
+
+def b3(name, lo, hi, c0=0, c1=16):
+    return view(name, slice(lo, hi), c0 if c1 is None else slice(c0, c1))
+
+
+def place(m):
     if m[0] == "k":
-        t, buf, lo, hi = COPIES[t][:4]
-        return (buf + str(t), lo, hi), (buf + str(t), lo, hi)
-    if m[0] == "b":
-        return ("BAR", 4 * t + 4, 4 * t + 5), ("BAR", 4 * t + 4, 4 * t + 5)
-    buf, rel, lo, w = {"p": ("ZW", "relp", 768, 128), "f": ("YR", "relf", 0, 128), "m": ("ML", "relm", 0, 72)}[m[0]]
-    return (buf, lo + w * t, lo + w * t + w), (rel, w * t, w * t + w)
+        k = COPIES[int(m[1:])]
+        return b(k[1] + str(k[0]), *k[2:4])
+    t = int(m[1])
+    x = TAB[t + (2 if m[0] in "zqy" else 1)]
+    buf, lo, w = {"p": ("ZW" + x, 768 + 128 * t, 128), "m": ("ML", 72 * t, 72), "f": ("RI" + x, 768 + 128 * t, 128), "b": ("BAR", 4 * t + 4, 1),
+                  "z": ("ZW" + x, 768, 128 * t + 128), "y": ("RI" + x, 768, 128 * t + 128), "q": ("QL", 192 * t, 64 * t + 64)}[m[0]]
+    return b(buf, lo, lo + w)
+
+
+def program():
+    ops = []
+    cyc = 0.83e-3
+    two = lambda *xs: all(SCRATCH[x[0]][2] in ("bfloat16", "float16", "uint16") for x in xs)
+
+    chain = [""]
+    def op(q, make, writes, reads, us, extra=None): ops.append((q, make, writes, reads, us, extra, q if q == "Y" or q in chain[0] else extra and extra[1][0] == "k" and "k"))
+    def vcost(a, rate): return 0.05 + a[3] * cyc * max(GAT, rate) if a[4] else max(64, a[3] * rate) * cyc
+    def ind(w, o): return (w[0], w[1], w[2], 16 * o[3], o)
+    def ts(out, a, s1, s2, o0, o1=None):
+        col = [x for x in (s1, s2) if isinstance(x, tuple)]
+        o = (o0,) if o1 is None else (o0, o1)
+        op("V", lambda e, ap: e.tensor_scalar(ap(out), ap(a), ap(s1), ap(s2), *o), [out], [a] + col, vcost(a, 0.5 if two(out, a) else 1))
+    def tt(out, a, c, o):
+        op("V", lambda e, ap: e.tensor_tensor(ap(out), ap(a), ap(c), o), [out], [a, c], vcost(a, 1 if "pb" in (a[0][:2], c[0][:2]) else 2))
+    def cp(out, a): op("V", lambda e, ap: e.tensor_copy(ap(out), ap(a)), [out], [a], vcost(a, 0.5 if two(out, a) else 1))
+    def ms(out, c): op("V", lambda e, ap: e.memset(ap(out), c), [out], [], vcost(out, 0.5 if two(out) else 1))
+    def scan(out, a, c, o0, o1):
+        op("V", lambda e, ap: e.tensor_tensor_scan(ap(out), ap(a), ap(c), 0.0, o0, o1), [out], [a, c], vcost(a, 0.5 if two(out, a, c) else 1))
+    def act(out, a, f=F.Copy, bias=0.0, scale=1.0, accum=None):
+        cols = [x for x in (bias, scale) if isinstance(x, tuple)]
+        def make(e, ap):
+            if accum is None:
+                return e.activation(ap(out), ap(a), f, bias=ap(bias), scale=ap(scale))
+            return e.activation(ap(out), ap(a), f, bias=ap(bias), scale=ap(scale), accum_out=ap(accum))
+        op("S", make, [out] + ([accum] if accum else []), [a] + cols, (0.065 + a[3] * cyc * GAT if a[4] else max(64, a[3]) * cyc) + (0.14 if accum else 0))
+    def mm(out, l, r, start=True, stop=True):
+        op("T", lambda e, ap: e.matmul(ap(out), ap(l), ap(r), start, stop), [out], [l, r],
+           max(min(64, l[3]), r[3]) * cyc / 2 * (1 if two(l) else 4))
+    def iota(out, pat, base, cm=0):
+        if SCRATCH[out[0]][2] == "int32":
+            op("G", lambda e, ap: e.iota(ap(out), pat, base, cm), [out], [], 0.13 + 2 * cyc * out[3])
+        else:
+            op("G", lambda e, ap: e.iota(ap(out), pat, base, cm, allow_small_or_imprecise_dtypes=True), [out], [], 0.13 + 2 * cyc * out[3])
+    def keep(out, a, pat=None, base=0, cm=0):
+        op("G", lambda e, ap: e.affine_select(ap(out), ap(a), pat or [[0, a[3]]], A.is_equal, 0.0, base, cm), [out], [a], 0.17 + 2 * cyc * a[3])
+    size = lambda x: 128 * x[3] * (2 if two(x) else 4)
+    def dma(q, sem, moves, load):
+        sb = [x[0] for x in moves]
+        op(q, moves, sb if load else [], [] if load else sb, 0.07 * len(moves), ("dma", sem, sum(size(x) for x in sb), load))
+    def push(m, x, after=()):
+        op("G", None, [], [x] + list(after), 0.2, ("push", m, x))
+        op("R", None, [place(m)], [], 0.0, ("arrive", m, size(x)))
+    def copies(when, after):
+        for i, (_, buf, lo, hi, _, w) in enumerate(COPIES):
+            if w == when:
+                push("k%d" % i, b(buf, lo, hi), [after])
+
+    sl = slice
+    dma("Y", "lp", [(b("PI"), "p0", sl(None))], True)
+    dma("S", "lw", [(b("WK", 0, 1), "wt", sl(None)), (b("WK", 1, 2), "km", sl(None))], True)
+    dma("Y", "lz", [(b("ZW", 0, 768), "zp", sl(None))], True)
+    dma("Y", "lr", [(b("RI", 0, 768), "rt", sl(None))], True)
+    dma("S", "lx0", [(b("XT", 16, 2064), "ax", sl(0, 2048))], True)
+    dma("Y", "lx1", [(b("XT", 2064, 4112), "ax", sl(2048, 4096))], True)
+    dma("Y", "le", [(b("EI"), "ex", sl(None))], True)
+    C = lambda j: b("COL", j, j + 1)
+    IP = lambda j: b("IP", j, j + 1)
+    half = lambda buf, h: b(buf, 64 * h, 64 * h + 64)
+    pb = lambda k, lo=0, hi=128, st=1: b("pb%d" % k, lo, hi, st)
+    BC = lambda k: b("BC", 128 * k, 128 * k + 128)
+    SEL = lambda k, name="SEL": b(name, 16 - k, 144 - k)
+    chain[0] = "G"
+    iota(IP(0), [[0, 1]], 0, 1)
+    iota(b("IOT"), [[1, 128]], 0)
+    iota(b("G16"), [[1, 8], [0, 16]], 0)
+    iota(b("R16"), [[0, 8], [1, 16]], 0)
+    iota(b("C2Z"), [[0, 64], [2048, 2]], 0)
+    iota(b("C2K"), [[0, 128]], 2048)
+    chain[0] = ""
+    iota(b("NEW"), [[1, 256]], 3840 - 2048)
+    ms(b("RST"), -1.0e9)
+    ms(b("RST", 0, 128, 16), 1.0e9)
+    ts(IP(1), IP(0), 15, None, A.bitwise_and)
+    ts(IP(2), IP(0), 4, None, A.arith_shift_right)
+    cp(b("COL", 0, 3), b("IP", 0, 3))
+    act(b("ONES"), b("IOT"), F.Sigmoid, bias=40.0)
+    ts(b("I"), b("IOT"), C(0), None, A.is_equal)
+    ms(b("BAR", 0, 1), 896.0)
+    cp(b3("EX", 0, 128, 0, None), b("I"))
+    for w in (1, 2, 4):
+        cp(b3("EX", 0, 128, w, 2 * w), b3("EX", 0, 128, 0, w))
+    for lo in range(0, 128, 32):
+        cp(b3("EX", lo, lo + 32, 8, 16), b3("EX", lo, lo + 32, 0, 8))
+    ts(b("BB"), b("G16"), C(2), None, A.is_equal)
+    ts(b("MASK"), b("R16"), C(1), None, A.is_equal)
+    for name, k in (("NI", -1.0), ("IHH", -0.5)):
+        ts(b(name), b("I"), k, None, A.mult)
+    for name, k in (("NIH", -1.0), ("I8", 8192.0)) + ((("IQ", 0.25), ("NG", -0.25), ("NQ", -2.0 ** -9)) if FT else (("I128", 128.0),)):
+        act(b(name), b("I"), scale=k)
+    for h in range(2):
+        ts(half("AF", h), b("PI", h, 128, 2), -2.0, -2048.0, A.mult, A.add)
+    ts(b("WI2", 0, 1), b("WK", 0, 1), 6, None, A.arith_shift_right)
+    ts(b("WI2", 1, 2), b("WK", 0, 1), 63, None, A.bitwise_and)
+    cp(b("COL", 4, 6), b("WI2", 0, 2))
+    for j, k in enumerate((-32.0, -0.5, 32.0, 0.5)):
+        ts(b("WE", 128 * j + 8, 128 * j + 136), b("BB"), C(4 + j % 2), k, A.mult, A.mult)
+    ts(b("WI2", 2, 3), b("WK", 1, 2), 2176.0, None, A.add)
+    ts(b("WI2", 3, 4), b("WK", 1, 2), 1, None, A.bitwise_and)
+    ts(b("WI2", 4, 5), b("WI2", 2, 3), 4095, None, A.bitwise_and)
+    ts(b("KC", 0, 1), b("WI2", 4, 5), 32.0, -67584.0, A.mult, A.add)
+    tt(C(6), b("WI2", 3, 4), b("WI2", 4, 5), A.subtract)
+    ts(b("KC", 1, 2), C(6), 65536.0, 2.0 ** 27, A.mult, A.add)
+    ms(b("WE", 0, 8), 0.0)
+    PACK = ((32.0, 64.0), (65536.0, 0.0))
+    for j, (k, c) in enumerate(PACK):
+        act(b("WE", j, j + 1), b("KC", j, j + 1), scale=1.0 / k, bias=c)
+    ms(b("CR", 0, 192 + 256 * FT), 0.0)
+    for j, terms in enumerate(((2.0 ** 23, -34816.0, -0.5), (1.5 * 2.0 ** 35,), (-1.5 * 2.0 ** 35, -2.0 ** 23, 36864.0), (1.5 * 2.0 ** 23,), (-1.5 * 2.0 ** 23,))[:3 + 2 * FT]):
+        for i, k in enumerate(terms):
+            ms(b("CR", 64 * j, 64 * j + 64, p0=32 * i, p=32 * i + 1), k)
+    for i, k in enumerate((0.5, 2.0 ** -10)[:2 * FT]):
+        ms(b("CR", 321, 448, 2, p0=32 * i, p=32 * i + 1), k)
+    if not FT:
+        iota(b("FLI"), [[0, 256]], 0)
+    for h in range(2):
+        act(half("P", h), b("PI", h, 128, 2))
+        act(b("WE", 520 + 64 * h, 584 + 64 * h), b("EI", h, 128, 2), bias=-2048.0)
+    act(b("N8"), b("BB", 0, 128, 16), scale=-2048.0)
+    act(b("B4"), b("BB", 0, 128, 16), scale=4096.0)
+    act(b("IH"), b("I"))
+    act(b("B8H"), b("BB", 0, 128, 16))
+    act(b("KL"), b("IOT", 0, 8))
+    for zero in (b("CFZ"), b("SEL"), b("EH", 0, 256, 2)):
+        iota(zero, [[0, zero[3]]], 0)
+    for zero in [b("FL", 0, 256, 2)] + [b("XT" + x, 0, 16) for x in sorted(set(TAB))]:
+        ms(zero, 0.0)
+    for k in range(16):
+        if k < BG:
+            keep(BC(k), b("BB"), [[-16, 8], [0, 16]], -k, 1)
+        elif k < BG + BS:
+            act(BC(k), b("BB"), scale=b("MASK", k, k + 1))
+        else:
+            ts(BC(k), b("BB"), b("MASK", k, k + 1), None, A.mult)
+    act(b("BB8"), b("BB"), scale=8192.0)
+    act(b("MBIG"), b("MASK"), scale=-14336.0, bias=16384.0)
+    cp(b("SEL", 16, 144, 16), b("BB", 0, 128, 16))
+    if FT:
+        act(b("SEQ"), b("SEL"), scale=2.0 ** -9)
+    iota(b("JNK"), [[0, 2], [1, 64]], 4096)
+    tt(b("NXD"), b("MASK"), b("JNK"), A.mult)
+    for lo in (0, 256):
+        iota(b("RQ", lo, lo + 256), [[0, 16], [255, 16]], 0)
+
+    SP, edge = [], {(e, h): 128 * h for e in range(2) for h in range(2)}
+    for i, ((e, h), w) in enumerate(zip(SETS, SW)):
+        lo = edge[e, h] - w * h
+        SP.append((e, SB[i], lo, lo + w))
+        edge[e, h] = lo if h else lo + w
+    VP = ((0, 64, 64 + VA), (0, 64 + VA, edge[0, 1]), (0, edge[0, 0], 64), (1, 64, edge[1, 1]), (1, edge[1, 0], 64 - VB4), (1, 64 - VB4, 64))
+    v0, v1 = min(edge[0, 0], edge[1, 0]), max(edge[0, 1], edge[1, 1])
+    bank = lambda k, w: b3("pb%d" % k, 0, w) if k < 3 else pb(k, 0, 16 * w)
+    sbank = lambda i: bank(SP[i][1], SP[i][3] - SP[i][2])
+    spreads = [(k, lo, min(lo + 32, v1)) for k, lo in zip((6, 7, 3), range(v0, v1, 32))]
+    ZP = ((0, ZV[0]), (ZV[0] + ZV[1], 64), (ZV[0], ZV[0] + ZV[1]))
+    fh = lambda h: b("FS", 128 * h + 1, 128 * h + 128, 2)
+
+    for t in range(4):
+        n = 768 + 128 * t
+        x, nx = TAB[t], TAB[t + 1]
+        stay = not LANES[t]
+        XW, XQ = b("XT" + x, 16, 4112), b("XT" + x, 0, 4112)
+        ZW, RW = b("ZW" + x, 0, n), b("RI" + x, 0, n)
+        WH, WL, NH, NL, EB = [b("WE" + x, lo, lo + 128) for lo in range(8, 648, 128)]
+        chain[0] = "VST"
+        u, AE, K2 = pb(4, 257, 384, 2), half("AF", 0), half("C2K", 0)
+        mm(pb(4, 256, 384), NL, b("C2Z"), True, False)
+        mm(u, NH, K2, False, False)
+        mm(pb(5, 64, 128), b("IHH"), K2, True, False)
+        for l, r in ((NH, AE), (NL, AE), *[(b("ONES"), half("CR", j)) for j in range(3)], (WH, K2), (WH, AE), (WL, K2)):
+            mm(u, l, r, False, False)
+        mm(u, WL, AE, False, True)
+        mm(pb(7), b("AF"), b("IHH"))
+        mm(pb(5, 64, 128), b("IHH"), AE, False, True)
+        ts(b("VG", 0, 128, 2), u, -2048.0, None, A.add)
+        ts(b("VG", 1, 128, 2), u, b("KC" + x, 0, 1), b("KC" + x, 1, 2), A.mult, A.add)
+        scan(b("SQ"), pb(4, 256, 384), b("VG"), A.mult, A.add)
+        act(b("PT"), pb(7), bias=-1024.0)
+        for k, (lo, hi) in enumerate(ZP):
+            mm(b3("pb%d" % k, 0, hi - lo), b("PT"), b3("EX", 64 + lo, 64 + hi), True, False)
+        ts(b("H2"), b("SQ", 1, 128, 2), 5, 4095, A.arith_shift_right, A.bitwise_and)
+        ts(b("C16"), b("H2"), n / 4096.0, -31.0 / 64.0, A.mult, A.add)
+        if t < 3 or not stay:
+            buf, lo = ("ZW" + nx, n) if stay else ("PN", 128 * t)
+            for h in range(2):
+                keep(b(buf, lo + h, lo + 128, 2), half("P", h))
+            if not stay:
+                push("p%d" % t, b(buf, lo, lo + 128))
+        copies(2 * t, b("C16") if t else b("PI"))
+        def factors(h):
+            v = b("VG", 0, 128, 2)
+            act(b("UC", 128 * h, 128 * h + 128, 2), v, bias=2080.0)
+            act(b("UC", 128 * h + 1, 128 * h + 128, 2), v, scale=2048.0, bias=65536.0 - 2.0 ** 22 + 32.0 * 77 * t)
+        zget = lambda k: (b("ZG", 16 * ZP[k][0], 16 * ZP[k][1]), ind(ZW, b("C16", *ZP[k])))
+        def numbers(_):
+            cp(b("CFZ", 64, 128), b("C16"))
+            for h in range(2):
+                mm(pb(4), b("CFZ", 64 - 64 * h, 192 - 64 * h), b("IH"), h == 0, False)
+        def zdiff(k):
+            lo, hi = ZP[k]
+            mm(b3("pb%d" % k, 0, hi - lo), b("NI"), b("ZG", 16 * lo, 16 * hi), False, True)
+        def zsum(i):
+            for m in range(8 * i, 8 * i + 8):
+                mm(b("pb4", m, 128, 16, 64), b("ZG", m, 1024, 16), b("N8"), False, False)
+        def zmax(i):
+            for m in range(4 * i, 4 * i + 4):
+                tt(b3("AB", 0, 64, m, None), b("ZG", m, 1024, 16), pb(5, 64, 128), A.max)
+        def zabs(i):
+            k, m0, m1 = ZO[i]
+            lo, hi = ZP[k]
+            act(b3("AB", 64 + lo, 64 + hi, m0, m1), b3("pb%d" % k, 0, hi - lo, m0, m1), F.Abs, scale=0.5)
+        def sums(i):
+            for m in range(4 * i, 4 * i + 4):
+                mm(pb(4, m, 128, 16), b3("AB", 0, 128, m, None), b("B4"), False, m == 15)
+        def spread_p(i):
+            k, lo, hi = spreads[i]
+            mm(bank(k, hi - lo), b("PT"), b3("EX", lo, hi))
+        def beside(i):
+            k, lo, hi = spreads[i]
+            act(b("PRS", 16 * lo, 16 * hi), bank(k, hi - lo))
+        winners = (lambda: scan(b("SC"), b("RST"), pb(4), A.max, A.min),
+                   lambda: ts(b("LA"), b("SC", 15, 128, 16), 2047, None, A.bitwise_and),
+                   lambda: tt(b("LM"), ind(b("LA"), b("KL")), b("MASK"), A.mult),
+                   lambda: mm(pb(4, 128, 136), b("LM"), b("B8H")), lambda: cp(b("L16"), pb(4, 128, 136)))
+        L16 = lambda h: b("L16", 4 * h, 4 * h + 4)
+        twice = lambda buf, h: b(buf, 128 * h, 128 * h + 128)
+        lanes, EH = b, b("EH", 1, 256, 2)
+        elect = {
+            "z": lambda k: (act if k == 1 else cp)(*zget(k)), "q": numbers, "u": zsum, "t": zdiff, "b": zabs, "w": sums, "m": zmax,
+            "n": lambda i: winners[i](), "o": spread_p, "p": beside, "U": factors,
+            "E": lambda h: act(half("E16", h), ind(RW, L16(h))),
+            "H": lambda h: ts(b("EH", 128 * h + 1, 128 * h + 128, 2), ind(RW, L16(h)) if HG[h] else half("E16", h), -2048.0, None, A.add),
+            "S": lambda h: scan(twice("ES", h), twice("EH", h), twice("UC", h), A.mult, A.add),
+            "A": lambda h: ts(half("SA", h), b("ES", 128 * h + 1, 128 * h + 128, 2), 5, 4095, A.arith_shift_right, A.bitwise_and),
+            "B": lambda h: cp(half("E216", h), half("SA", h))}
+        def fill(i):
+            mm(sbank(i), b("PT"), b3("EX", SP[i][2], SP[i][3]), True, False)
+        LST, VBS = ("E16", "E216"), ("VB", "VB2")
+        def vpiece(e, lo, hi):
+            tt(b(VBS[e], 16 * lo, 16 * hi), ind(XW, lanes(LST[e], lo, hi)), b("PRS", 16 * lo, 16 * hi), A.is_ge)
+        def sgather(i):
+            e, _, lo, hi = SP[i]
+            y = b("XG", 512 * i, 512 * i + 16 * (hi - lo))
+            act(y, ind(XW, lanes(LST[e], lo, hi)))
+            mm(sbank(i), b("NI"), y, False, True)
+        def ssign(i):
+            e, _, lo, hi = SP[i]
+            act(b(VBS[e], 16 * lo, 16 * hi), sbank(i), F.Sigmoid, bias=128.0, scale=-256.0)
+        VOTES = {(0, 1): 6, (0, 0): 4, (1, 1): 7, (1, 0): 6}
+        def count(e, h, slots):
+            for m in slots:
+                if e:
+                    mm(flags(h), SEL(m, "SEQ"), b("VB2", 1024 * h + m, 1024 * h + 1024, 16), False, False)
+                else:
+                    mm(votes(h), SEL(m), b("VB", 1024 * h + m, 1024 * h + 1024, 16), m == 0, m == 15)
+        flags = lambda h: pb(VOTES[1, h], 1, 128, 2)
+        votes = lambda h: pb(VOTES[0, h], 0, 64)
+        before = {
+            "d": lambda h: (act(half("BR", h), votes(h), F.Sigmoid, bias=bar, scale=-256.0) if ONS[h] & 1
+                            else ts(half("BR", h), votes(h), 256.0, bar, A.mult, A.is_lt)),
+            "e": lambda h: tt(half("Y1", h), half("BR", h), pb(5, 128 + 64 * h, 192 + 64 * h), A.mult),
+            "D": lambda h: act(b("D1", 128 * h + 1, 128 * h + 128, 2), half("E16", h), bias=-2048.0),
+            "i": lambda h: tt(b("D1", 128 * h, 128 * h + 128, 2), half("Y1", h), pb(5, 64 * h, 64 * h + 64), A.add),
+            "j": lambda h: (act(half("G9", h), votes(h), F.Sigmoid, bias=-2176.0, scale=256.0) if ONS[h] & 2
+                            else ts(half("G9", h), votes(h), 8.5, None, A.is_ge)),
+            "k": lambda h: (act if ONS[h] & 4 else cp)(half("TH", h), votes(h))}
+        bar = b("BAR", 4 * t, 4 * t + 1)
+        def opening(h):
+            mm(pb(VOTES[1, h], 0, 128), b("ONES"), b("CR", 320, 448), True, False)
+        def barred(h):
+            mm(flags(h), b("IQ"), half("BR", h), False, False)
+            mm(flags(h), b("NQ"), half("TH", h), False, False)
+            mm(flags(h), b("NG"), half("G9", h), False, False)
+        def flag(h):
+            for j in (3, 4):
+                mm(flags(h), b("ONES"), half("CR", j), False, j == 4)
+        def choose(h):
+            scan(twice("FS", h), pb(VOTES[1, h], 0, 128), twice("D1", h), A.mult, A.add)
+        def deltas():
+            mm(pb(5, 128, 256), b("IH"), EB, True, False)
+            mm(pb(5, 128, 256), b("NIH"), b("E2H"), False, False)
+            mm(pb(5, 0, 128), b("IH"), b("E2H"), False, False)
+            mm(pb(5, 0, 128), b("NIH"), EH, False, FT == 1)
+            if not FT:
+                mm(pb(5, 257, 512, 2), b("IH"), EH, False, True)
+        if not FT:
+            def count(e, h, slots):
+                for m in slots:
+                    mm(pb(VOTES[e, h], 0, 64), SEL(m), b(VBS[e], 1024 * h + m, 1024 * h + 1024, 16), m == 0 and (e, h) != (1, 0), m == 15 and (e, h) != (1, 1))
+            opening = lambda h: h or mm(pb(VOTES[1, h], 0, 64), b("I128"), half("BR", h), True, False)
+            barred = lambda h: h and mm(pb(VOTES[1, h], 0, 64), b("I128"), half("BR", h), False, True)
+            flag = lambda h: tt(b("FLI", 128 * h + 1, 128 * h + 128, 2), pb(VOTES[1, h], 0, 64), half("TH", h), A.is_ge)
+            choose = lambda h: scan(twice("FS", h), twice("FLI", h), pb(5, 256 + 128 * h, 384 + 128 * h), A.mult, A.add)
+            before.update({"D": lambda h: None,
+                           "i": lambda h: tt(pb(5, 256 + 128 * h, 384 + 128 * h, 2), half("Y1", h), pb(5, 64 * h, 64 * h + 64), A.add),
+                           "j": lambda h: ts(half("G9", h), votes(h), 8.5, 128.0, A.is_ge, A.mult),
+                           "k": lambda h: tt(half("TH", h), half("G9", h), votes(h), A.max)})
+        over = lambda k: b3("pb1", 4 * k, 4 * k + 4) if k < 8 else pb(7, 64 * k - 512, 64 * k - 448)
+        def names_over(i):
+            for k in range(4 * i, 4 * i + 4):
+                mm(over(k), BC(k), fh(1))
+        eq, common = lambda k: half("EQ", k), pb(4, 0, 64)
+        def compare(i):
+            for k in range(4 * i, 4 * i + 4):
+                tt(eq(k), fh(0), over(k), A.is_equal)
+                mm(common, b("I8"), eq(k), k == 0, k == 15)
+        def first_prepare():
+            mm(pb(3, 256, 320), BC(0), fh(0))
+            mm(pb(6), BC(0), b("FS", 1, 256, 2), True, False)
+            mm(pb(6), b("I"), b("MBIG"), False, False)
+        def first_common():
+            tt(b("EQ", 1024, 1088), fh(1), pb(3, 256, 320), A.is_equal)
+            mm(pb(6, 0, 64), b("BB8"), b("EQ", 1024, 1088), False, False)
+        def first_pick():
+            mm(pb(6, 64, 128), b("BB8"), eq(0), False, True)
+            for h in range(2):
+                scan(half("F0S", h), half("NXD", h), pb(6, 64 * h, 64 * h + 64), A.max, A.min)
+        first = (lambda: act(b("FQ"), fh(0), bias=2064.0), first_prepare, first_common, first_pick,
+                 lambda: cp(b("MS", 72 * t, 72 * t + 8), b("F0S", 15, 128, 16)))
+        piece = lambda buf, i: b(buf, 16 * QP[i][1], 16 * QP[i][2])
+        shared = {"x": compare, "F": lambda i: first[i](),
+                  "Q": lambda _: tt(b("Q16"), b("FQ"), common, A.min),
+                  "G": lambda i: (act if QP[i][0] == "S" else cp)(piece("GQ", i), ind(XQ, b("Q16", *QP[i][1:]))),
+                  "M": lambda i: scan(piece("SQM", i), b("RQ", 0, 16 * (QP[i][2] - QP[i][1])), piece("GQ", i), A.min, A.max)}
+        adapt = (lambda: ts(b("E2H"), b("E216"), -2048.0, None, A.add), deltas)
+        step = {"g": sgather, "s": ssign, "f": fill, **before, **elect, **shared, "P": names_over, "r": opening, "y": barred, "l": flag, "h": choose, "a": lambda i: adapt[i](),
+                "c": lambda i: count(i // 4, i // 2 % 2, range(8 * (i % 2), 8 * (i % 2) + 8)), "v": lambda i: vpiece(*VP[i])}
+        for y in ORDER.split():
+            step[y[0]](int(y[1]))
+        chain[0] = "T"
+        for k in range(16):
+            mm(pb(2, 0, 4), SEL(k), eq(k), k == 0, k == 15)
+        for h in range(2):
+            mm(pb(3, 2 * h, 256, 4), b("IH"), b("NEW", 64 * t, 64 * t + 64), h == 0, False)
+            mm(pb(3, 2 * h, 256, 4), b("NIH"), fh(h), False, False)
+            mm(pb(3, 2 * h + 1, 256, 4), b("IH"), fh(h), False, False)
+        mm(pb(3, 1, 256, 2), b("IH"), b("C2K"), False, True)
+        if t < 3:
+            mm(pb(6), b("ONES"), b("BR"))
+            act(b("JNK"), pb(6), accum=b("CNT"))
+        act(b("FL", 1, 256, 4), common, F.Sign)
+        act(b("FL", 3, 256, 4), pb(2, 0, 4), F.Sign)
+        B = 3856 + 64 * t
+        chain[0] = "VST"
+        if t:
+            act(b("XT" + nx, 3856, B), place("q%d" % (t - 1)))
+        for j, (k, c) in enumerate(PACK if nx else ()):
+            act(b("KC" + nx, j, j + 1), b("WE" + nx, j, j + 1), scale=k, bias=-k * c)
+        rec, msg = b("SQM", 15, 1024, 16), b("MS", 72 * t, 72 * t + 72)
+        if not stay:
+            cp(b("MS", 72 * t + 8, 72 * t + 72), rec)
+            push("m%d" % t, msg)
+            rec = b("ML", 72 * t + 8, 72 * t + 72)
+        cp(b("XT" + nx, B, B + 64), rec)
+        act(b("XT" + nx, 4112, 4176), rec)
+        chain[0] = ""
+        for h in range(2):
+            act(half("PB", h), half("P", h) if stay else b("ZW" + nx, n + h, n + 128, 2), bias=2302.75)
+        for lo in (0, 128):
+            scan(b("FF", lo, lo + 128), b("FL", lo, lo + 128), pb(3, lo, lo + 128), A.mult, A.add)
+        names = b("RI" + nx, n, n + 128) if stay else b("FN", 128 * t, 128 * t + 128)
+        if t < 3 or not stay:
+            act(names, b("FF", 1, 256, 2))
+        if not stay:
+            push("f%d" % t, names)
+        if t < 3:
+            cp(b("CI", 0, 1), b("CNT"))
+            ts(b("CI", 1, 2), b("CI", 0, 1), 1, None, A.bitwise_and)
+            ts(b("BARS", 4 * t, 4 * t + 1), b("CI", 1, 2), 256.0, 896.0, A.mult, A.add)
+            push("b%d" % t, b("BARS", 4 * t, 4 * t + 1))
+            copies(2 * t + 1, b("BARS", 4 * t, 4 * t + 1) if t else b(GATE))
+            if t < 2:
+                push("z%d" % t, b("ZW" + nx, 768, n + 128), [b("BARS", 4 * t, 4 * t + 1)] if t else [])
+            push("q%d" % t, b("XT" + nx, 3856, B + 64))
+            push("y%d" % t, b("RI" + nx, 768, n + 128))
+        if t == 2:
+            for lo in range(0, 384, 128):
+                act(b("YR", lo, lo + 128), b("RI", 768 + lo, 896 + lo))
+            dma("Y", "o0", [(b("YR", 0, 384), "yr", sl(0, 384))], False)
+        if t == 3:
+            act(b("YR", 384, 512), b("FF", 1, 256, 2) if stay else b("RI", 1152, 1280))
+            dma("Y", "o1", [(b("YR", 384, 512), "yr", sl(384, 512))], False)
+        XN, src = b("XT" + nx, 16, 4176), "MS" if stay else "ML"
+        chain[0] = "VST"
+        if t < 3:
+            for h in range(2):
+                tt(half("AF", h), ind(XN, b(src, 72 * t + 4 * h, 72 * t + 4 * h + 4)), half("PB", h), A.subtract)
+            ts(b("P"), b("AF"), -0.5, -1024.0, A.mult, A.add)
+        else:
+            tt(b("AF"), ind(XN, b(src, 72 * t, 72 * t + 8)), b("PB"), A.subtract)
+            for h in range(2):
+                ts(b("YP", h, 128, 2), half("AF", h), -0.5, -1024.0, A.mult, A.add)
+            dma("S", "o2", [(b("YP"), "yp", sl(None))], False)
+    return ops
+
+
+def regions(o):
+    return [(y[0], y[2], isw) for isw, xs in ((False, o[3]), (True, o[2])) for x in xs for y in ([x, x[4]] if x[4] else [x])]
+
+
+def late(o):
+    k = o[5]
+    if k and k[0] == "dma":
+        return DMA + k[2] / 3.0e5
+    if k and k[0] == "arrive":
+        return 2 * HOP + k[2] / 1.2e5 + (SLACK if k[1][0] in "zqy" else 0.0)
+    return HOP if k else LAT
+
+
+def depends(ops):
+    deps, acc, last = [{} for _ in ops], {}, {}
+    for i, o in enumerate(ops):
+        if o[0] == "R":
+            deps[i][i - 1] = 0.0
+        elif o[6]:
+            if o[6] in last:
+                deps[i][last[o[6]]] = 0.0
+            last[o[6]] = i
+        for buf, m, isw in regions(o):
+            for m2, w2, j in acc.get(buf, []):
+                same = ops[j][0] == o[0] and not ops[j][5]
+                hit = m & m2 and (isw or w2)
+                if j != i and (hit or (buf[:2] == "pb" and (not same or o[0] == "T"))):
+                    d = late(ops[j]) if not same or (hit and w2 and not (o[0] == "T" and isw)) else 0.0
+                    deps[i][j] = max(deps[i].get(j, 0.0), d)
+        for buf, m, isw in regions(o):
+            old = acc.get(buf, [])
+            if buf[:2] == "pb":
+                old = [y for y in old if ops[y[2]][0] == o[0] and o[0] != "T"] if not old or ops[old[-1][2]][0] != o[0] or o[0] == "T" else old
+                if old and ops[old[-1][2]][0] == o[0]:
+                    for j, d in deps[old[-1][2]].items():
+                        if ops[j][0] != o[0] and any(r[0] == buf for r in regions(ops[j])):
+                            deps[i][j] = max(deps[i].get(j, 0.0), d)
+            acc[buf] = [y for y in old if not (isw and y[0] & ~m == 0 and buf[:2] != "pb")] + [(m, isw, i)]
+    return deps
+
+
+def schedule(ops):
+    ops = [o[:4] + (o[4] * FAC,) + o[5:] for o in ops]
+    n, deps = len(ops), depends(ops)
+    succ = [[] for _ in ops]
+    for i in range(n):
+        for j, d in deps[i].items():
+            succ[j].append((i, d))
+    rank = [0.0] * n
+    for i in range(n - 1, -1, -1):
+        rank[i] = ops[i][4] + max([d + rank[j] for j, d in succ[i]], default=late(ops[i]))
+        rank[i] += 8.0 if ops[i][5] and ops[i][5][:2] == ("push", "k0") else 0.0
+    for i in range(n):
+        rank[i] += 100.0 if ops[i][5] and ops[i][5][0] == "push" else 0.0
+    left, ready, at, free, order, busy = [len(d) for d in deps], set(), [0.0] * n, {}, [], {}
+    ready.update(i for i in range(n) if not left[i])
+    while ready:
+        est = {i: max(at[i], free.get(ops[i][0], 0.0)) for i in ready}
+        t0 = min(est.values())
+        q = ops[min(i for i in ready if est[i] == t0)][0]
+        mine = [i for i in ready if ops[i][0] == q]
+        i = max((j for j in mine if est[j] <= t0), key=lambda j: (rank[j], -j))
+        for j in mine:
+            if t0 < est[j] < t0 + ops[i][4] and est[j] + max(rank[j], ops[j][4] + rank[i]) < t0 + max(rank[i], ops[i][4] + rank[j]):
+                if est[i] <= t0 or rank[j] > rank[i]:
+                    i = j
+        ready.remove(i)
+        order.append(i)
+        DBG.append((est[i], i, rank[i]))
+        end = est[i] + ops[i][4]
+        if q != "R":
+            free[q] = end
+        k = ops[i][5]
+        if k and k[0] == "dma":
+            busy[q] = max(busy.get("Y", 0.0), busy.get("S", 0.0), end + DMA) + k[2] / 3.0e5
+            end = busy[q] - late(ops[i])
+        if k and k[0] == "arrive" and k[1][0] == "k":
+            way = COPIES[int(k[1][1:])][4]
+            busy[way] = max(busy.get(way, 0.0), end + 2 * HOP) + k[2] / 1.2e5
+            end = busy[way] - late(ops[i])
+        for j, d in succ[i]:
+            at[j] = max(at[j], end + d)
+            left[j] -= 1
+            if not left[j]:
+                ready.add(j)
+    return [ops[i] for i in order]
+
+
+_PLAN, _WAYS = [], {}
+DBG = []
+
+
+def plan(T, topo):
+    if not _PLAN:
+        _PLAN.extend(schedule(program()))
+        for m in WRITES:
+            for r in range(N):
+                _WAYS[m, r] = hops(T, topo, T.cores[r], T.cores[(r + shift(m)) % N], m)
+    return _PLAN
 
 
 def relay_program(g, core, T, topo):
     sent = 0
-    for m in WRITES:
+    for m in [o[5][1] for o in plan(T, topo) if o[5] and o[5][0] == "push"]:
         for r in range(N):
-            src, dst = T.cores[r], T.cores[(r + shift(m)) % N]
-            h = hops(T, topo, src, dst, m)
-            if len(h) < 2 or h[0] != core:
-                continue
-            g.wait_ge(T.sem["a" + m], len(topo.engines(src, core)))
-            a, b = [T[x[0]][:, x[1]:x[2]] for x in places(m)]
-            sent += send(g, topo, core, dst, a, b, T.sem["a" + m], T.sem.rl)
+            h = _WAYS[m, r]
+            if core in h:
+                i, x = h.index(core), place(m)
+                g.wait_ge(T.sem["a" + m], len(engines(topo, h[i - 1], core, m)))
+                sent += send(g, topo, core, h[i + 1], m, T[x[0]][x[1]], T[x[0]][x[1]], T.sem["a" + m], T.sem.rl)
     if sent:
         g.wait_ge(T.sem.rl, sent)
-
-
-def bits(lo, hi, st, unit=1):
-    n = len(range(lo, hi, st))
-    return unit * (((1 << (st * n)) - 1) // ((1 << st) - 1)) << lo
 
 
 def rank_program(g, core, T, topo):
@@ -98,21 +632,29 @@ def rank_program(g, core, T, topo):
     own = {"V": "sv", "S": "sa", "T": "st", "G": "sg"}
     total, acc, clk, evc = {}, {}, {q: {} for q in eng}, {}
 
-    def merge(a, b):
-        for s, c in b.items():
-            if a.get(s, 0) < c:
-                a[s] = c
+    def ap(x):
+        if not isinstance(x, tuple):
+            return x
+        return T[x[0]][x[1]].indirect(ap(x[4])) if x[4] else T[x[0]][x[1]]
 
-    def note(buf, m, isw, sem, cnt, q):
-        keep = [x for x in acc.get(buf, []) if not (isw and x[0] & ~m == 0) and x[:3] != (m, isw, sem)]
-        acc[buf] = keep + [(m, isw, sem, cnt, q)]
+    def merge(a, c):
+        for s, k in c.items():
+            if a.get(s, 0) < k:
+                a[s] = k
+
+    def done(regs, sem, inc, q, clock):
+        total[sem] = total.get(sem, 0) + inc
+        evc[(sem, total[sem])] = dict(clock, **{sem: total[sem]})
+        for buf, m, isw in regs:
+            keep = [x for x in acc.get(buf, []) if not (isw and x[0] & ~m == 0) and x[:3] != (m, isw, sem)]
+            acc[buf] = keep + [(m, isw, sem, total[sem], q)]
 
     def waits(q, regs):
         need = {}
         for buf, m, isw in regs:
             ps = buf[:2] == "pb"
             for m2, w2, sem, cnt, q2 in acc.get(buf, []):
-                if q2 == q and own.get(q) == sem:
+                if q2 == q:
                     if not m & m2 or not w2 or (q == "T" and isw):
                         continue
                 elif not (ps or (m & m2 and (isw or w2))):
@@ -128,437 +670,32 @@ def rank_program(g, core, T, topo):
         for s, c in need.items():
             merge(clk[q], evc[(s, c)])
 
-    def regions(reads, writes):
-        return [r + (isw,) for isw, xs in ((False, reads), (True, writes)) for x in xs for r in x[1]]
-
-    def op(q, make, writes, reads, sem=None, inc=1):
-        regs = regions(reads, writes)
+    sent = 0
+    for o in plan(T, topo):
+        q, regs, kind = o[0], regions(o), o[5]
+        if q == "R":
+            src = _WAYS[kind[1], (rank - shift(kind[1])) % N][-2]
+            done(regs, "a" + kind[1], len(engines(topo, src, core, kind[1])), "D", {})
+            continue
         waits(q, regs)
-        sem = sem or own[q]
-        make(eng[q]).then_inc(T.sem[sem], inc)
-        total[sem] = total.get(sem, 0) + inc
-        c = dict(clk[q])
-        c[sem] = total[sem]
-        evc[(sem, total[sem])] = c
-        for r in regs:
-            note(*r, sem, total[sem], q if inc == 1 else "D")
-
-    def b(name, lo=0, hi=None, st=1, p=128, p0=0):
-        hi = SHAPE.get(name, [128])[0] if hi is None else hi
-        return (T[name][p0:p, lo:hi:st], [(name, bits(lo, hi, st))])
-
-    def b3(name, lo, hi, c0=0, c1=16):
-        ap = T[name][:, lo:hi, c0] if c1 is None else T[name][:, lo:hi, c0:c1]
-        return (ap, [(name, bits(16 * lo + c0, 16 * hi, 16, 1 if c1 is None else (1 << (c1 - c0)) - 1))])
-
-    def ind(w, o): return (w[0].indirect(o[0]), w[1] + o[1])
-    def ts(out, a, s1, s2, o0, o1=None):
-        ins = [a]
-        if isinstance(s1, tuple):
-            ins.append(s1)
-            s1 = s1[0]
-        if o1 is None:
-            op("V", lambda e: e.tensor_scalar(out[0], a[0], s1, s2, o0), [out], ins)
+        if kind is None:
+            o[1](eng[q], ap).then_inc(T.sem[own[q]], 1)
+            done(regs, own[q], 1, q, clk[q])
+        elif kind[0] == "dma":
+            for x, name, ix in o[1]:
+                a, c = ap(x), T[name][:, ix] if ix.stop else T[name][:]
+                (eng[q].dma_start(a, c) if kind[3] else eng[q].dma_start(c, a)).then_inc(T.sem[kind[1]], 16)
+            done(regs, kind[1], 16 * len(o[1]), "D", clk[q])
         else:
-            op("V", lambda e: e.tensor_scalar(out[0], a[0], s1, s2, o0, o1), [out], ins)
-    def tt(out, a, c, o): op("V", lambda e: e.tensor_tensor(out[0], a[0], c[0], o), [out], [a, c])
-    def cp(out, a): op("V", lambda e: e.tensor_copy(out[0], a[0]), [out], [a])
-    def ms(out, c): op("V", lambda e: e.memset(out[0], c), [out], [])
-    def scan(out, a, c, o0, o1): op("V", lambda e: e.tensor_tensor_scan(out[0], a[0], c[0], 0.0, o0, o1), [out], [a, c])
-    def act(out, a, f=F.Copy, bias=0.0, scale=1.0, accum=None):
-        ins, outs = [a], [out]
-        kw = {"bias": bias, "scale": scale}
-        for k in kw:
-            if isinstance(kw[k], tuple):
-                ins.append(kw[k])
-                kw[k] = kw[k][0]
-        if accum is not None:
-            outs.append(accum)
-            kw["accum_out"] = accum[0]
-        op("S", lambda e: e.activation(out[0], a[0], f, **kw), outs, ins)
-    def mm(out, l, r, start=True, stop=True): op("T", lambda e: e.matmul(out[0], l[0], r[0], start, stop), [out], [l, r])
-    def dma(q, sem, out, in_, w, r): op(q, lambda e: e.dma_start(out, in_), w, r, sem, 16)
-    def iota(out, pat, base, cm, small=True):
-        if small:
-            op("G", lambda e: e.iota(out[0], pat, base, cm, allow_small_or_imprecise_dtypes=True), [out], [])
-        else:
-            op("G", lambda e: e.iota(out[0], pat, base, cm), [out], [])
-    def keep(out, a, pat, base): op("G", lambda e: e.affine_select(out[0], a[0], pat, A.is_equal, 0.0, base, 0), [out], [a])
-
-    sent = [0]
-    def push(m, x, watch=None):
-        waits("G", regions([x], []))
-        h = hops(T, topo, core, T.cores[(rank + shift(m)) % N], m)
-        n_ = send(g, topo, core, h[0], b(*places(m)[len(h) - 1])[0], x[0], T.sem["a" + m], T.sem[watch or "ls"])
-        if watch:
-            total[watch] = n_
-            evc[(watch, n_)] = {watch: n_}
-            note(*x[1][0], False, watch, n_, "D")
-        else:
-            sent[0] += n_
-    def arrive(m):
-        src = T.cores[(rank - shift(m)) % N]
-        sem, cnt = "a" + m, len(topo.engines(([src] + hops(T, topo, src, core, m))[-2], core))
-        total[sem] = cnt
-        evc[(sem, cnt)] = {sem: cnt}
-        note(*b(*places(m)[0])[1][0], True, sem, cnt, "D")
-    def copy_out(when, last):
-        for i, (t, buf, lo, hi, _, w) in enumerate(COPIES):
-            if w == when and last == (i == len(COPIES) - 1):
-                push("k%d" % i, b(buf, lo, hi), "lu%d" % t if (buf, hi) == ("XT", 4112) else None)
-
-    dma("Y", "lp", T.PI[:], T.p0[:], [b("PI")], [])
-    dma("S", "lw", T.EI[:, 128:129], T.wt[:], [b("EI", 128, 129)], [])
-    dma("S", "lk", T.EI[:, 129:130], T.km[:], [b("EI", 129, 130)], [])
-    dma("Y", "lz", T.ZW[:, 0:768], T.zp[:], [b("ZW", 0, 768)], [])
-    dma("Y", "lr", T.RI[:, 0:768], T.rt[:], [b("RI", 0, 768)], [])
-    dma("S", "lx0", T.XT[:, 16:2064], T.ax[:, 0:2048], [b("XT", 16, 2064)], [])
-    dma("Y", "lx1", T.XT[:, 2064:4112], T.ax[:, 2048:4096], [b("XT", 2064, 4112)], [])
-    dma("Y", "le", T.EI[:, 0:128], T.ex[:], [b("EI", 0, 128)], [])
-    for m in WRITES:
-        arrive(m)
-    C = lambda j: b("COL", j, j + 1)
-    IP = lambda j: b("IP", j, j + 1)
-    half = lambda buf, h: b(buf, 64 * h, 64 * h + 64)
-    pb = lambda k, lo=0, hi=128, st=1: b("pb%d" % k, lo, hi, st)
-    BC = lambda k: b("BC", 128 * k, 128 * k + 128)
-    SEL = lambda k: b("SEL", 16 - k, 144 - k)
-    def weights(x):
-        return [lambda: ts(b("WI2", 0, 1), b("EI" + x, 128, 129), 6, None, A.arith_shift_right),
-                lambda: ts(b("WI2", 1, 2), b("EI" + x, 128, 129), 63, None, A.bitwise_and),
-                lambda: cp(b("COL", 4, 6), b("WI2", 0, 2)),
-                lambda: ts(b("WH" + x), b("BB"), C(4), -32.0, A.mult, A.mult),
-                lambda: ts(b("WL" + x), b("BB"), C(5), -0.5, A.mult, A.mult),
-                lambda: act(b("KC" + x), b("EI" + x, 129, 130))]
-    def offsets(x):
-        mm(pb(5, 0, 64), b("WL" + x), half("C2K", 0), True, False)
-        mm(pb(5, 0, 64), b("WH" + x), half("C2K", 0), False, False)
-        mm(pb(5, 64, 128), b("IHH"), half("C2K", 0), False, False)
-    def explicit(x):
-        for h in range(2):
-            act(half("EBH" + x, h), b("EI" + x, h, 128, 2), bias=-2048.0)
-    iota(IP(0), [[0, 1]], 0, 1, False)
-    iota(b("IOT"), [[1, 128]], 0, 0)
-    iota(b("G16"), [[1, 8], [0, 16]], 0, 0)
-    iota(b("R16"), [[0, 8], [1, 16]], 0, 0)
-    iota(b("KLI"), [[1, 8]], 0, 0, False)
-    ms(b("RST"), -1.0e9)
-    ms(b("FLI"), 0.0)
-    cp(C(0), IP(0))
-    ts(IP(1), IP(0), 15, None, A.bitwise_and)
-    ts(IP(2), IP(0), 4, None, A.arith_shift_right)
-    ms(b("RST", 0, 128, 16), 1.0e9)
-    for j in (1, 2):
-        cp(C(j), IP(j))
-    act(b("ONES"), b("IOT"), F.Sigmoid, bias=40.0)
-    ts(b("I"), b("IOT"), C(0), None, A.is_equal)
-    ms(b("BAR", 0, 1), 3.5)
-    cp(b3("EX", 0, 128, 0, None), b("I"))
-    ts(b("NI"), b("I"), -1.0, None, A.mult)
-    cp(b3("EX", 0, 128, 1, 2), b3("EX", 0, 128, 0, 1))
-    ts(b("BB"), b("G16"), C(2), None, A.is_equal)
-    cp(b3("EX", 0, 128, 2, 4), b3("EX", 0, 128, 0, 2))
-    ms(b("XT", 0, 16), 0.0)
-    cp(b3("EX", 0, 128, 4, 8), b3("EX", 0, 128, 0, 4))
-    ts(b("MASK"), b("R16"), C(1), None, A.is_equal)
-    ms(b("C2K"), 2048.0)
-    ts(b("IHH"), b("I"), -0.5, None, A.mult)
-    ts(half("AF", 0), b("PI", 0, 128, 2), -2.0, -2048.0, A.mult, A.add)
-    for f_ in weights(""):
-        f_()
-    offsets("")
-    for h in range(2):
-        act(half("P", h), b("PI", h, 128, 2))
-    push("p0", b("PI"))
-    iota(b("NEW"), [[1, 256]], 3840 - 2048, 0)
-    keep(b("ZW1", 768, 896), b("PI"), [[0, 128]], 0)
-    waits("G", regions([b("XT", 16, 4112)], []))
-    copy_out(0, False)
-    act(b("NB"), b("BB"), scale=-2048.0)
-    act(b("B4"), b("BB", 0, 128, 16), scale=4096.0)
-    act(b("IH"), b("I"))
-    act(b("B8H"), b("BB", 0, 128, 16))
-    act(b("KL"), b("KLI"))
-    bcv = lambda k: lambda: ts(BC(k), b("BB"), b("MASK", k, k + 1), None, A.mult)
-    later = [bcv(k) for k in range(16)] + [
-        lambda: ts(b("NIH"), b("I"), -1.0, None, A.mult), lambda: ts(b("I128"), b("I"), 128.0, None, A.mult),
-        lambda: ts(b("I8"), b("I"), 8192.0, None, A.mult), lambda: ts(b("BB8"), b("BB"), 8192.0, None, A.mult),
-        lambda: ts(b("MBIG"), b("MASK"), -14336.0, 16384.0, A.mult, A.add), lambda: ms(b("FL"), 0.0),
-        lambda: ms(b("XT1", 0, 16), 0.0), lambda: ms(b("XT3", 0, 16), 0.0), lambda: ms(b("SEL"), 0.0), lambda: cp(b("SEL", 16, 144, 16), b("BB", 0, 128, 16))]
-    def spare(k):
-        for _ in range(min(k, len(later))):
-            later.pop(0)()
-
-    SP, edge = [], {(e, h): 128 * h for e in range(2) for h in range(2)}
-    for i, ((e, h), w) in enumerate(zip(SETS, SW)):
-        lo = edge[e, h] - w * h
-        SP.append((e, i % 4, lo, lo + w))
-        edge[e, h] = lo if h else lo + w
-    VP = ((0, 64, 64 + VA), (0, 64 + VA, edge[0, 1]), (0, edge[0, 0], 64), (1, 64, edge[1, 1]), (1, edge[1, 0], 64))
-    v0, v1 = min(edge[0, 0], edge[1, 0]), max(edge[0, 1], edge[1, 1])
-    copies = [(k, lo, min(lo + 32, v1)) for k, lo in zip((6, 7, 2), range(v0, v1, 32))]
-    bank = lambda k, w: b3("pb%d" % k, 0, w) if k < 3 else pb(k, 0, 16 * w)
-    sbank = lambda i: bank(SP[i][1], SP[i][3] - SP[i][2])
-    ZP = ((0, ZV[0]), (ZV[0] + ZV[1], 64), (ZV[0], ZV[0] + ZV[1]))
-    fh = lambda h: b("FS", 128 * h + 1, 128 * h + 128, 2)
-    fall = b("FS", 1, 256, 2)
-
-    def names_prepare(t):
-        for k in range(16):
-            mm(pb(7, 64, 128), SEL(k), half("EQ", k + 1), k == 0, k == 15)
-        for h in range(2):
-            mm(pb(3, 2 * h, 256, 4), b("IH"), b("NEW", 64 * t, 64 * t + 64), h == 0, False)
-            mm(pb(3, 2 * h, 256, 4), b("NIH"), fh(h), False, False)
-            mm(pb(3, 2 * h + 1, 256, 4), b("IH"), fh(h), False, False)
-        mm(pb(3, 1, 256, 2), b("IH"), b("C2K"), False, True)
-    def names_flags():
-        act(b("FL", 1, 256, 4), pb(4, 0, 64), F.Sign)
-        act(b("FL", 3, 256, 4), pb(7, 64, 128), F.Sign)
-    def names():
-        scan(b("FF"), b("FL"), pb(3, 0, 256), A.mult, A.add)
-    def names_out(t):
-        act(b("FO", 128 * t, 128 * t + 128), b("FF", 1, 256, 2))
-        push("f%d" % t, b("FO", 128 * t, 128 * t + 128))
-    def bar_count():
-        mm(pb(6), b("ONES"), b("BR"))
-        act(b("JNK"), pb(6), accum=b("CNT"))
-    def bar(t):
-        return [lambda: cp(b("CI", 0, 1), b("CNT")), lambda: ts(b("CI", 1, 2), b("CI", 0, 1), 1, None, A.bitwise_and),
-                lambda: ts(b("BARS", 4 * t, 4 * t + 1), b("CI", 1, 2), 3.5, None, A.add), lambda: push("b%d" % t, b("BARS", 4 * t, 4 * t + 1))]
-
-    for t in range(4):
-        n = 768 + 128 * t
-        x, nx = [str(u) if PLAY[u] else "" for u in (t, t + 1)]
-        stay = nx != ""
-        XW, XQ = b("XT" + x, 16, 4112), b("XT" + x, 0, 4112)
-        ZW, RW = b("ZW" + x, 0, n), b("RI" + x, 0, n)
-        mm(pb(5, 0, 64), b("WH" + x), half("AF", 0), False, False)
-        mm(pb(5, 0, 64), b("WL" + x), half("AF", 0), False, False)
-        mm(pb(5, 64, 128), b("IHH"), half("AF", 0), False, True)
-        if x:
-            later += bar(t - 1)
-        if t == 0:
-            cp(b3("EX", 0, 128, 8, 16), b3("EX", 0, 128, 0, 8))
-        mm(pb(7), b("P"), b("I"))
-        mm(pb(4), b("P"), b("NB"), True, False)
-        cp(b("UI"), pb(5, 0, 64))
-        spare(1)
-        ts(b("UM"), b("UI"), 4095, None, A.bitwise_and)
-        spare(1)
-        tt(b("SQ"), b("UM"), b("UM"), A.mult)
-        act(b("PT"), pb(7))
-        for k, (lo, hi) in enumerate(ZP):
-            mm(b3("pb%d" % k, 0, hi - lo), b("PT"), b3("EX", 64 + lo, 64 + hi), True, False)
-        def spread_p(i):
-            k, lo, hi = copies[i]
-            mm(bank(k, hi - lo), b("PT"), b3("EX", lo, hi))
-        spread_p(0)
-        spread_p(1)
-        ts(pb(5, 128, 192), b("UM"), b("KC" + x), None, A.mult)
-        ts(b("T1"), b("SQ"), 5, 4095, A.arith_shift_right, A.bitwise_and)
-        spare(1)
-        tt(b("H1"), b("T1"), pb(5, 128, 192), A.add)
-        spare(1)
-        ts(b("H2"), b("H1"), 4095, None, A.bitwise_and)
-        spare(1)
-        ts(b("C16"), b("H2"), n / 4096.0, -31.0 / 64.0, A.mult, A.add)
-        spare(1)
-        if t:
-            for h in range(2):
-                keep(b("ZW" + nx, n + h, n + 128, 2) if stay else b("PN", 128 * t + h, 128 * t + 128, 2), half("P", h), [[0, 64]], 0)
-            if not stay:
-                push("p%d" % t, b("PN", 128 * t, 128 * t + 128))
-            copy_out(t, False)
-        for h in range(2):
-            act(half("U2", h), b("UM"))
-        def zsum(lo, hi, m):
-            mm(b("pb4", m, 128, 16, hi, lo), b("ZG", 16 * lo + m, 16 * hi, 16), b("NB", 0, 128, 16), False, False)
-        def zdiff(k):
-            lo, hi = ZP[k]
-            mm(b3("pb%d" % k, 0, hi - lo), b("NI"), b("ZG", 16 * lo, 16 * hi), False, True)
-        def zabs(k, m0, m1):
-            lo, hi = ZP[k]
-            act(b3("AB", 64 + lo, 64 + hi, m0, m1), b3("pb%d" % k, 0, hi - lo, m0, m1), F.Abs, scale=0.5)
-        zget = lambda k: (b("ZG", 16 * ZP[k][0], 16 * ZP[k][1]), ind(ZW, b("C16", *ZP[k])))
-        cp(*zget(0))
-        act(*zget(1))
-        cp(b("CF"), b("C16"))
-        cp(*zget(2))
-        zdiff(0)
-        zdiff(1)
-        for h in range(2):
-            mm(b("pb4", p0=64 * h, p=64 * h + 64), b("CF"), b("IH"), False, False)
-        zdiff(2)
-        for m in range(16):
-            zsum(0, 64, m)
-            tt(b3("AB", 0, 64, m, None), b("ZG", m, 1024, 16), pb(5, 64, 128), A.max)
-        done, summed = [0, 0, 0], 0
-        for k, m1 in ZO:
-            zabs(k, done[k], m1)
-            done[k] = m1
-            for m in range(summed, min(done)):
-                mm(pb(4, m, 128, 16), b3("AB", 0, 128, m, None), b("B4"), False, m == 15)
-            summed = min(done)
-        spread_p(2)
-        if x:
-            names()
-        spare(4)
-        for k, lo, hi in copies:
-            act(b("PRS", 16 * lo, 16 * hi), bank(k, hi - lo))
-        if x:
-            act(b("RI" + x, n - 128, n), b("FF", 1, 256, 2))
-        def fill(i):
-            mm(sbank(i), b("PT"), b3("EX", SP[i][2], SP[i][3]), True, False)
-        fill(0)
-        fill(1)
-        if t == 0:
-            explicit("")
-        if t == 2:
-            act(b("RI", n - 128, n), b("YR", 128 * t - 128, 128 * t))
-            copy_out(t, True)
-        scan(b("SC"), b("RST"), pb(4), A.max, A.min)
-        spare(1)
-        ts(b("LA"), b("SC", 15, 128, 16), 2047, None, A.bitwise_and)
-        spare(1)
-        tt(b("LM"), ind(b("LA"), b("KL")), b("MASK"), A.mult)
-        spare(3)
-        mm(pb(4, 128, 136), b("LM"), b("B8H"))
-        cp(b("L16"), pb(4, 128, 136))
-        spare(1)
-        fill(2)
-        fill(3)
-        LST, VBS = ("E16", "E216"), ("VB", "VB2")
-        def vpiece(e, lo, hi):
-            tt(b(VBS[e], 16 * lo, 16 * hi), ind(XW, b(LST[e], lo, hi)), b("PRS", 16 * lo, 16 * hi), A.is_ge)
-        def sgather(i):
-            e, _, lo, hi = SP[i]
-            y = b("XG", 512 * i, 512 * i + 16 * (hi - lo))
-            act(y, ind(XW, b(LST[e], lo, hi)))
-            mm(sbank(i), b("NI"), y, False, True)
-        def ssign(i):
-            e, _, lo, hi = SP[i]
-            act(b(VBS[e], 16 * lo, 16 * hi), sbank(i), F.Sigmoid, bias=128.0, scale=-256.0)
-        VOTES = {(0, 1): 6, (0, 0): 4, (1, 1): 7, (1, 0): 6}
-        def count(e, h, slots):
-            for m in slots:
-                mm(pb(VOTES[e, h], 0, 64), SEL(m), b(VBS[e], 1024 * h + m, 1024 * h + 1024, 16), m == 0 and (e, h) != (1, 0), m == 15 and (e, h) != (1, 1))
-        votes = lambda h: pb(VOTES[0, h], 0, 64)
-        before = {
-            "d": lambda h: ts(half("BR", h), votes(h), b("BAR", 4 * t, 4 * t + 1), None, A.is_lt),
-            "e": lambda h: tt(half("Y1", h), half("BR", h), pb(5, 128 + 64 * h, 192 + 64 * h), A.mult),
-            "i": lambda h: tt(pb(5, 256 + 128 * h, 384 + 128 * h, 2), half("Y1", h), pb(5, 64 * h, 64 * h + 64), A.add),
-            "j": lambda h: ts(half("G9", h), votes(h), 8.5, 128.0, A.is_ge, A.mult),
-            "k": lambda h: tt(half("TH", h), half("G9", h), votes(h), A.max)}
-        def barred(h):
-            mm(pb(VOTES[1, h], 0, 64), b("I128"), half("BR", h), h == 0, h == 1)
-        def flag(h):
-            tt(b("FLI", 128 * h + 1, 128 * h + 128, 2), pb(VOTES[1, h], 0, 64), half("TH", h), A.is_ge)
-        def choose(h):
-            scan(b("FS", 128 * h, 128 * h + 128), b("FLI", 128 * h, 128 * h + 128), pb(5, 256 + 128 * h, 384 + 128 * h), A.mult, A.add)
-        def deltas():
-            mm(pb(5, 128, 256), b("IH"), b("EBH" + x), True, False)
-            mm(pb(5, 128, 256), b("NIH"), b("E2H"), False, False)
-            mm(pb(5, 0, 128), b("IH"), b("E2H"), False, False)
-            mm(pb(5, 0, 128), b("NIH"), b("EH"), False, False)
-            mm(pb(5, 257, 512, 2), b("IH"), b("EH"), False, True)
-        act(b("E16"), ind(RW, b("L16")))
-        tt(b("EU"), ind(RW, b("L16")), b("U2"), A.mult)
-        spare(1)
-        act(pb(5), b("E16"), bias=77.0 * t)
-        ts(b("SH"), b("EU"), 5, None, A.arith_shift_right)
-        spare(len(later))
-        adapt = (lambda: tt(b("SM"), b("SH"), pb(5), A.add), lambda: ts(b("SA"), b("SM"), 4095, None, A.bitwise_and),
-                 lambda: cp(b("E216"), b("SA")), lambda: ts(b("E2H"), b("E216"), -2048.0, None, A.add),
-                 lambda: ts(b("EH"), b("E16"), -2048.0, None, A.add), deltas)
-        step = {"g": sgather, "s": ssign, "f": fill, **before, "r": barred, "l": flag, "h": choose, "a": lambda i: adapt[i](),
-                "c": lambda i: count(i // 4, i // 2 % 2, range(8 * (i % 2), 8 * (i % 2) + 8)), "v": lambda i: vpiece(*VP[i])}
-        for y in ORDER.split():
-            step[y[0]](int(y[1]))
-        if x:
-            names_out(t - 1)
-        if t == 0:
-            later += weights("1")
-            explicit("1")
-            act(b("JNK"), b("MASK"), scale=4096.0)
-            for h in range(2):
-                tt(half("NXD", h), half("MASK", h), b("IOT", 0, 64), A.mult)
-            ms(b("RQ"), 255.0)
-        spread = lambda k: b3("pb%d" % (k // 4), 4 * (k % 4), 4 * (k % 4) + 4) if k < 12 else pb(k // 4, 64 * (k % 4), 64 * (k % 4) + 64)
-        for k in range(16):
-            mm(spread(k), BC(k), fh(1))
-        flag(0)
-        if t == 0:
-            ms(b("RQ", 0, 1024, 16), 0.0)
-        choose(0)
-        if t == 0:
-            tt(b("NXD"), b("NXD"), b("JNK"), A.add)
-        act(b("FQ"), fh(0), bias=2064.0)
-        mm(pb(7, 0, 64), BC(0), fh(0))
-        mm(pb(6), BC(0), fall, True, False)
-        mm(pb(6), b("I"), b("MBIG"), False, False)
-        for k in range(16):
-            tt(half("EQ", k + 1), fh(0), spread(k), A.is_equal)
-            mm(pb(4, 0, 64), b("I8"), half("EQ", k + 1), k == 0, k == 15)
-            if k == EQ0:
-                tt(half("EQ", 0), fh(1), pb(7, 0, 64), A.is_equal)
-                mm(pb(6), b("BB8"), b("EQ", 0, 128), False, True)
-        for h in range(2):
-            scan(half("F0S", h), half("NXD", h), pb(6, 64 * h, 64 * h + 64), A.max, A.min)
-        spare(1)
-        tt(b("Q16"), b("FQ"), pb(4, 0, 64), A.min)
-        cp(b("MS", 72 * t, 72 * t + 8), b("F0S", 15, 128, 16))
-        for lo, hi in ((0, QA), (QA, QS)):
-            act(b("GQ", 16 * lo, 16 * hi), ind(XQ, b("Q16", lo, hi)))
-        cp(b("GQ", 16 * QS, 1024), ind(XQ, b("Q16", QS, 64)))
-        names_prepare(t)
-        if t < 3:
-            bar_count()
-        names_flags()
-        B = 3856 + 64 * t
-        if stay:
-            for h in range(2):
-                act(half("PB", h), half("P", h), bias=2302.75)
-        for lo, hi in ((QS, 64), (0, QA), (QA, QS)):
-            spare(1)
-            scan(b("SQM", 16 * lo, 16 * hi), b("RQ", 16 * lo, 16 * hi), b("GQ", 16 * lo, 16 * hi), A.min, A.max)
-        rec = b("SQM", 15, 1024, 16)
-        if stay:
-            spare(1)
-            cp(b("XT" + nx, B, B + 64), rec)
-            act(b("XT" + nx, 4112, 4176), rec)
-            act(b("MS", 72 * t + 8, 72 * t + 72), rec)
-            push("m%d" % t, b("MS", 72 * t, 72 * t + 72))
-            spare(len(later))
-            src, XN = "MS", b("XT" + nx, 16, 4176)
-        else:
-            cp(b("MS", 72 * t + 8, 72 * t + 72), rec)
-            push("m%d" % t, b("MS", 72 * t, 72 * t + 72))
-            names()
-            names_out(t)
-            if t == 1:
-                for f_ in bar(t) + weights("3"):
-                    f_()
-                explicit("3")
-                act(b("RI", n - 128, n), b("YR", 128 * t - 128, 128 * t))
-            act(b("XT", B - 64, B), b("ML", 72 * t - 64, 72 * t))
-            for h in range(2):
-                act(half("PB", h), b("ZW", n + h, n + 128, 2), bias=2302.75)
-            cp(b("XT", B, B + 64), b("ML", 72 * t + 8, 72 * t + 72))
-            act(b("XT", 4112, 4176), b("ML", 72 * t + 8, 72 * t + 72))
-            src, XN = "ML", b("XT", 16, 4176)
-        if t < 3:
-            offsets(nx)
-            for h in range(2):
-                tt(half("AF", h), ind(XN, b(src, 72 * t + 4 * h, 72 * t + 4 * h + 4)), half("PB", h), A.subtract)
-            ts(b("P"), b("AF"), -0.5, -1024.0, A.mult, A.add)
-        else:
-            tt(b("AF"), ind(XN, b(src, 72 * t, 72 * t + 8)), b("PB"), A.subtract)
-            for h in range(2):
-                ts(b("YP", h, 128, 2), half("AF", h), -0.5, -1024.0, A.mult, A.add)
-    dma("Y", "o0", T.yr[:, 0:384], T.YR[:, 0:384], [], [b("YR", 0, 384)])
-    dma("Y", "o1", T.yr[:, 384:512], T.YR[:, 384:512], [], [b("YR", 384, 512)])
-    dma("S", "o2", T.yp[:], T.YP[:], [], [b("YP")])
+            m, x = kind[1:]
+            k = COPIES[int(m[1:])] if m[0] == "k" else None
+            watch = "lu%d" % k[0] if k and (k[1], k[3]) == ("XT", 4112) else None
+            k = send(g, topo, core, _WAYS[m, rank][1], m, ap(place(m)), ap(x), T.sem["a" + m], T.sem[watch or "ls"])
+            if watch:
+                done([(x[0], x[2], False)], watch, k, "D", {})
+            else:
+                sent += k
     for s in sorted(total):
         if clk["G"].get(s, 0) < total[s]:
             g.wait_ge(T.sem[s], total[s])
-    g.wait_ge(T.sem.ls, sent[0])
+    g.wait_ge(T.sem.ls, sent)

import numpy as np
from concourse.mybir import AluOpType as A, ActivationFunctionType as F

N, WORLD = 8, 256
PLAY = (0, 1, -4, -1, 0)
SETS = ((0, 1), (0, 0), (1, 1), (1, 0), (1, 0))
SW = [32, 32, 24, 18, 10]
SB = (0, 1, 2, 3, 0)
HG = (0, 1)
FT = 0
BG = 0
BS = 0
FAC = 1.2
ONS = (0, 0)
VB4 = 16
ORDER = "o1 o0 q0 z1 o2 z0 U0 t0 b0 t1 z2 b1 t2 u0 m0 m1 b2 m2 u1 b4 w0 w1 b3 m3 w2 w3 f2 p1 f1 p0 n0 n1 n2 p2 n3 U1 f3 n4 E1 H1 S1 v1 E0 H0 A1 f0 S0 v0 g0 g1 s0 B1 f4 A0 c2 v2 B0 g2 s1 v3 c3 j1 c0 g4 a0 v5 c1 d1 a1 g3 d0 s2 k1 v4 j0 s4 c6 s3 c7 e1 i1 r0 k0 y1 c4 l1 e0 h1 c5 i0 l0 P0 P1 h0 P2 P3 F1 x0 x1 x2 x3 F0 F2 Q0 G1 F3 M1 G0 M0 G2 M2 F4"
VA = 8
ZO = ((0, 0, 16), (1, 0, 8), (2, 0, 8), (1, 8, 16), (2, 8, 16))
QP = (("S", 0, 30), ("V", 38, 64), ("S", 30, 38))
ZV = [16, 22]
LAT, GAT, HOP, DMA = 0.18, 1.5, 2.0, 1.7
SLACK = 6.0
GATE = "FQ"
_D = {"f": "float32", "b": "bfloat16", "h": "float16", "i": "int32", "u": "uint16"}
_S = """XT 4176 b;ZW 1280 b;RI 1280 i;WE 648 h;KC 4 f;YR 512 f;EI 128 i;WK 4 i;QL 576 b
WI2 16 i;COL 16 f;PI 128 b;PN 512 b;P 128 b;PT 128 b;FN 512 i
PRS 2048 b;PB 128 f;IP 4 i;IOT 128 f;R16 128 f;G16 128 f;NEW 256 h;KL 8 u;I 128 b;EX 128x16 b;BB 128 b;N8 8 b
B4 8 b;B8H 8 h;IH 128 h;NIH 128 h;I8 128 b;I128 128 b;FLI 256 b;IQ 128 b;NG 128 b;NQ 128 b;SEQ 144 b;C2Z 128 h;BB8 128 b;ONES 128 b;C2K 128 h;IHH 128 h;MASK 128 f;MBIG 128 b;NXD 128 f;RST 128 f;RQ 512 b
SEL 144 b;BC 2048 h;BAR 16 f;BARS 16 f;CR 448 b;VG 128 f;UC 256 f;SQ 128 i;H2 64 i;C16 64 u;CFZ 192 h
ZG 1024 b;AB 128x16 b;SC 128 i;LA 8 i;LM 128 h;L16 8 u;E16 128 u;EH 256 h;ES 256 i;SA 128 i;E216 128 u;E2H 128 h
VB 2048 b;VB2 2048 b;XG 3072 b;NI 128 b;BR 128 b;G9 128 b;TH 128 b;Y1 128 f;D1 256 f;FS 256 h;JNK 128 f;CNT 1 f;CI 2 i
FQ 64 f;EQ 1088 b;Q16 64 u;GQ 1024 b;SQM 1024 b;F0S 128 f;FL 256 b;FF 256 f;MS 288 u;ML 576 u;AF 128 h;YP 128 f"""
TAB = [str(t) if PLAY[t] else "" for t in range(5)]
for _t in range(1, 4):
    if PLAY[_t]:
        _S += ";XT%d 4176 b;ZW%d %d b;RI%d %d i;WE%d 648 h;KC%d 4 f" % (_t, _t, 768 + 128 * _t, _t, 768 + 128 * _t, _t, _t)
SHAPE = {x.split()[0]: [int(v) for v in x.split()[1].split("x")] for x in _S.replace("\n", ";").split(";")}
SCRATCH = {x.split()[0]: ("sbuf", [128] + SHAPE[x.split()[0]], _D[x.split()[2]]) for x in _S.replace("\n", ";").split(";")}
for _b in range(8):
    SHAPE["pb%d" % _b] = [32, 16] if _b < 3 else [512]
    SCRATCH["pb%d" % _b] = ("psum", [128] + SHAPE["pb%d" % _b], "float32")
OWNER = [(PLAY[t] + 1 + t % 3) % N for t in range(4)]
LANES = [(OWNER[t] - PLAY[t + 1]) % N for t in range(4)]
COPIES = ((1, "WE", 0, 520, 0, 0), (1, "ZW", 0, 768, 1, 0), (1, "XT", 16, 1040, 1, 0), (1, "XT", 1040, 2064, 0, 0),
          (1, "XT", 2064, 3088, 1, 0), (1, "XT", 3088, 4112, 0, 0), (1, "RI", 0, 448, 3, 0), (1, "RI", 448, 768, 2, 0), (1, "WE", 520, 648, 1, 0),
          (2, "XT", 16, 1040, 2, 1), (2, "WE", 0, 648, 0, 1), (2, "XT", 1040, 2064, 2, 1), (2, "XT", 2064, 3088, 0, 1), (2, "XT", 3088, 4112, 0, 1),
          (2, "RI", 0, 768, 2, 1), (2, "ZW", 0, 768, 0, 1),
          (3, "XT", 16, 1040, 2, 3), (3, "XT", 1040, 2064, 3, 3), (3, "WE", 0, 648, 0, 3), (3, "XT", 2064, 3088, 1, 3), (3, "XT", 3088, 4112, 0, 3),
          (3, "ZW", 0, 768, 1, 3), (3, "RI", 0, 384, 2, 3), (3, "RI", 384, 768, 3, 3))
MESSAGES = ([k + str(t) for t in range(4) if LANES[t] for k in "pmf"] + [k + str(t) for t in range(3) for k in "bqyz"[:4 - t // 2]])
WRITES = MESSAGES + ["k%d" % i for i in range(len(COPIES))]
SEMAPHORES = (["sv", "sa", "st", "sg", "ls", "lu1", "lu2", "lu3", "rl", "lp", "lw", "lz", "lr", "le", "lx0", "lx1", "o0", "o1", "o2"]
              + ["a" + m for m in WRITES])


def shift(m):
    if m[0] == "k":
        return -PLAY[COPIES[int(m[1:])][0]]
    t = int(m[1])
    return PLAY[t] - PLAY[t + 1] if m[0] == "b" else PLAY[t + 1] - PLAY[t + 2] if m[0] in "zqy" else LANES[t]


def hops(T, topo, src, dst, m):
    if dst in topo.cores_of(src) or (m[0] != "k" and topo.may_write(src, dst)):
        return [src, dst]
    way = COPIES[int(m[1:])][4] if m[0] == "k" else 0
    idle = lambda cores, to: [x for x in cores if (topo.die(x) != topo.die(src)) == way % 2 and topo.may_write(x, to) and T.rank_of(x) is None]
    if way < 2:
        return [src, idle(topo.cores_of(src), dst)[0 if m[0] == "k" else -1], dst]
    far = idle([x for x in range(WORLD) if topo.mates(x, dst)], dst)[0]
    return [src, idle(topo.cores_of(src), far)[0], far, dst]


def engines(topo, src, dst, m):
    e = topo.engines(src, dst)
    if dst not in topo.cores_of(src) or m[0] == "m" or (m[0] == "k" and COPIES[int(m[1:])][0] == 1):
        return e
    return e[len(e) // 2:] if m[0] == "k" else e[:len(e) // 2]


def send(g, topo, src, dst, m, out, in_, rsem, lsem):
    rid, pid = topo.addr(dst, src)
    e = engines(topo, src, dst, m)
    g.remote_dma(out, in_, rsem, lsem, pid, rid, sum(1 << x for x in e))
    return len(e)


def view(name, *ix, p=(0, 128)):
    sh = SHAPE[name]
    ix = tuple(slice(*x.indices(n)) if isinstance(x, slice) else x for x, n in zip(ix + (slice(None),) * len(sh), sh))
    cols = np.arange(int(np.prod(sh))).reshape(sh)[ix].reshape(-1)
    m = np.zeros(int(np.prod(sh)), np.uint8)
    m[cols] = 1
    return (name, (slice(*p),) + ix, int.from_bytes(np.packbits(m, bitorder="little").tobytes(), "little"), len(cols), None)


def b(name, lo=0, hi=None, st=1, p=128, p0=0):
    return view(name, slice(lo, hi, st), p=(p0, p))


def b3(name, lo, hi, c0=0, c1=16):
    return view(name, slice(lo, hi), c0 if c1 is None else slice(c0, c1))


def place(m):
    if m[0] == "k":
        k = COPIES[int(m[1:])]
        return b(k[1] + str(k[0]), *k[2:4])
    t = int(m[1])
    x = TAB[t + (2 if m[0] in "zqy" else 1)]
    buf, lo, w = {"p": ("ZW" + x, 768 + 128 * t, 128), "m": ("ML", 72 * t, 72), "f": ("RI" + x, 768 + 128 * t, 128), "b": ("BAR", 4 * t + 4, 1),
                  "z": ("ZW" + x, 768, 128 * t + 128), "y": ("RI" + x, 768, 128 * t + 128), "q": ("QL", 192 * t, 64 * t + 64)}[m[0]]
    return b(buf, lo, lo + w)


def program():
    ops = []
    cyc = 0.83e-3
    two = lambda *xs: all(SCRATCH[x[0]][2] in ("bfloat16", "float16", "uint16") for x in xs)

    chain = [""]
    def op(q, make, writes, reads, us, extra=None): ops.append((q, make, writes, reads, us, extra, q if q == "Y" or q in chain[0] else extra and extra[1][0] == "k" and "k"))
    def vcost(a, rate): return 0.05 + a[3] * cyc * max(GAT, rate) if a[4] else max(64, a[3] * rate) * cyc
    def ind(w, o): return (w[0], w[1], w[2], 16 * o[3], o)
    def ts(out, a, s1, s2, o0, o1=None):
        col = [x for x in (s1, s2) if isinstance(x, tuple)]
        o = (o0,) if o1 is None else (o0, o1)
        op("V", lambda e, ap: e.tensor_scalar(ap(out), ap(a), ap(s1), ap(s2), *o), [out], [a] + col, vcost(a, 0.5 if two(out, a) else 1))
    def tt(out, a, c, o):
        op("V", lambda e, ap: e.tensor_tensor(ap(out), ap(a), ap(c), o), [out], [a, c], vcost(a, 1 if "pb" in (a[0][:2], c[0][:2]) else 2))
    def cp(out, a): op("V", lambda e, ap: e.tensor_copy(ap(out), ap(a)), [out], [a], vcost(a, 0.5 if two(out, a) else 1))
    def ms(out, c): op("V", lambda e, ap: e.memset(ap(out), c), [out], [], vcost(out, 0.5 if two(out) else 1))
    def scan(out, a, c, o0, o1):
        op("V", lambda e, ap: e.tensor_tensor_scan(ap(out), ap(a), ap(c), 0.0, o0, o1), [out], [a, c], vcost(a, 0.5 if two(out, a, c) else 1))
    def act(out, a, f=F.Copy, bias=0.0, scale=1.0, accum=None):
        cols = [x for x in (bias, scale) if isinstance(x, tuple)]
        def make(e, ap):
            if accum is None:
                return e.activation(ap(out), ap(a), f, bias=ap(bias), scale=ap(scale))
            return e.activation(ap(out), ap(a), f, bias=ap(bias), scale=ap(scale), accum_out=ap(accum))
        op("S", make, [out] + ([accum] if accum else []), [a] + cols, (0.065 + a[3] * cyc * GAT if a[4] else max(64, a[3]) * cyc) + (0.14 if accum else 0))
    def mm(out, l, r, start=True, stop=True):
        op("T", lambda e, ap: e.matmul(ap(out), ap(l), ap(r), start, stop), [out], [l, r],
           max(min(64, l[3]), r[3]) * cyc / 2 * (1 if two(l) else 4))
    def iota(out, pat, base, cm=0):
        if SCRATCH[out[0]][2] == "int32":
            op("G", lambda e, ap: e.iota(ap(out), pat, base, cm), [out], [], 0.13 + 2 * cyc * out[3])
        else:
            op("G", lambda e, ap: e.iota(ap(out), pat, base, cm, allow_small_or_imprecise_dtypes=True), [out], [], 0.13 + 2 * cyc * out[3])
    def keep(out, a, pat=None, base=0, cm=0):
        op("G", lambda e, ap: e.affine_select(ap(out), ap(a), pat or [[0, a[3]]], A.is_equal, 0.0, base, cm), [out], [a], 0.17 + 2 * cyc * a[3])
    size = lambda x: 128 * x[3] * (2 if two(x) else 4)
    def dma(q, sem, moves, load):
        sb = [x[0] for x in moves]
        op(q, moves, sb if load else [], [] if load else sb, 0.07 * len(moves), ("dma", sem, sum(size(x) for x in sb), load))
    def push(m, x, after=()):
        op("G", None, [], [x] + list(after), 0.2, ("push", m, x))
        op("R", None, [place(m)], [], 0.0, ("arrive", m, size(x)))
    def copies(when, after):
        for i, (_, buf, lo, hi, _, w) in enumerate(COPIES):
            if w == when:
                push("k%d" % i, b(buf, lo, hi), [after])

    sl = slice
    dma("Y", "lp", [(b("PI"), "p0", sl(None))], True)
    dma("S", "lw", [(b("WK", 0, 1), "wt", sl(None)), (b("WK", 1, 2), "km", sl(None))], True)
    dma("Y", "lz", [(b("ZW", 0, 768), "zp", sl(None))], True)
    dma("Y", "lr", [(b("RI", 0, 768), "rt", sl(None))], True)
    dma("S", "lx0", [(b("XT", 16, 2064), "ax", sl(0, 2048))], True)
    dma("Y", "lx1", [(b("XT", 2064, 4112), "ax", sl(2048, 4096))], True)
    dma("Y", "le", [(b("EI"), "ex", sl(None))], True)
    C = lambda j: b("COL", j, j + 1)
    IP = lambda j: b("IP", j, j + 1)
    half = lambda buf, h: b(buf, 64 * h, 64 * h + 64)
    pb = lambda k, lo=0, hi=128, st=1: b("pb%d" % k, lo, hi, st)
    BC = lambda k: b("BC", 128 * k, 128 * k + 128)
    SEL = lambda k, name="SEL": b(name, 16 - k, 144 - k)
    chain[0] = "G"
    iota(IP(0), [[0, 1]], 0, 1)
    iota(b("IOT"), [[1, 128]], 0)
    iota(b("G16"), [[1, 8], [0, 16]], 0)
    iota(b("R16"), [[0, 8], [1, 16]], 0)
    iota(b("C2Z"), [[0, 64], [2048, 2]], 0)
    iota(b("C2K"), [[0, 128]], 2048)
    chain[0] = ""
    iota(b("NEW"), [[1, 256]], 3840 - 2048)
    ms(b("RST"), -1.0e9)
    ms(b("RST", 0, 128, 16), 1.0e9)
    ts(IP(1), IP(0), 15, None, A.bitwise_and)
    ts(IP(2), IP(0), 4, None, A.arith_shift_right)
    cp(b("COL", 0, 3), b("IP", 0, 3))
    act(b("ONES"), b("IOT"), F.Sigmoid, bias=40.0)
    ts(b("I"), b("IOT"), C(0), None, A.is_equal)
    ms(b("BAR", 0, 1), 896.0)
    cp(b3("EX", 0, 128, 0, None), b("I"))
    for w in (1, 2, 4):
        cp(b3("EX", 0, 128, w, 2 * w), b3("EX", 0, 128, 0, w))
    for lo in range(0, 128, 32):
        cp(b3("EX", lo, lo + 32, 8, 16), b3("EX", lo, lo + 32, 0, 8))
    ts(b("BB"), b("G16"), C(2), None, A.is_equal)
    ts(b("MASK"), b("R16"), C(1), None, A.is_equal)
    for name, k in (("NI", -1.0), ("IHH", -0.5)):
        ts(b(name), b("I"), k, None, A.mult)
    for name, k in (("NIH", -1.0), ("I8", 8192.0)) + ((("IQ", 0.25), ("NG", -0.25), ("NQ", -2.0 ** -9)) if FT else (("I128", 128.0),)):
        act(b(name), b("I"), scale=k)
    for h in range(2):
        ts(half("AF", h), b("PI", h, 128, 2), -2.0, -2048.0, A.mult, A.add)
    ts(b("WI2", 0, 1), b("WK", 0, 1), 6, None, A.arith_shift_right)
    ts(b("WI2", 1, 2), b("WK", 0, 1), 63, None, A.bitwise_and)
    cp(b("COL", 4, 6), b("WI2", 0, 2))
    for j, k in enumerate((-32.0, -0.5, 32.0, 0.5)):
        ts(b("WE", 128 * j + 8, 128 * j + 136), b("BB"), C(4 + j % 2), k, A.mult, A.mult)
    ts(b("WI2", 2, 3), b("WK", 1, 2), 2176.0, None, A.add)
    ts(b("WI2", 3, 4), b("WK", 1, 2), 1, None, A.bitwise_and)
    ts(b("WI2", 4, 5), b("WI2", 2, 3), 4095, None, A.bitwise_and)
    ts(b("KC", 0, 1), b("WI2", 4, 5), 32.0, -67584.0, A.mult, A.add)
    tt(C(6), b("WI2", 3, 4), b("WI2", 4, 5), A.subtract)
    ts(b("KC", 1, 2), C(6), 65536.0, 2.0 ** 27, A.mult, A.add)
    ms(b("WE", 0, 8), 0.0)
    PACK = ((32.0, 64.0), (65536.0, 0.0))
    for j, (k, c) in enumerate(PACK):
        act(b("WE", j, j + 1), b("KC", j, j + 1), scale=1.0 / k, bias=c)
    ms(b("CR", 0, 192 + 256 * FT), 0.0)
    for j, terms in enumerate(((2.0 ** 23, -34816.0, -0.5), (1.5 * 2.0 ** 35,), (-1.5 * 2.0 ** 35, -2.0 ** 23, 36864.0), (1.5 * 2.0 ** 23,), (-1.5 * 2.0 ** 23,))[:3 + 2 * FT]):
        for i, k in enumerate(terms):
            ms(b("CR", 64 * j, 64 * j + 64, p0=32 * i, p=32 * i + 1), k)
    for i, k in enumerate((0.5, 2.0 ** -10)[:2 * FT]):
        ms(b("CR", 321, 448, 2, p0=32 * i, p=32 * i + 1), k)
    if not FT:
        iota(b("FLI"), [[0, 256]], 0)
    for h in range(2):
        act(half("P", h), b("PI", h, 128, 2))
        act(b("WE", 520 + 64 * h, 584 + 64 * h), b("EI", h, 128, 2), bias=-2048.0)
    act(b("N8"), b("BB", 0, 128, 16), scale=-2048.0)
    act(b("B4"), b("BB", 0, 128, 16), scale=4096.0)
    act(b("IH"), b("I"))
    act(b("B8H"), b("BB", 0, 128, 16))
    act(b("KL"), b("IOT", 0, 8))
    for zero in (b("CFZ"), b("SEL"), b("EH", 0, 256, 2)):
        iota(zero, [[0, zero[3]]], 0)
    for zero in [b("FL", 0, 256, 2)] + [b("XT" + x, 0, 16) for x in sorted(set(TAB))]:
        ms(zero, 0.0)
    for k in range(16):
        if k < BG:
            keep(BC(k), b("BB"), [[-16, 8], [0, 16]], -k, 1)
        elif k < BG + BS:
            act(BC(k), b("BB"), scale=b("MASK", k, k + 1))
        else:
            ts(BC(k), b("BB"), b("MASK", k, k + 1), None, A.mult)
    act(b("BB8"), b("BB"), scale=8192.0)
    act(b("MBIG"), b("MASK"), scale=-14336.0, bias=16384.0)
    cp(b("SEL", 16, 144, 16), b("BB", 0, 128, 16))
    if FT:
        act(b("SEQ"), b("SEL"), scale=2.0 ** -9)
    iota(b("JNK"), [[0, 2], [1, 64]], 4096)
    tt(b("NXD"), b("MASK"), b("JNK"), A.mult)
    for lo in (0, 256):
        iota(b("RQ", lo, lo + 256), [[0, 16], [255, 16]], 0)

    SP, edge = [], {(e, h): 128 * h for e in range(2) for h in range(2)}
    for i, ((e, h), w) in enumerate(zip(SETS, SW)):
        lo = edge[e, h] - w * h
        SP.append((e, SB[i], lo, lo + w))
        edge[e, h] = lo if h else lo + w
    VP = ((0, 64, 64 + VA), (0, 64 + VA, edge[0, 1]), (0, edge[0, 0], 64), (1, 64, edge[1, 1]), (1, edge[1, 0], 64 - VB4), (1, 64 - VB4, 64))
    v0, v1 = min(edge[0, 0], edge[1, 0]), max(edge[0, 1], edge[1, 1])
    bank = lambda k, w: b3("pb%d" % k, 0, w) if k < 3 else pb(k, 0, 16 * w)
    sbank = lambda i: bank(SP[i][1], SP[i][3] - SP[i][2])
    spreads = [(k, lo, min(lo + 32, v1)) for k, lo in zip((6, 7, 3), range(v0, v1, 32))]
    ZP = ((0, ZV[0]), (ZV[0] + ZV[1], 64), (ZV[0], ZV[0] + ZV[1]))
    fh = lambda h: b("FS", 128 * h + 1, 128 * h + 128, 2)

    for t in range(4):
        n = 768 + 128 * t
        x, nx = TAB[t], TAB[t + 1]
        stay = not LANES[t]
        XW, XQ = b("XT" + x, 16, 4112), b("XT" + x, 0, 4112)
        ZW, RW = b("ZW" + x, 0, n), b("RI" + x, 0, n)
        WH, WL, NH, NL, EB = [b("WE" + x, lo, lo + 128) for lo in range(8, 648, 128)]
        chain[0] = "VST"
        u, AE, K2 = pb(4, 257, 384, 2), half("AF", 0), half("C2K", 0)
        mm(pb(4, 256, 384), NL, b("C2Z"), True, False)
        mm(u, NH, K2, False, False)
        mm(pb(5, 64, 128), b("IHH"), K2, True, False)
        for l, r in ((NH, AE), (NL, AE), *[(b("ONES"), half("CR", j)) for j in range(3)], (WH, K2), (WH, AE), (WL, K2)):
            mm(u, l, r, False, False)
        mm(u, WL, AE, False, True)
        mm(pb(7), b("AF"), b("IHH"))
        mm(pb(5, 64, 128), b("IHH"), AE, False, True)
        ts(b("VG", 0, 128, 2), u, -2048.0, None, A.add)
        ts(b("VG", 1, 128, 2), u, b("KC" + x, 0, 1), b("KC" + x, 1, 2), A.mult, A.add)
        scan(b("SQ"), pb(4, 256, 384), b("VG"), A.mult, A.add)
        act(b("PT"), pb(7), bias=-1024.0)
        for k, (lo, hi) in enumerate(ZP):
            mm(b3("pb%d" % k, 0, hi - lo), b("PT"), b3("EX", 64 + lo, 64 + hi), True, False)
        ts(b("H2"), b("SQ", 1, 128, 2), 5, 4095, A.arith_shift_right, A.bitwise_and)
        ts(b("C16"), b("H2"), n / 4096.0, -31.0 / 64.0, A.mult, A.add)
        if t < 3 or not stay:
            buf, lo = ("ZW" + nx, n) if stay else ("PN", 128 * t)
            for h in range(2):
                keep(b(buf, lo + h, lo + 128, 2), half("P", h))
            if not stay:
                push("p%d" % t, b(buf, lo, lo + 128))
        copies(2 * t, b("C16") if t else b("PI"))
        def factors(h):
            v = b("VG", 0, 128, 2)
            act(b("UC", 128 * h, 128 * h + 128, 2), v, bias=2080.0)
            act(b("UC", 128 * h + 1, 128 * h + 128, 2), v, scale=2048.0, bias=65536.0 - 2.0 ** 22 + 32.0 * 77 * t)
        zget = lambda k: (b("ZG", 16 * ZP[k][0], 16 * ZP[k][1]), ind(ZW, b("C16", *ZP[k])))
        def numbers(_):
            cp(b("CFZ", 64, 128), b("C16"))
            for h in range(2):
                mm(pb(4), b("CFZ", 64 - 64 * h, 192 - 64 * h), b("IH"), h == 0, False)
        def zdiff(k):
            lo, hi = ZP[k]
            mm(b3("pb%d" % k, 0, hi - lo), b("NI"), b("ZG", 16 * lo, 16 * hi), False, True)
        def zsum(i):
            for m in range(8 * i, 8 * i + 8):
                mm(b("pb4", m, 128, 16, 64), b("ZG", m, 1024, 16), b("N8"), False, False)
        def zmax(i):
            for m in range(4 * i, 4 * i + 4):
                tt(b3("AB", 0, 64, m, None), b("ZG", m, 1024, 16), pb(5, 64, 128), A.max)
        def zabs(i):
            k, m0, m1 = ZO[i]
            lo, hi = ZP[k]
            act(b3("AB", 64 + lo, 64 + hi, m0, m1), b3("pb%d" % k, 0, hi - lo, m0, m1), F.Abs, scale=0.5)
        def sums(i):
            for m in range(4 * i, 4 * i + 4):
                mm(pb(4, m, 128, 16), b3("AB", 0, 128, m, None), b("B4"), False, m == 15)
        def spread_p(i):
            k, lo, hi = spreads[i]
            mm(bank(k, hi - lo), b("PT"), b3("EX", lo, hi))
        def beside(i):
            k, lo, hi = spreads[i]
            act(b("PRS", 16 * lo, 16 * hi), bank(k, hi - lo))
        winners = (lambda: scan(b("SC"), b("RST"), pb(4), A.max, A.min),
                   lambda: ts(b("LA"), b("SC", 15, 128, 16), 2047, None, A.bitwise_and),
                   lambda: tt(b("LM"), ind(b("LA"), b("KL")), b("MASK"), A.mult),
                   lambda: mm(pb(4, 128, 136), b("LM"), b("B8H")), lambda: cp(b("L16"), pb(4, 128, 136)))
        L16 = lambda h: b("L16", 4 * h, 4 * h + 4)
        twice = lambda buf, h: b(buf, 128 * h, 128 * h + 128)
        lanes, EH = b, b("EH", 1, 256, 2)
        elect = {
            "z": lambda k: (act if k == 1 else cp)(*zget(k)), "q": numbers, "u": zsum, "t": zdiff, "b": zabs, "w": sums, "m": zmax,
            "n": lambda i: winners[i](), "o": spread_p, "p": beside, "U": factors,
            "E": lambda h: act(half("E16", h), ind(RW, L16(h))),
            "H": lambda h: ts(b("EH", 128 * h + 1, 128 * h + 128, 2), ind(RW, L16(h)) if HG[h] else half("E16", h), -2048.0, None, A.add),
            "S": lambda h: scan(twice("ES", h), twice("EH", h), twice("UC", h), A.mult, A.add),
            "A": lambda h: ts(half("SA", h), b("ES", 128 * h + 1, 128 * h + 128, 2), 5, 4095, A.arith_shift_right, A.bitwise_and),
            "B": lambda h: cp(half("E216", h), half("SA", h))}
        def fill(i):
            mm(sbank(i), b("PT"), b3("EX", SP[i][2], SP[i][3]), True, False)
        LST, VBS = ("E16", "E216"), ("VB", "VB2")
        def vpiece(e, lo, hi):
            tt(b(VBS[e], 16 * lo, 16 * hi), ind(XW, lanes(LST[e], lo, hi)), b("PRS", 16 * lo, 16 * hi), A.is_ge)
        def sgather(i):
            e, _, lo, hi = SP[i]
            y = b("XG", 512 * i, 512 * i + 16 * (hi - lo))
            act(y, ind(XW, lanes(LST[e], lo, hi)))
            mm(sbank(i), b("NI"), y, False, True)
        def ssign(i):
            e, _, lo, hi = SP[i]
            act(b(VBS[e], 16 * lo, 16 * hi), sbank(i), F.Sigmoid, bias=128.0, scale=-256.0)
        VOTES = {(0, 1): 6, (0, 0): 4, (1, 1): 7, (1, 0): 6}
        def count(e, h, slots):
            for m in slots:
                if e:
                    mm(flags(h), SEL(m, "SEQ"), b("VB2", 1024 * h + m, 1024 * h + 1024, 16), False, False)
                else:
                    mm(votes(h), SEL(m), b("VB", 1024 * h + m, 1024 * h + 1024, 16), m == 0, m == 15)
        flags = lambda h: pb(VOTES[1, h], 1, 128, 2)
        votes = lambda h: pb(VOTES[0, h], 0, 64)
        before = {
            "d": lambda h: (act(half("BR", h), votes(h), F.Sigmoid, bias=bar, scale=-256.0) if ONS[h] & 1
                            else ts(half("BR", h), votes(h), 256.0, bar, A.mult, A.is_lt)),
            "e": lambda h: tt(half("Y1", h), half("BR", h), pb(5, 128 + 64 * h, 192 + 64 * h), A.mult),
            "D": lambda h: act(b("D1", 128 * h + 1, 128 * h + 128, 2), half("E16", h), bias=-2048.0),
            "i": lambda h: tt(b("D1", 128 * h, 128 * h + 128, 2), half("Y1", h), pb(5, 64 * h, 64 * h + 64), A.add),
            "j": lambda h: (act(half("G9", h), votes(h), F.Sigmoid, bias=-2176.0, scale=256.0) if ONS[h] & 2
                            else ts(half("G9", h), votes(h), 8.5, None, A.is_ge)),
            "k": lambda h: (act if ONS[h] & 4 else cp)(half("TH", h), votes(h))}
        bar = b("BAR", 4 * t, 4 * t + 1)
        def opening(h):
            mm(pb(VOTES[1, h], 0, 128), b("ONES"), b("CR", 320, 448), True, False)
        def barred(h):
            mm(flags(h), b("IQ"), half("BR", h), False, False)
            mm(flags(h), b("NQ"), half("TH", h), False, False)
            mm(flags(h), b("NG"), half("G9", h), False, False)
        def flag(h):
            for j in (3, 4):
                mm(flags(h), b("ONES"), half("CR", j), False, j == 4)
        def choose(h):
            scan(twice("FS", h), pb(VOTES[1, h], 0, 128), twice("D1", h), A.mult, A.add)
        def deltas():
            mm(pb(5, 128, 256), b("IH"), EB, True, False)
            mm(pb(5, 128, 256), b("NIH"), b("E2H"), False, False)
            mm(pb(5, 0, 128), b("IH"), b("E2H"), False, False)
            mm(pb(5, 0, 128), b("NIH"), EH, False, FT == 1)
            if not FT:
                mm(pb(5, 257, 512, 2), b("IH"), EH, False, True)
        if not FT:
            def count(e, h, slots):
                for m in slots:
                    mm(pb(VOTES[e, h], 0, 64), SEL(m), b(VBS[e], 1024 * h + m, 1024 * h + 1024, 16), m == 0 and (e, h) != (1, 0), m == 15 and (e, h) != (1, 1))
            opening = lambda h: h or mm(pb(VOTES[1, h], 0, 64), b("I128"), half("BR", h), True, False)
            barred = lambda h: h and mm(pb(VOTES[1, h], 0, 64), b("I128"), half("BR", h), False, True)
            flag = lambda h: tt(b("FLI", 128 * h + 1, 128 * h + 128, 2), pb(VOTES[1, h], 0, 64), half("TH", h), A.is_ge)
            choose = lambda h: scan(twice("FS", h), twice("FLI", h), pb(5, 256 + 128 * h, 384 + 128 * h), A.mult, A.add)
            before.update({"D": lambda h: None,
                           "i": lambda h: tt(pb(5, 256 + 128 * h, 384 + 128 * h, 2), half("Y1", h), pb(5, 64 * h, 64 * h + 64), A.add),
                           "j": lambda h: ts(half("G9", h), votes(h), 8.5, 128.0, A.is_ge, A.mult),
                           "k": lambda h: tt(half("TH", h), half("G9", h), votes(h), A.max)})
        over = lambda k: b3("pb1", 4 * k, 4 * k + 4) if k < 8 else pb(7, 64 * k - 512, 64 * k - 448)
        def names_over(i):
            for k in range(4 * i, 4 * i + 4):
                mm(over(k), BC(k), fh(1))
        eq, common = lambda k: half("EQ", k), pb(4, 0, 64)
        def compare(i):
            for k in range(4 * i, 4 * i + 4):
                tt(eq(k), fh(0), over(k), A.is_equal)
                mm(common, b("I8"), eq(k), k == 0, k == 15)
        def first_prepare():
            mm(pb(3, 256, 320), BC(0), fh(0))
            mm(pb(6), BC(0), b("FS", 1, 256, 2), True, False)
            mm(pb(6), b("I"), b("MBIG"), False, False)
        def first_common():
            tt(b("EQ", 1024, 1088), fh(1), pb(3, 256, 320), A.is_equal)
            mm(pb(6, 0, 64), b("BB8"), b("EQ", 1024, 1088), False, False)
        def first_pick():
            mm(pb(6, 64, 128), b("BB8"), eq(0), False, True)
            for h in range(2):
                scan(half("F0S", h), half("NXD", h), pb(6, 64 * h, 64 * h + 64), A.max, A.min)
        first = (lambda: act(b("FQ"), fh(0), bias=2064.0), first_prepare, first_common, first_pick,
                 lambda: cp(b("MS", 72 * t, 72 * t + 8), b("F0S", 15, 128, 16)))
        piece = lambda buf, i: b(buf, 16 * QP[i][1], 16 * QP[i][2])
        shared = {"x": compare, "F": lambda i: first[i](),
                  "Q": lambda _: tt(b("Q16"), b("FQ"), common, A.min),
                  "G": lambda i: (act if QP[i][0] == "S" else cp)(piece("GQ", i), ind(XQ, b("Q16", *QP[i][1:]))),
                  "M": lambda i: scan(piece("SQM", i), b("RQ", 0, 16 * (QP[i][2] - QP[i][1])), piece("GQ", i), A.min, A.max)}
        adapt = (lambda: ts(b("E2H"), b("E216"), -2048.0, None, A.add), deltas)
        step = {"g": sgather, "s": ssign, "f": fill, **before, **elect, **shared, "P": names_over, "r": opening, "y": barred, "l": flag, "h": choose, "a": lambda i: adapt[i](),
                "c": lambda i: count(i // 4, i // 2 % 2, range(8 * (i % 2), 8 * (i % 2) + 8)), "v": lambda i: vpiece(*VP[i])}
        for y in ORDER.split():
            step[y[0]](int(y[1]))
        chain[0] = "T"
        for k in range(16):
            mm(pb(2, 0, 4), SEL(k), eq(k), k == 0, k == 15)
        for h in range(2):
            mm(pb(3, 2 * h, 256, 4), b("IH"), b("NEW", 64 * t, 64 * t + 64), h == 0, False)
            mm(pb(3, 2 * h, 256, 4), b("NIH"), fh(h), False, False)
            mm(pb(3, 2 * h + 1, 256, 4), b("IH"), fh(h), False, False)
        mm(pb(3, 1, 256, 2), b("IH"), b("C2K"), False, True)
        if t < 3:
            mm(pb(6), b("ONES"), b("BR"))
            act(b("JNK"), pb(6), accum=b("CNT"))
        act(b("FL", 1, 256, 4), common, F.Sign)
        act(b("FL", 3, 256, 4), pb(2, 0, 4), F.Sign)
        B = 3856 + 64 * t
        chain[0] = "VST"
        if t:
            act(b("XT" + nx, 3856, B), place("q%d" % (t - 1)))
        for j, (k, c) in enumerate(PACK if nx else ()):
            act(b("KC" + nx, j, j + 1), b("WE" + nx, j, j + 1), scale=k, bias=-k * c)
        rec, msg = b("SQM", 15, 1024, 16), b("MS", 72 * t, 72 * t + 72)
        if not stay:
            cp(b("MS", 72 * t + 8, 72 * t + 72), rec)
            push("m%d" % t, msg)
            rec = b("ML", 72 * t + 8, 72 * t + 72)
        cp(b("XT" + nx, B, B + 64), rec)
        act(b("XT" + nx, 4112, 4176), rec)
        chain[0] = ""
        for h in range(2):
            act(half("PB", h), half("P", h) if stay else b("ZW" + nx, n + h, n + 128, 2), bias=2302.75)
        for lo in (0, 128):
            scan(b("FF", lo, lo + 128), b("FL", lo, lo + 128), pb(3, lo, lo + 128), A.mult, A.add)
        names = b("RI" + nx, n, n + 128) if stay else b("FN", 128 * t, 128 * t + 128)
        if t < 3 or not stay:
            act(names, b("FF", 1, 256, 2))
        if not stay:
            push("f%d" % t, names)
        if t < 3:
            cp(b("CI", 0, 1), b("CNT"))
            ts(b("CI", 1, 2), b("CI", 0, 1), 1, None, A.bitwise_and)
            ts(b("BARS", 4 * t, 4 * t + 1), b("CI", 1, 2), 256.0, 896.0, A.mult, A.add)
            push("b%d" % t, b("BARS", 4 * t, 4 * t + 1))
            copies(2 * t + 1, b("BARS", 4 * t, 4 * t + 1) if t else b(GATE))
            if t < 2:
                push("z%d" % t, b("ZW" + nx, 768, n + 128), [b("BARS", 4 * t, 4 * t + 1)] if t else [])
            push("q%d" % t, b("XT" + nx, 3856, B + 64))
            push("y%d" % t, b("RI" + nx, 768, n + 128))
        if t == 2:
            for lo in range(0, 384, 128):
                act(b("YR", lo, lo + 128), b("RI", 768 + lo, 896 + lo))
            dma("Y", "o0", [(b("YR", 0, 384), "yr", sl(0, 384))], False)
        if t == 3:
            act(b("YR", 384, 512), b("FF", 1, 256, 2) if stay else b("RI", 1152, 1280))
            dma("Y", "o1", [(b("YR", 384, 512), "yr", sl(384, 512))], False)
        XN, src = b("XT" + nx, 16, 4176), "MS" if stay else "ML"
        chain[0] = "VST"
        if t < 3:
            for h in range(2):
                tt(half("AF", h), ind(XN, b(src, 72 * t + 4 * h, 72 * t + 4 * h + 4)), half("PB", h), A.subtract)
            ts(b("P"), b("AF"), -0.5, -1024.0, A.mult, A.add)
        else:
            tt(b("AF"), ind(XN, b(src, 72 * t, 72 * t + 8)), b("PB"), A.subtract)
            for h in range(2):
                ts(b("YP", h, 128, 2), half("AF", h), -0.5, -1024.0, A.mult, A.add)
            dma("S", "o2", [(b("YP"), "yp", sl(None))], False)
    return ops


def regions(o):
    return [(y[0], y[2], isw) for isw, xs in ((False, o[3]), (True, o[2])) for x in xs for y in ([x, x[4]] if x[4] else [x])]


def late(o):
    k = o[5]
    if k and k[0] == "dma":
        return DMA + k[2] / 3.0e5
    if k and k[0] == "arrive":
        return 2 * HOP + k[2] / 1.2e5 + (SLACK if k[1][0] in "zqy" else 0.0)
    return HOP if k else LAT


def depends(ops):
    deps, acc, last = [{} for _ in ops], {}, {}
    for i, o in enumerate(ops):
        if o[0] == "R":
            deps[i][i - 1] = 0.0
        elif o[6]:
            if o[6] in last:
                deps[i][last[o[6]]] = 0.0
            last[o[6]] = i
        for buf, m, isw in regions(o):
            for m2, w2, j in acc.get(buf, []):
                same = ops[j][0] == o[0] and not ops[j][5]
                hit = m & m2 and (isw or w2)
                if j != i and (hit or (buf[:2] == "pb" and (not same or o[0] == "T"))):
                    d = late(ops[j]) if not same or (hit and w2 and not (o[0] == "T" and isw)) else 0.0
                    deps[i][j] = max(deps[i].get(j, 0.0), d)
        for buf, m, isw in regions(o):
            old = acc.get(buf, [])
            if buf[:2] == "pb":
                old = [y for y in old if ops[y[2]][0] == o[0] and o[0] != "T"] if not old or ops[old[-1][2]][0] != o[0] or o[0] == "T" else old
                if old and ops[old[-1][2]][0] == o[0]:
                    for j, d in deps[old[-1][2]].items():
                        if ops[j][0] != o[0] and any(r[0] == buf for r in regions(ops[j])):
                            deps[i][j] = max(deps[i].get(j, 0.0), d)
            acc[buf] = [y for y in old if not (isw and y[0] & ~m == 0 and buf[:2] != "pb")] + [(m, isw, i)]
    return deps


def schedule(ops):
    ops = [o[:4] + (o[4] * FAC,) + o[5:] for o in ops]
    n, deps = len(ops), depends(ops)
    succ = [[] for _ in ops]
    for i in range(n):
        for j, d in deps[i].items():
            succ[j].append((i, d))
    rank = [0.0] * n
    for i in range(n - 1, -1, -1):
        rank[i] = ops[i][4] + max([d + rank[j] for j, d in succ[i]], default=late(ops[i]))
        rank[i] += 8.0 if ops[i][5] and ops[i][5][:2] == ("push", "k0") else 0.0
    for i in range(n):
        rank[i] += 100.0 if ops[i][5] and ops[i][5][0] == "push" else 0.0
    left, ready, at, free, order, busy = [len(d) for d in deps], set(), [0.0] * n, {}, [], {}
    ready.update(i for i in range(n) if not left[i])
    while ready:
        est = {i: max(at[i], free.get(ops[i][0], 0.0)) for i in ready}
        t0 = min(est.values())
        q = ops[min(i for i in ready if est[i] == t0)][0]
        mine = [i for i in ready if ops[i][0] == q]
        i = max((j for j in mine if est[j] <= t0), key=lambda j: (rank[j], -j))
        for j in mine:
            if t0 < est[j] < t0 + ops[i][4] and est[j] + max(rank[j], ops[j][4] + rank[i]) < t0 + max(rank[i], ops[i][4] + rank[j]):
                if est[i] <= t0 or rank[j] > rank[i]:
                    i = j
        ready.remove(i)
        order.append(i)
        DBG.append((est[i], i, rank[i]))
        end = est[i] + ops[i][4]
        if q != "R":
            free[q] = end
        k = ops[i][5]
        if k and k[0] == "dma":
            busy[q] = max(busy.get("Y", 0.0), busy.get("S", 0.0), end + DMA) + k[2] / 3.0e5
            end = busy[q] - late(ops[i])
        if k and k[0] == "arrive" and k[1][0] == "k":
            way = COPIES[int(k[1][1:])][4]
            busy[way] = max(busy.get(way, 0.0), end + 2 * HOP) + k[2] / 1.2e5
            end = busy[way] - late(ops[i])
        for j, d in succ[i]:
            at[j] = max(at[j], end + d)
            left[j] -= 1
            if not left[j]:
                ready.add(j)
    return [ops[i] for i in order]


_PLAN, _WAYS = [], {}
DBG = []


def plan(T, topo):
    if not _PLAN:
        _PLAN.extend(schedule(program()))
        for m in WRITES:
            for r in range(N):
                _WAYS[m, r] = hops(T, topo, T.cores[r], T.cores[(r + shift(m)) % N], m)
    return _PLAN


def relay_program(g, core, T, topo):
    sent = 0
    for m in [o[5][1] for o in plan(T, topo) if o[5] and o[5][0] == "push"]:
        for r in range(N):
            h = _WAYS[m, r]
            if core in h:
                i, x = h.index(core), place(m)
                g.wait_ge(T.sem["a" + m], len(engines(topo, h[i - 1], core, m)))
                sent += send(g, topo, core, h[i + 1], m, T[x[0]][x[1]], T[x[0]][x[1]], T.sem["a" + m], T.sem.rl)
    if sent:
        g.wait_ge(T.sem.rl, sent)


def rank_program(g, core, T, topo):
    rank = T.rank_of(core)
    if rank is None:
        relay_program(g, core, T, topo)
        return
    eng = {"V": g.vector, "S": g.scalar, "T": g.tensor, "G": g, "Y": g.sync}
    own = {"V": "sv", "S": "sa", "T": "st", "G": "sg"}
    total, acc, clk, evc = {}, {}, {q: {} for q in eng}, {}

    def ap(x):
        if not isinstance(x, tuple):
            return x
        return T[x[0]][x[1]].indirect(ap(x[4])) if x[4] else T[x[0]][x[1]]

    def merge(a, c):
        for s, k in c.items():
            if a.get(s, 0) < k:
                a[s] = k

    def done(regs, sem, inc, q, clock):
        total[sem] = total.get(sem, 0) + inc
        evc[(sem, total[sem])] = dict(clock, **{sem: total[sem]})
        for buf, m, isw in regs:
            keep = [x for x in acc.get(buf, []) if not (isw and x[0] & ~m == 0) and x[:3] != (m, isw, sem)]
            acc[buf] = keep + [(m, isw, sem, total[sem], q)]

    def waits(q, regs):
        need = {}
        for buf, m, isw in regs:
            ps = buf[:2] == "pb"
            for m2, w2, sem, cnt, q2 in acc.get(buf, []):
                if q2 == q:
                    if not m & m2 or not w2 or (q == "T" and isw):
                        continue
                elif not (ps or (m & m2 and (isw or w2))):
                    continue
                if clk[q].get(sem, 0) < cnt and need.get(sem, 0) < cnt:
                    need[sem] = cnt
        for s in sorted(need):
            c = need[s]
            if clk[q].get(s, 0) >= c or any(s2 != s and evc[(s2, c2)].get(s, 0) >= c for s2, c2 in need.items()):
                continue
            eng[q].wait_ge(T.sem[s], c)
            merge(clk[q], evc[(s, c)])
        for s, c in need.items():
            merge(clk[q], evc[(s, c)])

    sent = 0
    for o in plan(T, topo):
        q, regs, kind = o[0], regions(o), o[5]
        if q == "R":
            src = _WAYS[kind[1], (rank - shift(kind[1])) % N][-2]
            done(regs, "a" + kind[1], len(engines(topo, src, core, kind[1])), "D", {})
            continue
        waits(q, regs)
        if kind is None:
            o[1](eng[q], ap).then_inc(T.sem[own[q]], 1)
            done(regs, own[q], 1, q, clk[q])
        elif kind[0] == "dma":
            for x, name, ix in o[1]:
                a, c = ap(x), T[name][:, ix] if ix.stop else T[name][:]
                (eng[q].dma_start(a, c) if kind[3] else eng[q].dma_start(c, a)).then_inc(T.sem[kind[1]], 16)
            done(regs, kind[1], 16 * len(o[1]), "D", clk[q])
        else:
            m, x = kind[1:]
            k = COPIES[int(m[1:])] if m[0] == "k" else None
            watch = "lu%d" % k[0] if k and (k[1], k[3]) == ("XT", 4112) else None
            k = send(g, topo, core, _WAYS[m, rank][1], m, ap(place(m)), ap(x), T.sem["a" + m], T.sem[watch or "ls"])
            if watch:
                done([(x[0], x[2], False)], watch, k, "D", {})
            else:
                sent += k
    for s in sorted(total):
        if clk["G"].get(s, 0) < total[s]:
            g.wait_ge(T.sem[s], total[s])
    g.wait_ge(T.sem.ls, sent)
